import numpy as np, ml_dtypes
CORES = [9,25,41,57]
N = 4
import mx_ref
BF = ml_dtypes.bfloat16
def gentries(a):
    return np.ascontiguousarray(a.reshape(8, 16, -1).transpose(0, 2, 1)).reshape(8, -1)
def gtable(e):
    e = np.asarray(e); return np.ascontiguousarray(e.reshape(8, -1, 16).transpose(0, 2, 1)).reshape(128, -1).astype(np.int32)
def gcols(t, e):
    v = np.concatenate([t.reshape(8, 16, -1, 4), np.zeros((8, 16, 1, 4), BF)], axis=2)
    return np.ascontiguousarray(np.stack([v[g][:, e[g]] for g in range(8)])).reshape(128, -1)
def tile(rs):
    return np.stack(rs, axis=2).reshape(128, -1).astype(BF)
def pick(q, e):
    c = np.concatenate([q[0].reshape(128, -1, 4), np.zeros((128, 1, 4), np.uint8)], axis=1); s = np.concatenate([q[1], np.ones((16, 1), np.uint8)], axis=1)
    return (np.ascontiguousarray(c[:, e].reshape(128, -1)), np.ascontiguousarray(s[:, e]))
def join(*qs):
    return (np.concatenate([q[0] for q in qs], axis=1), np.concatenate([q[1] for q in qs], axis=1))
def put(q, e, v):
    c, s = q[0].reshape(128, -1, 4).copy(), q[1].copy(); c[:, e] = v[0].reshape(128, -1, 4); s[:, e] = v[1]
    return (c.reshape(128, -1), s)
def pk(c, s):
    return (np.ascontiguousarray(c), mx_ref.live(s))
def emit(q):
    return q[0], q[1]
def packed(v, rng):
    q = [mx_ref.quantize(np.ascontiguousarray(v[r])) for r in range(N)]
    return np.stack([a for a, b in q]), np.stack([mx_ref.plane(b, rng) for a, b in q])
def values_of_codes():
    e, c = np.zeros((128, 128, 4), np.float32), np.zeros((128, 2, 4), np.uint8)
    e[np.arange(128), np.arange(128), 0] = 1
    c[:127, :, 0] = np.arange(256).reshape(2, 128).T[:127]
    return mx_ref.matmul(mx_ref.quantize(e.reshape(128, 512).astype(BF)), (c.reshape(128, 8), np.full((16, 2), 127, np.uint8))).T.reshape(-1).astype(np.float64)
CODE_VALUE, SCALE_VALUE = values_of_codes(), 2.0 ** (np.arange(256) - 127.0)
def decode(q):
    return (CODE_VALUE[q[0]].reshape(16, 8, -1, 4) * SCALE_VALUE[q[1]][:, None, :, None] + 0.0).reshape(128, -1).astype(np.float32)
def f(rng, *shape):
    return mx_ref.flush((rng.standard_normal(shape, dtype=np.float32) * np.exp2(rng.integers(-2, 3, shape[:-1] + (1,)))).astype(BF))
def wide(rng, *shape, cols=0):
    v = rng.standard_normal(shape, dtype=np.float32) * np.exp2(rng.integers(-12, 13, shape)).astype(np.float32)
    if cols: v *= np.repeat(np.exp2(rng.integers(-cols, cols + 1, shape[:-2] + (1, shape[-1] // 4))) * (rng.random(shape[:-2] + (1, shape[-1] // 4)) > 0.0625), 4, axis=-1).astype(np.float32)
    return mx_ref.flush(v.astype(BF))
C, T, R = 320, 2560, 3
def big(v):
    v = v.astype(np.float32)
    v[np.abs(v) < np.float32(2.0 ** -12)] = 0
    return v.astype(BF)
def numbers_of(rng):
    return {"x": big(f(rng, N, 128, 4 * C)), "u": np.array(f(rng, N, 128, 512)), "v": np.array(f(rng, N, 128, 512))}
def lists_of(t):
    return np.stack([gtable(t[r]) for r in range(N)])
def layers(rng, still=[], full=False):
    w = np.zeros((N, 512, 512), np.float32)
    k = rng.random((N, 512, 512))
    k[:, :, np.isin(np.arange(512) // 4 % 16, still)] = 2
    e = np.argpartition(k, 8, axis=2)[:, :, :8]
    a = rng.integers(4, 16, (N, 512, 8)) * 0.25 * rng.choice([-1.0, 1.0], (N, 512, 8))
    if full: a = 4.0 * rng.choice([-1.0, 1.0], (N, 512, 1)) * np.ones((1, 1, 8))
    np.put_along_axis(w, e, a.astype(np.float32), axis=2)
    w[:, np.isin(np.arange(512) % 16, still)] = 0
    return w
def weights(rng, w):
    c, s = packed(np.ascontiguousarray(w.reshape(N, 512, 128, 4).transpose(0, 2, 1, 3)).reshape(N, 128, 2048).astype(BF), rng)
    return {"wc": c, "ws": s}
def setup_inputs(rng):
    return {**numbers_of(rng), "p": lists_of(rng.integers(0, T, (N, 8, C))), **weights(rng, layers(rng))}
def setup_inputs_ties(rng):
    d = numbers_of(rng)
    x = d["x"].reshape(N, 8, 16, C, 4)
    x[:, :, 0] = 0
    x[:, :, 0, :, 0] = rng.integers(0, 3, (N, 8, C)).astype(np.float32).astype(BF)
    u = d["u"].reshape(N, 128, 128, 4)
    u[:, :, ::16] = 0
    o = rng.permutation(N)
    for r in range(N):
        for h in range(0, 128, 16): u[r, h, h, 0] = 0.0 if r == o[0] else -1.0 if r == o[1] else 1.0
    t = rng.integers(0, T, (N, 8, C))
    t[o[:2]] = C * rng.integers(0, 4, (2, 8, C))
    t[o[2]] = rng.integers(0, T)
    t[o[3]] = C * (7 - np.arange(8))[:, None]
    return {"x": x.reshape(N, 128, 4 * C), "u": u.reshape(N, 128, 512), "v": d["v"], "p": lists_of(t), **weights(rng, layers(rng, [0]))}
def setup_inputs_near(rng):
    d = numbers_of(rng)
    x = d["x"].astype(np.float32).reshape(N, 8, 16, C, 4)
    x[:, :, 0] = 0
    x[:, :, 8:] = 0
    u = d["u"].reshape(N, 128, 128, 4)
    u[:, :, ::16] = 0
    t = rng.integers(0, T, (N, 8, C))
    o = rng.permutation(N) % 4
    for r in range(N):
        s = rng.integers(0, 16, (8, C))
        if o[r] == 1:
            s[5:] = np.minimum(s[5:], 12)
            s[5:, 4:9] = [15, 15, 14, 13, 12]
            t[r] = np.minimum(t[r], T - 2)
            t[r, 5, :16] = T - 1
            t[r, 6, :9] = T - 1
            t[r, 7, :7] = T - 1
        if o[r] < 3: x[r, :, 8] = ((s[:, :, None] >> np.arange(4)) & 1) * np.exp2(np.arange(4) - 22.0)
        if o[r] < 2:
            x[r, :, 0, :, 0] = rng.choice([-1.0, 1.0], (8, 1))
            x[r, :, 11, :, 0] = 2.0 ** -10
        if o[r] == 2:
            for g in rng.permutation(8)[:4]: x[r, g, 0, rng.integers(C), 0] = 2.0 ** 26 * rng.choice([-1.0, 1.0])
        if o[r] == 3:
            x[r, :, 10, :, 0] = np.where(s < 8, 1.125 * 2.0 ** -29, 0.0)
            x[r, :, 11, :, 0] = np.where(s < 8, 0.0, 2.0 ** -29)
        k = 1.0 if o[r] == 0 else 2.0 ** -30
        for h in range(0, 128, 16):
            if o[r] < 2:
                u[r, h, h, 0] = k
                u[r, h + 11, h, 0] = k
            if o[r] == 2: u[r, h, h, 0] = 2.0 ** 30
            if o[r] < 3: u[r, h + 8, h] = k
            else:
                u[r, h + 10, h, 0] = 1.125 * k
                u[r, h + 11, h, 0] = 1.25 * k
    return {"x": x.reshape(N, 128, 4 * C).astype(BF), "u": u.reshape(N, 128, 512), "v": d["v"], "p": lists_of(t), **weights(rng, layers(rng, [0, 8, 9, 10, 11, 12, 13, 14, 15]))}
def setup_inputs_fine(rng):
    d = numbers_of(rng)
    x = (1.0 + (2 * rng.integers(0, 64, (N, 8, 2, 8, C, 4)) + 1) * 2.0 ** -7) * np.exp2(-rng.integers(8, 15, (N, 8, 2, 8, C, 4))) * rng.choice([-1.0, 1.0], (N, 8, 2, 8, C, 4))
    np.put_along_axis(x[..., 0], rng.integers(0, 8, (N, 8, 2, 1, C)), 1.96875 * rng.choice([-1.0, 1.0], (N, 8, 2, 1, C)), axis=3)
    x = x * np.exp2(rng.integers(-1, 3, (N, 8, 2, 1, C, 1)))
    return {"x": x.astype(np.float32).reshape(N, 128, 4 * C).astype(BF), "u": d["u"], "v": d["v"], "p": lists_of(rng.integers(0, T, (N, 8, C))), **weights(rng, layers(rng))}
def setup_inputs_ends(rng):
    k = int(rng.integers(0, 2))
    o = np.roll(np.array([2, 3, k, 1 - k])[np.arange(N) % 4], int(rng.integers(0, N)))
    sign = np.array([1.0, -1.0, 1.0, 1.0])
    x = np.zeros((N, 8, 16, C, 4))
    u = np.array(f(rng, N, 128, 512)).reshape(N, 128, 128, 4)
    v = (rng.integers(0, 2, (N, 128, 512)) * 2.0 - 1.0) * 2.0 ** 30
    w = layers(rng, full=True)
    t = np.zeros((N, 8, C), np.int64)
    for r in range(N):
        a = 2.0 ** 26 * rng.choice([1.0, 0.875, 0.75], (8, 1, C, 1))
        if o[r] == 0: x[r] = a
        if o[r] == 1:
            x[r] = -a
            t[r] = T - 1
        if o[r] < 2:
            w[r] = np.abs(w[r]) * (sign[o[r]] * sign[o[r - 1]])
            if o[r - 1] == 3:
                w[r, :, :64] = np.sum(w[r].reshape(512, 8, 64), axis=1)
                w[r, :, 64:] = 0
        if o[r] == 2:
            x[r] = 2.0 ** -30
            w[r] = 0
            t[r] = (T - 1) * rng.integers(0, 2, (8, C))
        if o[r] == 3:
            x[r] = 2.0 ** 26 * rng.choice([-1.0, 1.0], (8, 1, C, 1))
            x[r, 0] = 2.0 ** 26
            t[r] = (T - 1) * (rng.permutation(8) % 2)[:, None]
        h = rng.permutation(6) % 2 * 2.0 - 1.0
        for g in range(8): u[r, :, 16 * g] = 0.0 if g in (0, 7) else (2.0 ** -30 if o[r] == 2 else 2.0 ** 30) * float(h[g - 1])
    v = (np.where(v < 0, -1.0, 1.0) * np.where(rng.permutation(N) % 2, 2.0 ** -30, 2.0 ** 30)[:, None, None]).astype(np.float32).astype(BF)
    return {"x": x.astype(np.float32).reshape(N, 128, 4 * C).astype(BF), "u": u.reshape(N, 128, 512), "v": v.astype(np.float32).astype(BF), "p": lists_of(t), **weights(rng, w)}
def setup_inputs_spread(rng):
    d = setup_inputs(rng)
    d["x"] = big(wide(rng, N, 128, 4 * C, cols=6))
    return d
def check_inputs(d):
    b = []
    for k, most in (("x", 2.0 ** 26), ("u", 2.0 ** 30), ("v", 2.0 ** 30)):
        a = np.abs(d[k].astype(np.float32))
        if not (np.isfinite(a).all() and ((a == 0) | (a >= 2.0 ** -30) & (a <= most)).all()): b.append("a value of " + k)
    if not ((d["p"] >= 0) & (d["p"] < T)).all(): b.append("an entry of p")
    none, least, most = [emit(mx_ref.quantize(np.full((128, 16), k, np.float32).astype(BF)))[1][0, 0] for k in (0.0, 2.0 ** -30, 2.0 ** 30)]
    for r in range(N):
        if ((d["wc"][r] == 0x7F) | (d["wc"][r] == 0xFF)).any(): b.append("wc: a code that is no number")
        s = mx_ref.live(d["ws"][r])
        if ((s != none) & ((s < least) | (s > most))).any(): b.append("ws: a scale out of range")
        a = np.abs(decode(pk(d["wc"][r], d["ws"][r])).astype(np.float64)).reshape(128, 512, 4)
        if not (np.sum(a, axis=(0, 2)) <= 32).all(): b.append("sizes in a column of W")
    return b
def order_of(t):
    place = np.argsort(np.argsort(T * t.reshape(-1) + np.arange(T))).reshape(8, C)
    o = np.argsort(place, axis=1)
    k = np.stack([np.searchsorted(place[g, o[g]], 8 * np.arange(C) + 7, side="right") for g in range(8)]) - 1
    k = np.maximum(k, 0)
    return place // 8, np.take_along_axis(o, k, axis=1), np.take_along_axis(o, np.minimum(k + 1, C - 1), axis=1)
def reference(x, u, v, p, wc, ws):
    qu = [mx_ref.quantize(u[r]) for r in range(N)]
    lay = [pk(wc[r], ws[r]) for r in range(N)]
    now = [x[r] for r in range(N)]
    pos = np.stack([gentries(p[r]) for r in range(N)]).astype(np.int64)
    for t in range(R):
        own, q = [], []
        for r in range(N):
            own.append(decode(mx_ref.quantize(now[r])).astype(BF))
            c, m, n = order_of(pos[r])
            z = ((gcols(own[r], m).astype(np.float32) + gcols(own[r], n).astype(np.float32)) * np.float32(0.5)).astype(BF)
            q.append(mx_ref.quantize(z))
            s = mx_ref.matmul(qu[r], q[r])[::16] + np.float32(0.0)
            step = np.argsort(np.argsort(s, axis=1, kind="stable"), axis=1)
            pos[r] += np.take_along_axis(step, c, axis=1)
        for r in range(N):
            came = pick(q[(r + N - 1) % N], np.arange(1, C, 2))
            h = tile([mx_ref.matmul(pick(lay[r], np.arange(128 * b, 128 * b + 128)), came) * np.float32(0.03125) for b in range(4)])
            c, m, n = order_of(pos[r])
            now[r] = (own[r].astype(np.float32) + gcols(h, c // 2).astype(np.float32)).astype(BF)
    y, pt = np.zeros((N, 128, C), np.float32), np.zeros((N, 8, C), np.float32)
    oc, osc = np.zeros((N, 128, 4 * C), np.uint8), np.zeros((N, 16, C), np.uint8)
    for r in range(N):
        q = mx_ref.quantize(now[r])
        y[r] = mx_ref.matmul(mx_ref.quantize(v[r]), q)
        pt[r] = pos[r]
        oc[r], osc[r] = emit(q)
    return {"y": y, "pt": pt, "oc": oc, "osc": osc}

@@ -1,0 +1,431 @@
+from concourse.mybir import dt, AluOpType as A, ActivationFunctionType as F
+
+C, P, R = 320, 128, 3
+NV = 3520
+NULL = 3528
+WW = 3936
+NS = 11
+WS = 3
+CS = 64 * WS
+BIG = 4194304.0
+
+SCRATCH, AT = {}, {}
+
+
+def _b(n, w, d="float32", where="sbuf"):
+    SCRATCH[n] = (where, [P, w], d)
+    AT[n] = (n, 0, w)
+
+
+def _t(n, d, parts, where="sbuf"):
+    a = 0
+    for k, w in parts:
+        AT[k] = (n, a, w)
+        a += w
+    SCRATCH[n] = (where, [P, a], d)
+
+
+for _n, _w in (("E16", C), ("JR", C), ("E32", 640), ("TNY", 1), ("MASK", C), ("MSKA", C), ("RS", C), ("MB0", C), ("MB", C),
+               ("KF0", C), ("KFA", C), ("KFB", C), ("KM", C), ("KS", C), ("S1", C), ("S2", C), ("OWD", 336), ("O2", C), ("O3", C), ("IX", C),
+               ("MM", C), ("MS", C), ("SM", C), ("SS", C), ("DD", C), ("DM", C), ("RA", C), ("NA", 20 - 4 * WS), ("ND", 20 - 4 * WS), ("STEP", C),
+               ("PT0", C), ("PT1", C), ("YB", C)):
+    _b(_n, _w)
+_t("SKB", "float32", [("SK", C), ("SKE", 16)])
+_t("CTAB", "float32", [("C16", 20), ("C1", 20), ("QP", 4), ("Q20", 4), ("ODD", 4), ("EVN", 4), ("NO", 4), ("NE", 4), ("DUMP", 20)])
+_t("FTAB", "float32", [("ACC", 20), ("RKP", 20), ("DU", 20), ("DT", 20), ("OW", 20), ("IXM", 20)])
+_t("VSB", "float16", [("VS%d" % k, 160) for k in range(20 - NS)])
+_b("GS", 640, "float16")
+_t("CTABI", "int32", [("QI", 4), ("QA", 4), ("QB", 4)])
+_t("ITAB", "int32", [("KI", 20), ("PI", 20), ("SI", 40), ("SH", 40), ("PL", 20), ("CI", 20), ("C2I", 20), ("MI", 20), ("MJ", 20), ("NJ", 20)])
+_t("UTAB", "uint16", [("OQ", 40)] + [(k, 20) for k in ("PERM", "RP", "OWU", "COFF", "C2OFF", "P2U", "IXU", "MOFF", "NOFF")])
+_b("UI", 8, "int32")
+_b("PR", C, "int32")
+_b("UL", 8, "uint16")
+for _n, _w in (("ZER", 512), ("ONE", 512), ("OB1", 512), ("OB2", 512), ("CDF", C), ("ONES", C), ("UT", 512), ("VT", 512), ("X", 4 * C),
+               ("Z", 4 * C), ("W", WW), ("CC", NV), ("D", 3536), ("G", 640), ("GT", 640), ("W2", 8 * C), ("N2", 4 * C), ("RS32", 640)):
+    _b(_n, _w, "bfloat16")
+_t("JUNK", "bfloat16", [("JUNK%d" % k, C) for k in range(NS)])
+_t("CMPB", "bfloat16", [("CMP%d" % k, C) for k in range(20 - NS)])
+_t("EBB", "bfloat16", [("EB%d" % k, 512) for k in range(4)])
+for _n, _w in (("FH", C), ("GB", C), ("HB", 160)):
+    _t(_n + "B", "bfloat16", [("%s%d" % (_n, k), _w) for k in range(4)])
+_t("CTB", "bfloat16", [("CT%d" % k, 4 * C) for k in range(5)])
+_t("PFB", "float32", [("PF%d" % k, 512) for k in range(4)], "psum")
+for _n in ("PS", "PSB", "PK", "PH"):
+    _b(_n, 512, "float32", "psum")
+for _n, _w in [("OB", P), ("U", P), ("UR", P), ("V", P), ("L", 512), ("X", C)] + [("%s%d" % (z, k), C) for k in range(R) for z in "ZA"]:
+    _b("q" + _n, _w, "float8_e4m3fn_x4")
+    _b("s" + _n, _w, "uint8")
+for _n, _d in (("q", "float8_e4m3fn_x4"), ("s", "uint8")):
+    _t(_n + "EB", _d, [("%sE%d" % (_n, k), P) for k in range(4)])
+    _t(_n + "CB", _d, [("%sC%d" % (_n, k), C) for k in range(5)])
+PSUM = ["PF0", "PF1", "PF2", "PF3", "PS", "PSB", "PK", "PH"]
+
+SEMAPHORES = ["cv", "cs", "ct", "cg", "dp", "dx", "du", "dv", "dw", "dz", "dd", "de", "dout", "dpt", "dy", "sent"] + ["arr%d" % k for k in range(R)]
+
+
+def region(s):
+    f = s.split("@")[0].split(":")
+    if len(f) < 3 or "@" in s:
+        return f[0], range(AT[f[0]][2])
+    return f[0], range(int(f[1]), int(f[2]), int((f + [1])[3]))
+
+
+def meet(a, b):
+    if a[-1] < b[0] or b[-1] < a[0]:
+        return False
+    return a.step == 1 or b.step == 1 or a.step != b.step or (a[0] - b[0]) % a.step == 0
+
+
+def rank_program(g, core, T, topo):
+    rank = T.rank_of(core)
+    if rank is None:
+        return
+    nxt = T.cores[(rank + 1) % len(T.cores)]
+    V, S, TE = g.vector, g.scalar, g.tensor
+    eng = {"v": V, "s": S, "t": TE, "g": g, "y": g.sync}
+    cnt, seen, wr, rd = {}, {e: {} for e in eng}, {}, {}
+
+    def ap(s):
+        s, _x, by = s.partition("@")
+        n, o, w = AT[s.split(":")[0]]
+        r = region(s)[1]
+        a, e = o + r.start, o + r.stop
+        v = T[n][:, a:e:r.step] if r.step > 1 else T[n][:, a:e]
+        return v.indirect(ap(by)) if by else v
+
+    def wait(e, deps):
+        most = {}
+        for s, n in deps:
+            most[s] = max(most.get(s, 0), n)
+        for s, n in most.items():
+            if seen[e].get(s, 0) < n:
+                eng[e].wait_ge(T.sem[s], n)
+                seen[e][s] = n
+
+    def deps_of(outs, ins, own):
+        d = []
+        for k, r in ins:
+            d += [x[1:] for x in wr.get(k, []) if meet(x[0], r)]
+            if k in PSUM:
+                d += [x[1:] for x in rd.get(k, []) if x[1] != own]
+        for k, r in outs:
+            for x in wr.get(k, []) + rd.get(k, []):
+                if (meet(x[0], r) or k in PSUM) and not (own == "ct" and x[1] == own):
+                    d.append(x[1:])
+        return d
+
+    def note(outs, ins, sem, n):
+        for k, r in ins:
+            rd[k] = [x for x in rd.get(k, []) if x[1] != sem or x[0] != r] + [(r, sem, n)]
+        for k, r in outs:
+            whole = len(r) == AT[k][2] or k in PSUM
+            wr[k] = ([] if whole else [x for x in wr.get(k, []) if x[0] != r]) + [(r, sem, n)]
+            if whole:
+                rd[k] = [x for x in rd.get(k, []) if x[2] == n and x[1] == sem]
+
+    def op(e, call, outs, ins, extra=()):
+        own = "c" + e
+        lists = [s.split("@")[1] for s in list(outs) + list(ins) if "@" in s]
+        o, i = [region(s) for s in outs], [region(s) for s in list(ins) + lists]
+        wait(e, deps_of(o, i, own) + list(extra))
+        cnt[own] = cnt.get(own, 0) + 1
+        call().then_inc(T.sem[own], 1)
+        note(o, i, own, cnt[own])
+
+    def dma(sem, moves, outs, ins):
+        o, i = [region(s) for s in outs], [region(s) for s in ins]
+        d = deps_of(o, i, "")
+        for q, to, fr in moves:
+            wait(q, d)
+            eng[q].dma_start(to, fr).then_inc(T.sem[sem], 16)
+            cnt[sem] = cnt.get(sem, 0) + 16
+        note(o, i, sem, cnt[sem])
+
+    def ts(o, i, s1, op0, s2=None, op1=None):
+        a1, a2 = [ap(s) if isinstance(s, str) else s for s in (s1, s2)]
+        names = [i] + [s for s in (s1, s2) if isinstance(s, str)]
+        if op1 is None:
+            op("v", lambda: V.tensor_scalar(ap(o), ap(i), a1, None, op0), [o], names)
+        else:
+            op("v", lambda: V.tensor_scalar(ap(o), ap(i), a1, a2, op0, op1), [o], names)
+
+    def tt(o, a, b, o2):
+        op("v", lambda: V.tensor_tensor(ap(o), ap(a), ap(b), o2), [o], [a, b])
+
+    def cp(o, i):
+        op("v", lambda: V.tensor_copy(ap(o), ap(i)), [o], [i])
+
+    def scan(o, a, b, init, op0, op1):
+        first = isinstance(init, str)
+        op("v", lambda: V.tensor_tensor_scan(ap(o), ap(a), ap(b), ap(init) if first else init, op0, op1), [o], [a, b] + ([init] if first else []))
+
+    def fill(n, c):
+        op("v", lambda: V.memset(ap(n), c), [n], [])
+
+    def quant(q, t):
+        op("v", lambda: V.quantize_mx(ap("q" + q), ap("s" + q), ap(t)), ["q" + q, "s" + q], [t])
+
+    def mm(ps, a, a0, b, start=True, stop=True, extra=()):
+        r = ":%d:%d" % (a0, a0 + P)
+        i = ["q" + a + r, "s" + a + r, "q" + b, "s" + b]
+        op("t", lambda: TE.matmul_mx(ap(ps + ":0:320"), ap(i[0]), ap(i[1]), ap(i[2]), ap(i[3]), start, stop), [ps], i, extra)
+
+    def act(o, i, f, acc=None, bias=None, scale=None):
+        kw = {}
+        if bias is not None:
+            kw["bias"] = ap(bias)
+        if scale is not None:
+            kw["scale"] = scale
+        if acc is not None:
+            kw["accum_out"] = ap(acc)
+        op("s", lambda: S.activation(ap(o), ap(i), f, **kw), [o] + [s for s in (acc,) if s], [i] + [s for s in (bias,) if s])
+
+    def iota(n, pattern, base=0, cm=0):
+        kw = {} if SCRATCH[AT[n.split(":")[0]][0]][2] == "int32" else {"allow_small_or_imprecise_dtypes": True}
+        op("g", lambda: g.iota(ap(n), pattern, base, cm, **kw), [n], [])
+
+    def sel(o, i, pattern, cop, c, base, cm):
+        op("g", lambda: g.affine_select(ap(o), ap(i), pattern, cop, c, base, cm), [o], [i])
+
+    dma("dp", [("ys"[k % 2], T.PR[k:P:16, :], T.p[:, :]) for k in range(16)], ["PR"], [])
+    dma("dx", [("y", T.X[:, :], T.x[:, :])], ["X"], [])
+    dma("du", [("y", T.UT[:, :], T.u[:, :])], ["UT"], [])
+
+    iota("QI:0:2", [[0, 2]], 0, 1)
+    iota("C1", [[1, 20]])
+    iota("E16", [[0, 20], [1, 16]])
+    iota("JR", [[1, C]])
+    iota("C16", [[16, 20]])
+    iota("E32", [[0, 20], [1, 32]])
+    iota("W", [[0, WW]], -160)
+    fill("ZER", 0.0)
+    fill("ONE", 1.0)
+    dma("dz", [("y", T.D[:, a:min(a + 512, 3536)], T.ZER[:, 0:min(512, 3536 - a)]) for a in range(0, 3536, 512)], ["D"], ["ZER"])
+    dma("dw", [("y", T.qL[:, 0:512].bitcast(dt.uint8), T.wc[:, :]), ("y", T.sL[:, 0:512], T.ws[:, :])], ["qL", "sL"], [])
+    dma("dv", [("y", T.VT[:, :], T.v[:, :])], ["VT"], [])
+    ts("QA:0:2", "QI:0:2", 15, A.bitwise_and)
+    ts("QB:0:2", "QI:0:2", 4, A.arith_shift_right, 1, A.bitwise_and)
+    cp("QP:0:1", "QA:0:1")
+    cp("ODD:0:1", "QB:0:1")
+    ts("Q20:0:1", "QP:0:1", 20.0, A.mult)
+    ts("PERM", "C1", "Q20:0:1", A.add)
+    ts("EVN:0:1", "ODD:0:1", -1.0, A.mult, 1.0, A.add)
+    ts("NO:0:1", "ODD:0:1", float(NULL), A.mult)
+    ts("NE:0:1", "EVN:0:1", float(NULL), A.mult)
+    ts("MASK", "E16", "QP:0:1", A.is_equal)
+    ts("RS", "E16", 0.0, A.is_gt)
+    ts("MB0", "E16", "QP:0:1", A.is_lt)
+    ts("CDF", "JR", -159.0, A.add)
+    ts("MB", "MB0", 2.0 * BIG, A.mult, -BIG, A.add)
+    ts("DUMP", "C16", "QP:0:1", A.add, 3600.0, A.add)
+    fill("SKE", 3600.0 * 512.0)
+    fill("ONES", 1.0)
+    act("RS32", "E32", F.Sign)
+    for b in range(4):
+        sel("EB%d" % b, "ZER", [[1, 512]], A.not_equal, 1.0, -b, -4)
+    iota("W2", [[0, 8 * C]])
+    iota("UI", [[16, 8]])
+    sel("OB1", "ONE", [[-16, 8], [0, 64]], A.is_ge, 0.0, 0, 1)
+    sel("OB2", "OB1", [[16, 8], [0, 64]], A.is_ge, 0.0, 15, -1)
+    cp("KF0", "PR@PERM")
+    ts("KFB", "KF0", 512.0, A.mult, 512.0, A.add)
+    tt("KFA", "KFB", "JR", A.add)
+
+    def unpack():
+        for b in range(4):
+            mm("PF%d" % b, "E%d" % b, 0, "X")
+        for b in range(4):
+            act("FH%d" % b, "PF%d:0:320" % b, F.Copy, scale=0.5)
+
+    def first_tiles():
+        for b in range(4):
+            quant("E%d" % b, "EB%d" % b)
+        quant("X", "X")
+        unpack()
+
+    def sides():
+        cp("UL", "UI")
+        quant("U", "UT")
+        quant("OB", "OB2")
+        op("v", lambda: V.tensor_copy(T.qUR[:, 0:P].bitcast(dt.uint32), T.qU[:, 0:P].bitcast(dt.uint32).indirect(T.UL[:, 0:8])), ["qUR"], ["qU", "UL"])
+        cp("sUR", "sU@UL")
+        fill("TNY", 2.0 ** -126)
+        ts("MSKA", "E16", "QP:0:1", A.is_le)
+
+    def half(k):
+        scan("VS%d" % k, "CMP%d:0:160" % k, "CMP%d:160:320" % k, 0.0, A.add, A.add)
+
+    def spread(sem, a, b):
+        moves = []
+        for h in range(8):
+            if h < 7:
+                moves.append((T.D[16 * (h + 1) + h:P:16, a:b], T.CC[16 * h:16 * h + 7 - h, a:b]))
+            if h:
+                moves.append((T.D[h:16 * h:16, a + 1:b + 1], T.CC[16 * h + 8:16 * h + 8 + h, a:b]))
+        dma(sem, [("ys"[k % 2], o, i) for k, (o, i) in enumerate(moves)], ["D:%d:%d" % (a, b)], ["CC:%d:%d" % (a, b)])
+
+    def order(kf, joined, nv, during, scalar_tail):
+        tt("KM", kf, "MASK", A.mult)
+        scan("KS", "RS", "KM", 0.0, A.mult, A.add)
+        for c in range(NS):
+            act("JUNK%d" % c, kf, F.Sign, acc="ACC:%d:%d" % (c, c + 1), bias="KS:%d:%d" % (16 * c + 15, 16 * c + 16), scale=-1.0)
+        n = 20 - NS
+        for k in range(n):
+            c = NS + k
+            ts("CMP%d" % k, kf, "KS:%d:%d" % (16 * c + 15, 16 * c + 16), A.is_lt)
+            if k:
+                half(k - 1)
+        half(n - 1)
+        ts("RP:0:%d" % NS, "ACC:0:%d" % NS, 319.0, A.add, 0.5, A.mult)
+        op("v", lambda: V.tensor_copy(ap("RP:%d:20" % NS), T.VSB[:, 159:160 * n:160]), ["RP:%d:20" % NS], ["VS%d" % k for k in range(n)])
+        cp("SK@RP", kf)
+        scan("S1", "SK", "MB", 0.0, A.min, A.max)
+        op("v", lambda: V.tensor_tensor_scan(ap("S2"), T.SKB[:, 1:C + 1], ap("MB"), 0.0, A.min, A.max), ["S2"], ["SK", "SKE", "MB"])
+        tt("SI:0:20", "S1:15:320:16", "SK:0:320:16", A.max)
+        tt("SI:20:40", "S2:15:320:16", "SK:1:320:16", A.max)
+        ts("SH", "SI", 9, A.arith_shift_right)
+        tt("DU", "SH:0:20", "SH:20:40", A.is_equal)
+        tt("DT", "DU", "DUMP", A.mult)
+        tt("OW", "DT", "SH:0:20", A.max)
+        cp("OWU", "OW")
+        cp("W@OWU", "CDF")
+        h = nv // 2
+        lo, hi = "0:%d" % h, "%d:%d" % (h, nv)
+        scan("CC:" + lo, "W:" + lo, "W:" + lo, -160.0, A.max, A.max)
+        spread("dd", 0, h)
+        scan("CC:" + hi, "W:" + hi, "W:" + hi, "CC:%d:%d" % (h - 1, h), A.max, A.max)
+        spread("de", h, nv)
+        scalar_tail()
+        cp("KI", "KS:15:320:16")
+        ts("RKP", "RP", 1120.0, A.add)
+        ts("PI", "KI", 9, A.arith_shift_right)
+        if joined:
+            iota("W", [[0, WW]], -160)
+            cp("OWD@RP", "JR")
+        ts("OQ:0:40:2", "PI", "EVN:0:1", A.mult, "NO:0:1", A.add)
+        ts("OQ:1:40:2", "PI", "ODD:0:1", A.mult, "NE:0:1", A.add)
+        if joined:
+            cp("OWD:320:321", "OWD:319:320")
+            ts("O2", "OWD:0:320", 512.0, A.mult)
+            tt("O3", "O2", "OWD:1:321", A.add)
+        during()
+        cp("G", "D@OQ")
+        op("v", lambda: V.transpose(ap("GT"), ap("G")), ["GT"], ["G"])
+        scan("GS", "RS32", "GT", 0.0, A.mult, A.add)
+        tt("PL", "GS:31:640:32", "RKP", A.add)
+        ts("C2I", "PL", 4, A.arith_shift_right)
+        cp("C2OFF", "C2I")
+
+    def lists1(again):
+        cp("P2U", "PL")
+        ts("CI", "PL", 3, A.arith_shift_right)
+        cp("W2@P2U", "ONES")
+        cp("COFF", "CI")
+        scan("N2", "W2:0:2560:2", "W2:1:2560:2", -160.0, A.add, A.add)
+        if again:
+            iota("W2", [[0, 8 * C]])
+
+    def lists2():
+        scan("IX", "N2:3:1280:4", "MB", 0.0, A.min, A.max)
+        tt("IXM", "IX:15:320:16", "N2:3:1280:64", A.max)
+        ts("IXU", "IXM", 159.0, A.add, 0.0, A.max)
+        tt("MM", "O3@IXU", "MASK", A.mult)
+        scan("MS", "RS", "MM", 0.0, A.mult, A.add)
+        ts("MJ", "MS:15:320:16", 2.0 ** -9, A.mult, -0.3125, A.add)
+        cp("MI", "MS:15:320:16")
+        cp("MOFF", "MJ")
+        ts("NJ", "MI", 511, A.bitwise_and)
+        cp("NOFF", "NJ")
+
+    order("KFA", True, 2576, first_tiles, lambda: None)
+    lists1(True)
+    names = ["KFA", "KFB"]
+    for t in range(R):
+        last = t == R - 1
+        lists2()
+        qz = "Z%d" % t
+        for b in range(4):
+            act("GB%d" % b, "FH%d@MOFF" % b, F.Copy)
+        if t == 0:
+            sides()
+        for b in range(4):
+            tt("Z:%d:1280:4" % b, "FH%d@NOFF" % b, "GB%d" % b, A.add)
+        quant(qz, "Z")
+        wait("g", [x[1:] for x in wr["q" + qz] + wr["s" + qz]])
+        rid, pid, _s = topo.addr(nxt)
+        m, arr = topo.mask(core, nxt), "arr%d" % t
+        n = 2 * len(topo.engines(core, nxt))
+        g.remote_dma(T["qA%d" % t][:, 0:C].bitcast(dt.uint8), T["q" + qz][:, 0:C].bitcast(dt.uint8), T.sem[arr], T.sem.sent, pid, rid, m)
+        g.remote_dma(T["sA%d" % t][:, 0:C], T["s" + qz][:, 0:C], T.sem[arr], T.sem.sent, pid, rid, m)
+        cnt["sent"], cnt[arr] = cnt.get("sent", 0) + n, n
+        mm("PS", "UR", 0, qz)
+        mm("PSB", "UR", 0, qz)
+        tt("SM", "PS:0:320", "MASK", A.mult)
+        act("DD", "PSB:0:320", F.Abs, bias="TNY", scale=1.01 * 2.0 ** -24)
+        scan("SS", "RS", "SM", 0.0, A.mult, A.add)
+        tt("DM", "DD", "MSKA", A.mult)
+        keys = "SS:%d:320:16" % (CS + 15)
+        act("NA", keys, F.Abs, bias="TNY", scale=1.01 * 2.0 ** -24)
+        tt("RA", "PS:0:320", "DM", A.subtract)
+        tt("ND", keys, "NA", A.subtract)
+        for w in range(WS, 5):
+            for e in range(4):
+                a = 4 * w + e
+                s, ct, d = "SS:%d:%d" % (16 * a + 15, 16 * a + 16), "CT%d:%%d:%%d:4" % w, "ND:%d:%d" % (a - 4 * WS, a - 4 * WS + 1)
+                if a:
+                    act(ct % (e, 64 * a), "PSB:0:%d" % (16 * a), F.Sign, bias=s, scale=-1.0)
+                act(ct % (64 * a + e, 64 * a + 64), "RA:%d:%d" % (16 * a, 16 * a + 16), F.Sign, bias=d, scale=-1.0)
+                if a < 19:
+                    act(ct % (64 * a + 64 + e, 4 * C), "PSB:%d:320" % (16 * a + 16), F.Sign, bias=d, scale=-1.0)
+            act("CT%d" % w, "CT%d" % w, F.Relu, scale=-1.0)
+        for w in range(5):
+            for e in range(4 if w < WS else 0):
+                a = 4 * w + e
+                s, ct = "SS:%d:%d" % (16 * a + 15, 16 * a + 16), "CT%d:%%d:%%d:4" % w
+                if a:
+                    ts(ct % (e, 64 * a), "PS:0:%d" % (16 * a), s, A.is_gt)
+                ts(ct % (64 * a + e, 64 * a + 64), "RA:%d:%d" % (16 * a, 16 * a + 16), s, A.is_ge)
+                if a < 19:
+                    ts(ct % (64 * a + 64 + e, 4 * C), "PS:%d:320" % (16 * a + 16), s, A.is_ge)
+            quant("C%d" % w, "CT%d" % w)
+            mm("PK", "OB", 0, "C%d" % w, w == 0, w == 4)
+        act("STEP", "PK:0:320", F.Copy, scale=512.0)
+        old, new = names[t % 2], names[(t + 1) % 2]
+        tt(new, "STEP@COFF", old, A.add)
+
+        def deal(t=t, arr=arr):
+            banks = ("PH", "PS", "PSB", "PK")
+            for b in range(4):
+                mm(banks[b], "L", P * b, "A%d" % t, extra=[(arr, cnt[arr])])
+            for b in range(4):
+                act("HB%d" % b, banks[b] + ":1:320:2", F.Copy, scale=0.03125)
+
+        def final(new=new):
+            if last:
+                tt("PT0", new, "JR", A.subtract)
+                ts("PT1", "PT0", 2.0 ** -9, A.mult, -1.0, A.add)
+                quant("V", "VT")
+
+        order(new, not last, (2896, 3216, NV)[t], final, deal)
+        if last:
+            dma("dpt", [("y", T.pt[:, :], T.PT1[0:P:16, :])], [], ["PT1"])
+        for b in range(4):
+            if last and b > 1:
+                cp("GB%d" % b, "HB%d@C2OFF" % b)
+            else:
+                act("GB%d" % b, "HB%d@C2OFF" % b, F.Copy)
+        if not last:
+            lists1(t + 1 < R - 1)
+        for b in range(4):
+            tt("X:%d:1280:4" % b, "GB%d" % b, "PF%d:0:320" % b, A.add)
+        quant("X", "X")
+        if not last:
+            unpack()
+
+    mm("PS", "V", 0, "X")
+    dma("dout", [("y", T.oc[:, :], T.qX[:, 0:C].bitcast(dt.uint8))] +
+        [("ys"[k % 2], T.osc[4 * k:4 * k + 4, :], T.sX[32 * k:32 * k + 4, 0:C]) for k in range(4)], [], ["qX", "sX"])
+    act("YB", "PS:0:320", F.Copy)
+    dma("dy", [("s", T.y[:, :], T.YB[:, :])], [], ["YB"])
+    wait("g", list(cnt.items()))

@@ -3,11 +3,13 @@ from concourse.mybir import dt, AluOpType as A, ActivationFunctionType as F
 C, P, R = 320, 128, 3
 NV = 3520
 NULL = 3528
-WW = 3936
-NS = 11
-WS = 3
-CS = 64 * WS
+WW = 2 * NV + C
+NS = 9
+SKEYS = (0, 19, 1, 18, 2, 17, 3, 16)
+VKEYS = tuple(a for a in range(20) if a not in SKEYS)
 BIG = 4194304.0
+HUGE = 1e25
+WHOLE = 12582912.0
 
 SCRATCH, AT = {}, {}
 
@@ -25,31 +27,35 @@ def _t(n, d, parts, where="sbuf"):
     SCRATCH[n] = (where, [P, a], d)
 
 
-for _n, _w in (("E16", C), ("JR", C), ("E32", 640), ("TNY", 1), ("MASK", C), ("MSKA", C), ("RS", C), ("MB0", C), ("MB", C),
-               ("KF0", C), ("KFA", C), ("KFB", C), ("KM", C), ("KS", C), ("S1", C), ("S2", C), ("OWD", 336), ("O2", C), ("O3", C), ("IX", C),
-               ("MM", C), ("MS", C), ("SM", C), ("SS", C), ("DD", C), ("DM", C), ("RA", C), ("NA", 20 - 4 * WS), ("ND", 20 - 4 * WS), ("STEP", C),
-               ("PT0", C), ("PT1", C), ("YB", C)):
+for _n, _w in (("E16", C), ("JR", C), ("JP0", C), ("JP", C), ("TNY", 1), ("MASK", C), ("RS", C), ("MB0", C), ("MB", C), ("SEL", C), ("HOLD", C),
+               ("KP", C), ("KFA", C), ("KFB", C), ("KM", C), ("KS", C), ("S1", C), ("S2", C), ("OWD", 336), ("O2", C), ("O3", C),
+               ("MM", C), ("MS", C), ("SM", C + 1), ("SS", C), ("SX", C), ("NA", 20), ("ND", 20), ("STEP", C), ("PT1", C), ("YB", C),
+               ("XA", 40), ("XB", 40), ("OW", 40)):
     _b(_n, _w)
 _t("SKB", "float32", [("SK", C), ("SKE", 16)])
-_t("CTAB", "float32", [("C16", 20), ("C1", 20), ("QP", 4), ("Q20", 4), ("ODD", 4), ("EVN", 4), ("NO", 4), ("NE", 4), ("DUMP", 20)])
-_t("FTAB", "float32", [("ACC", 20), ("RKP", 20), ("DU", 20), ("DT", 20), ("OW", 20), ("IXM", 20)])
-_t("VSB", "float16", [("VS%d" % k, 160) for k in range(20 - NS)])
+_t("CTAB", "float32", [("C16", 20), ("C1", 20), ("QP", 4), ("Q20", 4), ("ODD", 4), ("EVN", 4), ("NO", 4), ("NE", 4), ("CR", 4), ("CH", 4),
+                       ("TOP", 4), ("JT0", 20), ("JT", 20)])
+_t("FTAB", "float32", [("ACC", 20), ("TH", 12), ("IXM", 20)])
+_b("VSB", 160 * (20 - NS), "float16")
 _b("GS", 640, "float16")
-_t("CTABI", "int32", [("QI", 4), ("QA", 4), ("QB", 4)])
-_t("ITAB", "int32", [("KI", 20), ("PI", 20), ("SI", 40), ("SH", 40), ("PL", 20), ("CI", 20), ("C2I", 20), ("MI", 20), ("MJ", 20), ("NJ", 20)])
+_t("CTABI", "int32", [("QI", 4), ("QA", 4), ("QB", 4), ("QC", 4)])
+_t("ITAB", "int32", [("P1", 20), ("P2", 20), ("MI", 20), ("NJ", 20)])
 _t("UTAB", "uint16", [("OQ", 40)] + [(k, 20) for k in ("PERM", "RP", "OWU", "COFF", "C2OFF", "P2U", "IXU", "MOFF", "NOFF")])
+_b("R16", C, "uint16")
 _b("UI", 8, "int32")
 _b("PR", C, "int32")
+_b("PTAB", 20, "int32")
 _b("UL", 8, "uint16")
-for _n, _w in (("ZER", 512), ("ONE", 512), ("OB1", 512), ("OB2", 512), ("CDF", C), ("ONES", C), ("UT", 512), ("VT", 512), ("X", 4 * C),
-               ("Z", 4 * C), ("W", WW), ("CC", NV), ("D", 3536), ("G", 640), ("GT", 640), ("W2", 8 * C), ("N2", 4 * C), ("RS32", 640)):
+for _n, _w in (("ZER", 512), ("ONE", 512), ("ZD", 512), ("OB1", 512), ("OB2", 512), ("CDF", C), ("ONES", C), ("UT", 512), ("VT", 512), ("X", 4 * C),
+               ("Z", 4 * C), ("W", WW), ("CC", NV), ("D", 3536), ("G", 640), ("GT", 640), ("W2", 8 * C), ("N2", 4 * C), ("RKX", 640),
+               ("MBH", C), ("IX", C)):
     _b(_n, _w, "bfloat16")
 _t("JUNK", "bfloat16", [("JUNK%d" % k, C) for k in range(NS)])
 _t("CMPB", "bfloat16", [("CMP%d" % k, C) for k in range(20 - NS)])
 _t("EBB", "bfloat16", [("EB%d" % k, 512) for k in range(4)])
 for _n, _w in (("FH", C), ("GB", C), ("HB", 160)):
     _t(_n + "B", "bfloat16", [("%s%d" % (_n, k), _w) for k in range(4)])
-_t("CTB", "bfloat16", [("CT%d" % k, 4 * C) for k in range(5)])
+_t("CTB", "bfloat16", [("CT%d" % k, 4 * C) for k in range(6)])
 _t("PFB", "float32", [("PF%d" % k, 512) for k in range(4)], "psum")
 for _n in ("PS", "PSB", "PK", "PH"):
     _b(_n, 512, "float32", "psum")
@@ -58,10 +64,10 @@ for _n, _w in [("OB", P), ("U", P), ("UR", P), ("V", P), ("L", 512), ("X", C)] +
     _b("s" + _n, _w, "uint8")
 for _n, _d in (("q", "float8_e4m3fn_x4"), ("s", "uint8")):
     _t(_n + "EB", _d, [("%sE%d" % (_n, k), P) for k in range(4)])
-    _t(_n + "CB", _d, [("%sC%d" % (_n, k), C) for k in range(5)])
+    _t(_n + "CB", _d, [("%sC%d" % (_n, k), C) for k in range(6)])
 PSUM = ["PF0", "PF1", "PF2", "PF3", "PS", "PSB", "PK", "PH"]
 
-SEMAPHORES = ["cv", "cs", "ct", "cg", "dp", "dx", "du", "dv", "dw", "dz", "dd", "de", "dout", "dpt", "dy", "sent"] + ["arr%d" % k for k in range(R)]
+SEMAPHORES = ["cv", "cs", "ct", "cg", "dp", "dt", "dx", "du", "dv", "dw", "dz", "dd", "de", "dout", "dpt", "dy", "sent"] + ["arr%d" % k for k in range(R)]
 
 
 def region(s):
@@ -166,6 +172,9 @@ def rank_program(g, core, T, topo):
     def quant(q, t):
         op("v", lambda: V.quantize_mx(ap("q" + q), ap("s" + q), ap(t)), ["q" + q, "s" + q], [t])
 
+    def turn(o, i):
+        op("v", lambda: V.transpose(ap(o), ap(i)), [o], [i])
+
     def mm(ps, a, a0, b, start=True, stop=True, extra=()):
         r = ":%d:%d" % (a0, a0 + P)
         i = ["q" + a + r, "s" + a + r, "q" + b, "s" + b]
@@ -174,12 +183,12 @@ def rank_program(g, core, T, topo):
     def act(o, i, f, acc=None, bias=None, scale=None):
         kw = {}
         if bias is not None:
-            kw["bias"] = ap(bias)
+            kw["bias"] = ap(bias) if isinstance(bias, str) else bias
         if scale is not None:
             kw["scale"] = scale
         if acc is not None:
             kw["accum_out"] = ap(acc)
-        op("s", lambda: S.activation(ap(o), ap(i), f, **kw), [o] + [s for s in (acc,) if s], [i] + [s for s in (bias,) if s])
+        op("s", lambda: S.activation(ap(o), ap(i), f, **kw), [o] + [s for s in (acc,) if s], [i] + [s for s in (bias,) if isinstance(s, str)])
 
     def iota(n, pattern, base=0, cm=0):
         kw = {} if SCRATCH[AT[n.split(":")[0]][0]][2] == "int32" else {"allow_small_or_imprecise_dtypes": True}
@@ -189,72 +198,97 @@ def rank_program(g, core, T, topo):
         op("g", lambda: g.affine_select(ap(o), ap(i), pattern, cop, c, base, cm), [o], [i])
 
     dma("dp", [("ys"[k % 2], T.PR[k:P:16, :], T.p[:, :]) for k in range(16)], ["PR"], [])
+    dma("dt", [("s", T.PTAB[:, :], T.p[:, :])], ["PTAB"], [])
     dma("dx", [("y", T.X[:, :], T.x[:, :])], ["X"], [])
     dma("du", [("y", T.UT[:, :], T.u[:, :])], ["UT"], [])
 
     iota("QI:0:2", [[0, 2]], 0, 1)
+    iota("C16", [[16, 20]])
+    iota("JP0", [[1, 16], [16, 20]], 352)
     iota("C1", [[1, 20]])
     iota("E16", [[0, 20], [1, 16]])
     iota("JR", [[1, C]])
-    iota("C16", [[16, 20]])
-    iota("E32", [[0, 20], [1, 32]])
-    iota("W", [[0, WW]], -160)
+    iota("W:0:%d" % NV, [[0, NV]], -160)
     fill("ZER", 0.0)
     fill("ONE", 1.0)
-    dma("dz", [("y", T.D[:, a:min(a + 512, 3536)], T.ZER[:, 0:min(512, 3536 - a)]) for a in range(0, 3536, 512)], ["D"], ["ZER"])
-    dma("dw", [("y", T.qL[:, 0:512].bitcast(dt.uint8), T.wc[:, :]), ("y", T.sL[:, 0:512], T.ws[:, :])], ["qL", "sL"], [])
-    dma("dv", [("y", T.VT[:, :], T.v[:, :])], ["VT"], [])
     ts("QA:0:2", "QI:0:2", 15, A.bitwise_and)
     ts("QB:0:2", "QI:0:2", 4, A.arith_shift_right, 1, A.bitwise_and)
+    ts("QC:0:2", "QI:0:2", 31, A.bitwise_and)
     cp("QP:0:1", "QA:0:1")
     cp("ODD:0:1", "QB:0:1")
+    ts("TOP:0:1", "QC:0:1", 31.0, A.is_equal, 4096.0, A.mult)
     ts("Q20:0:1", "QP:0:1", 20.0, A.mult)
+    ts("JT0", "C16", "QP:0:1", A.add, 352.0, A.add)
+    ts("CR:0:1", "QP:0:1", -1.0 / 32, A.mult, 160.5 / 32, A.add)
+    ts("CH:0:1", "QP:0:1", -1.0 / 32, A.mult, 176.0 / 32, A.add)
+    ts("ZD", "ONE", "TOP:0:1", A.mult)
+    ts("JP", "JP0", 2.0 ** -9, A.mult)
+    ts("JT", "JT0", 2.0 ** -9, A.mult)
+    for a in range(0, 2560, 512):
+        act("D:%d:%d" % (a, a + 512), "ZER", F.Identity, bias="TOP:0:1")
+    dma("dz", [("y", T.D[:, a:min(a + 512, 3536)], T.ZD[:, 0:min(512, 3536 - a)]) for a in range(2560, 3536, 512)], ["D:2560:3536"], ["ZD"])
+    dma("dw", [("y", T.qL[:, 0:512].bitcast(dt.uint8), T.wc[:, :]), ("y", T.sL[:, 0:512], T.ws[:, :])], ["qL", "sL"], [])
+    dma("dv", [("y", T.VT[:, :], T.v[:, :])], ["VT"], [])
     ts("PERM", "C1", "Q20:0:1", A.add)
     ts("EVN:0:1", "ODD:0:1", -1.0, A.mult, 1.0, A.add)
     ts("NO:0:1", "ODD:0:1", float(NULL), A.mult)
     ts("NE:0:1", "EVN:0:1", float(NULL), A.mult)
-    ts("MASK", "E16", "QP:0:1", A.is_equal)
-    ts("RS", "E16", 0.0, A.is_gt)
+    fill("SKE", 3600.0)
+    fill("XA:0:40:2", 0.0)
+    ts("XB:0:40:2", "C16", "QP:0:1", A.add, float(NV), A.add)
     ts("MB0", "E16", "QP:0:1", A.is_lt)
-    ts("CDF", "JR", -159.0, A.add)
-    ts("MB", "MB0", 2.0 * BIG, A.mult, -BIG, A.add)
-    ts("DUMP", "C16", "QP:0:1", A.add, 3600.0, A.add)
-    fill("SKE", 3600.0 * 512.0)
-    fill("ONES", 1.0)
-    act("RS32", "E32", F.Sign)
     for b in range(4):
         sel("EB%d" % b, "ZER", [[1, 512]], A.not_equal, 1.0, -b, -4)
     iota("W2", [[0, 8 * C]])
     iota("UI", [[16, 8]])
     sel("OB1", "ONE", [[-16, 8], [0, 64]], A.is_ge, 0.0, 0, 1)
     sel("OB2", "OB1", [[16, 8], [0, 64]], A.is_ge, 0.0, 15, -1)
-    cp("KF0", "PR@PERM")
-    ts("KFB", "KF0", 512.0, A.mult, 512.0, A.add)
-    tt("KFA", "KFB", "JR", A.add)
+    tt("KP", "PR", "JP", A.add)
+    tt("KS:15:320:16", "PTAB", "JT", A.add)
+
+    def constants():
+        act("KFA", "KP@PERM", F.Copy)
+        act("MB", "MB0", F.Identity, bias=-BIG, scale=2.0 * BIG)
+        act("CDF", "JR", F.Identity, bias=-159.0)
+        act("MBH", "MB0", F.Identity, bias=-1024.0, scale=2048.0)
+        act("RS", "E16", F.Sign)
+        act("HOLD", "RS", F.Identity, bias=-HUGE, scale=2.0 * HUGE)
+        act("ONES", "ONE:0:320", F.Copy)
+        for a in range(0, 4 * C, 512):
+            act("CT5:%d:%d" % (a, min(a + 512, 4 * C)), "ZER:0:%d" % min(512, 4 * C - a), F.Copy)
 
     def unpack():
         for b in range(4):
             mm("PF%d" % b, "E%d" % b, 0, "X")
-        for b in range(4):
+        for b in range(2):
             act("FH%d" % b, "PF%d:0:320" % b, F.Copy, scale=0.5)
 
     def first_tiles():
+        ts("MASK", "E16", "QP:0:1", A.is_equal)
         for b in range(4):
             quant("E%d" % b, "EB%d" % b)
-        quant("X", "X")
-        unpack()
 
-    def sides():
-        cp("UL", "UI")
-        quant("U", "UT")
-        quant("OB", "OB2")
-        op("v", lambda: V.tensor_copy(T.qUR[:, 0:P].bitcast(dt.uint32), T.qU[:, 0:P].bitcast(dt.uint32).indirect(T.UL[:, 0:8])), ["qUR"], ["qU", "UL"])
-        cp("sUR", "sU@UL")
-        fill("TNY", 2.0 ** -126)
-        ts("MSKA", "E16", "QP:0:1", A.is_le)
+    def sides(k):
+        if k == 0:
+            quant("X", "X")
+            unpack()
+            for b in range(2, 4):
+                act("FH%d" % b, "PF%d:0:320" % b, F.Copy, scale=0.5)
+            act("SEL", "MASK", F.Identity, bias=-HUGE, scale=2.0 * HUGE)
+        elif k == 1:
+            cp("UL", "UI")
+            quant("U", "UT")
+        elif k == 2:
+            quant("OB", "OB2")
+        elif k == 3:
+            op("v", lambda: V.tensor_copy(T.qUR[:, 0:P].bitcast(dt.uint32), T.qU[:, 0:P].bitcast(dt.uint32).indirect(T.UL[:, 0:8])), ["qUR"], ["qU", "UL"])
+        elif k == 4:
+            act("sUR", "sU@UL", F.Copy)
+            fill("TNY", 2.0 ** -126)
+            fill("SM:0:1", -HUGE)
 
     def half(k):
-        scan("VS%d" % k, "CMP%d:0:160" % k, "CMP%d:160:320" % k, 0.0, A.add, A.add)
+        scan("VSB:%d:%d" % (160 * k, 160 * k + 160), "CMP%d:0:160" % k, "CMP%d:160:320" % k, 0.0, A.add, A.add)
 
     def spread(sem, a, b):
         moves = []
@@ -265,30 +299,38 @@ def rank_program(g, core, T, topo):
                 moves.append((T.D[h:16 * h:16, a + 1:b + 1], T.CC[16 * h + 8:16 * h + 8 + h, a:b]))
         dma(sem, [("ys"[k % 2], o, i) for k, (o, i) in enumerate(moves)], ["D:%d:%d" % (a, b)], ["CC:%d:%d" % (a, b)])
 
-    def order(kf, joined, nv, during, scalar_tail):
-        tt("KM", kf, "MASK", A.mult)
-        scan("KS", "RS", "KM", 0.0, A.mult, A.add)
-        for c in range(NS):
-            act("JUNK%d" % c, kf, F.Sign, acc="ACC:%d:%d" % (c, c + 1), bias="KS:%d:%d" % (16 * c + 15, 16 * c + 16), scale=-1.0)
-        n = 20 - NS
-        for k in range(n):
-            c = NS + k
-            ts("CMP%d" % k, kf, "KS:%d:%d" % (16 * c + 15, 16 * c + 16), A.is_lt)
-            if k:
-                half(k - 1)
-        half(n - 1)
-        ts("RP:0:%d" % NS, "ACC:0:%d" % NS, 319.0, A.add, 0.5, A.mult)
-        op("v", lambda: V.tensor_copy(ap("RP:%d:20" % NS), T.VSB[:, 159:160 * n:160]), ["RP:%d:20" % NS], ["VS%d" % k for k in range(n)])
+    def order(kf, first, joined, nv, during, scalar_tail):
+        row = "KP" if first else kf
+        if not first:
+            scan("KM", kf, "MASK", 0.0, A.max, A.mult)
+        ts("R16", row, 16.0, A.mult, "CR:0:1", A.add)
+        if not first:
+            scan("KS", "RS", "KM", 0.0, A.mult, A.add)
+        key = ["KS:%d:%d" % (16 * c + 15, 16 * c + 16) for c in range(20)]
+        for k in range(NS):
+            act("JUNK%d" % k, row, F.Sign, acc="ACC:%d:%d" % (k, k + 1), bias=key[2 * k], scale=-1.0)
+        if first:
+            constants()
+        ts("TH:0:10", "KS:31:320:32", 16.0, A.mult, "CH:0:1", A.add)
+        for k in range(10, 20 - NS):
+            ts("CMP%d" % k, row, key[2 * (NS + k - 10)], A.is_lt)
+        for k in range(10):
+            ts("CMP%d" % k, "R16", "TH:%d:%d" % (k, k + 1), A.is_lt)
+            half((k - 1) % (20 - NS))
+        for k in range(9, 19 - NS):
+            half(k)
+        ts("RP:0:%d:2" % (2 * NS), "ACC:0:%d" % NS, 319.0, A.add, 0.5, A.mult)
+        cp("RP:%d:20:2" % (2 * NS), "VSB:1759:%d:160" % (160 * (20 - NS)))
+        cp("RP:1:20:2", "VSB:159:1600:160")
         cp("SK@RP", kf)
         scan("S1", "SK", "MB", 0.0, A.min, A.max)
         op("v", lambda: V.tensor_tensor_scan(ap("S2"), T.SKB[:, 1:C + 1], ap("MB"), 0.0, A.min, A.max), ["S2"], ["SK", "SKE", "MB"])
-        tt("SI:0:20", "S1:15:320:16", "SK:0:320:16", A.max)
-        tt("SI:20:40", "S2:15:320:16", "SK:1:320:16", A.max)
-        ts("SH", "SI", 9, A.arith_shift_right)
-        tt("DU", "SH:0:20", "SH:20:40", A.is_equal)
-        tt("DT", "DU", "DUMP", A.mult)
-        tt("OW", "DT", "SH:0:20", A.max)
-        cp("OWU", "OW")
+        tt("P1", "S1:15:320:16", "SK:0:320:16", A.max)
+        tt("XB:1:40:2", "S1:15:320:16", "SK:0:320:16", A.max)
+        tt("P2", "S2:15:320:16", "SK:1:320:16", A.max)
+        tt("XA:1:40:2", "P1", "P2", A.is_equal)
+        scan("OW", "XA", "XB", 0.0, A.mult, A.add)
+        cp("OWU", "OW:1:40:2")
         cp("W@OWU", "CDF")
         h = nv // 2
         lo, hi = "0:%d" % h, "%d:%d" % (h, nv)
@@ -297,58 +339,70 @@ def rank_program(g, core, T, topo):
         scan("CC:" + hi, "W:" + hi, "W:" + hi, "CC:%d:%d" % (h - 1, h), A.max, A.max)
         spread("de", h, nv)
         scalar_tail()
-        cp("KI", "KS:15:320:16")
-        ts("RKP", "RP", 1120.0, A.add)
-        ts("PI", "KI", 9, A.arith_shift_right)
+        if first:
+            fill("RKX", 32768.0)
+        ts("OQ:0:40:2", "KS:15:320:16", "EVN:0:1", A.mult, "NO:0:1", A.add)
+        ts("OQ:1:40:2", "KS:15:320:16", "ODD:0:1", A.mult, "NE:0:1", A.add)
         if joined:
-            iota("W", [[0, WW]], -160)
+            iota("W:0:%d" % NV, [[0, NV]], -160)
             cp("OWD@RP", "JR")
-        ts("OQ:0:40:2", "PI", "EVN:0:1", A.mult, "NO:0:1", A.add)
-        ts("OQ:1:40:2", "PI", "ODD:0:1", A.mult, "NE:0:1", A.add)
+        ts("RKX:0:640:32", "RP", -160.0, A.add)
         if joined:
             cp("OWD:320:321", "OWD:319:320")
             ts("O2", "OWD:0:320", 512.0, A.mult)
             tt("O3", "O2", "OWD:1:321", A.add)
         during()
-        cp("G", "D@OQ")
-        op("v", lambda: V.transpose(ap("GT"), ap("G")), ["GT"], ["G"])
-        scan("GS", "RS32", "GT", 0.0, A.mult, A.add)
-        tt("PL", "GS:31:640:32", "RKP", A.add)
-        ts("C2I", "PL", 4, A.arith_shift_right)
-        cp("C2OFF", "C2I")
+        act("G:320:640", "D@OQ:20:40", F.Copy)
+        cp("G:0:320", "D@OQ:0:20")
+        turn("GT:0:320", "G:0:320")
+        turn("GT:320:640", "G:320:640")
+        scan("GS", "RKX", "GT", 4096.0, A.min, A.add)
+        ts("C2OFF", "GS:30:640:32", 1.0 / 16, A.mult, 80.0 - 15.0 / 32, A.add)
 
-    def lists1(again):
-        cp("P2U", "PL")
-        ts("CI", "PL", 3, A.arith_shift_right)
+    def add_x(b):
+        tt("X:%d:1280:4" % b, "GB%d" % b, "PF%d:0:320" % b, A.add)
+
+    def lists(again, deal):
+        ts("P2U", "GS:30:640:32", 1280.0, A.add)
+        ts("COFF", "GS:30:640:32", 1.0 / 8, A.mult, 160.0 - 7.0 / 16, A.add)
         cp("W2@P2U", "ONES")
-        cp("COFF", "CI")
+        deal(0)
         scan("N2", "W2:0:2560:2", "W2:1:2560:2", -160.0, A.add, A.add)
         if again:
             iota("W2", [[0, 8 * C]])
-
-    def lists2():
-        scan("IX", "N2:3:1280:4", "MB", 0.0, A.min, A.max)
+        deal(1)
+        scan("IX", "N2:3:1280:4", "MBH", 0.0, A.min, A.max)
+        deal(2)
         tt("IXM", "IX:15:320:16", "N2:3:1280:64", A.max)
+        deal(3)
         ts("IXU", "IXM", 159.0, A.add, 0.0, A.max)
+        deal(4)
         tt("MM", "O3@IXU", "MASK", A.mult)
         scan("MS", "RS", "MM", 0.0, A.mult, A.add)
-        ts("MJ", "MS:15:320:16", 2.0 ** -9, A.mult, -0.3125, A.add)
+        ts("MOFF", "MS:15:320:16", 2.0 ** -9, A.mult, -0.3125, A.add)
         cp("MI", "MS:15:320:16")
-        cp("MOFF", "MJ")
+        deal(5)
         ts("NJ", "MI", 511, A.bitwise_and)
+        deal(6)
         cp("NOFF", "NJ")
 
-    order("KFA", True, 2576, first_tiles, lambda: None)
-    lists1(True)
+    def new_x(k):
+        if k < 4:
+            add_x(k)
+        elif k == 4:
+            quant("X", "X")
+            unpack()
+        else:
+            ts("FH%d" % (k - 3), "PF%d:0:320" % (k - 3), 0.5, A.mult)
+
+    order("KFA", True, True, 2576, first_tiles, lambda: None)
+    lists(True, sides)
     names = ["KFA", "KFB"]
     for t in range(R):
         last = t == R - 1
-        lists2()
         qz = "Z%d" % t
         for b in range(4):
             act("GB%d" % b, "FH%d@MOFF" % b, F.Copy)
-        if t == 0:
-            sides()
         for b in range(4):
             tt("Z:%d:1280:4" % b, "FH%d@NOFF" % b, "GB%d" % b, A.add)
         quant(qz, "Z")
@@ -361,36 +415,29 @@ def rank_program(g, core, T, topo):
         cnt["sent"], cnt[arr] = cnt.get("sent", 0) + n, n
         mm("PS", "UR", 0, qz)
         mm("PSB", "UR", 0, qz)
-        tt("SM", "PS:0:320", "MASK", A.mult)
-        act("DD", "PSB:0:320", F.Abs, bias="TNY", scale=1.01 * 2.0 ** -24)
-        scan("SS", "RS", "SM", 0.0, A.mult, A.add)
-        tt("DM", "DD", "MSKA", A.mult)
-        keys = "SS:%d:320:16" % (CS + 15)
-        act("NA", keys, F.Abs, bias="TNY", scale=1.01 * 2.0 ** -24)
-        tt("RA", "PS:0:320", "DM", A.subtract)
-        tt("ND", keys, "NA", A.subtract)
-        for w in range(WS, 5):
-            for e in range(4):
-                a = 4 * w + e
-                s, ct, d = "SS:%d:%d" % (16 * a + 15, 16 * a + 16), "CT%d:%%d:%%d:4" % w, "ND:%d:%d" % (a - 4 * WS, a - 4 * WS + 1)
-                if a:
-                    act(ct % (e, 64 * a), "PSB:0:%d" % (16 * a), F.Sign, bias=s, scale=-1.0)
-                act(ct % (64 * a + e, 64 * a + 64), "RA:%d:%d" % (16 * a, 16 * a + 16), F.Sign, bias=d, scale=-1.0)
+        tt("SM:1:321", "PS:0:320", "SEL", A.min)
+        scan("SS", "HOLD", "SM:1:321", -HUGE, A.min, A.max)
+        act("NA", "SS:15:320:16", F.Abs, bias="TNY", scale=1.01 * 2.0 ** -24)
+        scan("SX", "SM:0:320", "HOLD", -HUGE, A.max, A.min)
+        tt("ND", "SS:15:320:16", "NA", A.subtract)
+        tt("CT5:0:1280:4", "PS:0:320", "SX", A.is_equal)
+        for w in range(3, 5):
+            ks = list(enumerate(SKEYS[4 * w - 12:4 * w - 8]))
+            for e, a in ks:
+                act("CT%d:%d:%d:4" % (w, e, 64 * a + 64), "PSB:0:%d" % (16 * a + 16), F.Sign, bias="SS:%d:%d" % (16 * a + 15, 16 * a + 16), scale=-1.0)
+            for e, a in ks:
                 if a < 19:
-                    act(ct % (64 * a + 64 + e, 4 * C), "PSB:%d:320" % (16 * a + 16), F.Sign, bias=d, scale=-1.0)
+                    act("CT%d:%d:1280:4" % (w, 64 * a + 64 + e), "PSB:%d:320" % (16 * a + 16), F.Sign, bias="ND:%d:%d" % (a, a + 1), scale=-1.0)
             act("CT%d" % w, "CT%d" % w, F.Relu, scale=-1.0)
-        for w in range(5):
-            for e in range(4 if w < WS else 0):
-                a = 4 * w + e
-                s, ct = "SS:%d:%d" % (16 * a + 15, 16 * a + 16), "CT%d:%%d:%%d:4" % w
-                if a:
-                    ts(ct % (e, 64 * a), "PS:0:%d" % (16 * a), s, A.is_gt)
-                ts(ct % (64 * a + e, 64 * a + 64), "RA:%d:%d" % (16 * a, 16 * a + 16), s, A.is_ge)
-                if a < 19:
-                    ts(ct % (64 * a + 64 + e, 4 * C), "PS:%d:320" % (16 * a + 16), s, A.is_ge)
+        tiles = (0, 5, 1, 3, 2, 4)
+        for w in tiles:
+            for e, a in enumerate(VKEYS[4 * w:4 * w + 4]):
+                s = "SS:%d:%d" % (16 * a + 15, 16 * a + 16)
+                ts("CT%d:%d:%d:4" % (w, e, 64 * a + 64), "PS:0:%d" % (16 * a + 16), s, A.is_gt)
+                ts("CT%d:%d:1280:4" % (w, 64 * a + 64 + e), "PS:%d:320" % (16 * a + 16), s, A.is_ge)
             quant("C%d" % w, "CT%d" % w)
-            mm("PK", "OB", 0, "C%d" % w, w == 0, w == 4)
-        act("STEP", "PK:0:320", F.Copy, scale=512.0)
+            mm("PK", "OB", 0, "C%d" % w, w == tiles[0], w == tiles[-1])
+        act("STEP", "PK:0:320", F.Copy)
         old, new = names[t % 2], names[(t + 1) % 2]
         tt(new, "STEP@COFF", old, A.add)
 
@@ -403,11 +450,10 @@ def rank_program(g, core, T, topo):
 
         def final(new=new):
             if last:
-                tt("PT0", new, "JR", A.subtract)
-                ts("PT1", "PT0", 2.0 ** -9, A.mult, -1.0, A.add)
+                ts("PT1", new, WHOLE, A.add, WHOLE + 1.0, A.subtract)
                 quant("V", "VT")
 
-        order(new, not last, (2896, 3216, NV)[t], final, deal)
+        order(new, False, not last, (2896, 3216, NV)[t], final, deal)
         if last:
             dma("dpt", [("y", T.pt[:, :], T.PT1[0:P:16, :])], [], ["PT1"])
         for b in range(4):
@@ -416,13 +462,11 @@ def rank_program(g, core, T, topo):
             else:
                 act("GB%d" % b, "HB%d@C2OFF" % b, F.Copy)
         if not last:
-            lists1(t + 1 < R - 1)
-        for b in range(4):
-            tt("X:%d:1280:4" % b, "GB%d" % b, "PF%d:0:320" % b, A.add)
-        quant("X", "X")
-        if not last:
-            unpack()
+            lists(t + 1 < R - 1, new_x)
 
+    for b in (2, 0, 3, 1):
+        add_x(b)
+    quant("X", "X")
     mm("PS", "V", 0, "X")
     dma("dout", [("y", T.oc[:, :], T.qX[:, 0:C].bitcast(dt.uint8))] +
         [("ys"[k % 2], T.osc[4 * k:4 * k + 4, :], T.sX[32 * k:32 * k + 4, 0:C]) for k in range(4)], [], ["qX", "sX"])

@@ -4,9 +4,10 @@ C, P, R = 320, 128, 3
 NV = 3520
 NULL = 3528
 WW = 2 * NV + C
-NS = 9
+NS = 10
 SKEYS = (0, 19, 1, 18, 2, 17, 3, 16)
 VKEYS = tuple(a for a in range(20) if a not in SKEYS)
+HALVES, LISTS = (":0:160", ":160:320"), (":0:10", ":10:20")
 BIG = 4194304.0
 HUGE = 1e25
 WHOLE = 12582912.0
@@ -28,18 +29,19 @@ def _t(n, d, parts, where="sbuf"):
 
 
 for _n, _w in (("E16", C), ("JR", C), ("JP0", C), ("JP", C), ("TNY", 1), ("MASK", C), ("RS", C), ("MB0", C), ("MB", C), ("SEL", C), ("HOLD", C),
-               ("KP", C), ("KFA", C), ("KFB", C), ("KM", C), ("KS", C), ("S1", C), ("S2", C), ("OWD", 336), ("O2", C), ("O3", C),
+               ("KP", C), ("KFA", C), ("KFB", C), ("KM", C), ("KS", C), ("S1", C), ("S2", C), ("OWD", 336), ("O0", C), ("O1", C), ("O2", C), ("O3", C),
                ("MM", C), ("MS", C), ("SM", C + 1), ("SS", C), ("SX", C), ("NA", 20), ("ND", 20), ("STEP", C), ("PT1", C), ("YB", C),
                ("XA", 40), ("XB", 40), ("OW", 40)):
     _b(_n, _w)
 _t("SKB", "float32", [("SK", C), ("SKE", 16)])
 _t("CTAB", "float32", [("C16", 20), ("C1", 20), ("QP", 4), ("Q20", 4), ("ODD", 4), ("EVN", 4), ("NO", 4), ("NE", 4), ("CR", 4), ("CH", 4),
                        ("TOP", 4), ("JT0", 20), ("JT", 20)])
-_t("FTAB", "float32", [("ACC", 20), ("TH", 12), ("IXM", 20)])
+_t("FTAB", "float32", [("ACC", 20), ("TH", 12), ("IXM", 20), ("NJ", 20)])
+_t("TAB", "bfloat16", [("TA", 12), ("TB", 12)])
 _b("VSB", 160 * (20 - NS), "float16")
 _b("GS", 640, "float16")
 _t("CTABI", "int32", [("QI", 4), ("QA", 4), ("QB", 4), ("QC", 4)])
-_t("ITAB", "int32", [("P1", 20), ("P2", 20), ("MI", 20), ("NJ", 20)])
+_t("ITAB", "int32", [("P1", 20), ("P2", 20), ("MI", 20)])
 _t("UTAB", "uint16", [("OQ", 40)] + [(k, 20) for k in ("PERM", "RP", "OWU", "COFF", "C2OFF", "P2U", "IXU", "MOFF", "NOFF")])
 _b("R16", C, "uint16")
 _b("UI", 8, "int32")
@@ -236,6 +238,7 @@ def rank_program(g, core, T, topo):
     fill("SKE", 3600.0)
     fill("XA:0:40:2", 0.0)
     ts("XB:0:40:2", "C16", "QP:0:1", A.add, float(NV), A.add)
+    fill("RKX", 32768.0)
     ts("MB0", "E16", "QP:0:1", A.is_lt)
     for b in range(4):
         sel("EB%d" % b, "ZER", [[1, 512]], A.not_equal, 1.0, -b, -4)
@@ -247,7 +250,6 @@ def rank_program(g, core, T, topo):
     tt("KS:15:320:16", "PTAB", "JT", A.add)
 
     def constants():
-        act("KFA", "KP@PERM", F.Copy)
         act("MB", "MB0", F.Identity, bias=-BIG, scale=2.0 * BIG)
         act("CDF", "JR", F.Identity, bias=-159.0)
         act("MBH", "MB0", F.Identity, bias=-1024.0, scale=2048.0)
@@ -290,6 +292,10 @@ def rank_program(g, core, T, topo):
     def half(k):
         scan("VSB:%d:%d" % (160 * k, 160 * k + 160), "CMP%d:0:160" % k, "CMP%d:160:320" % k, 0.0, A.add, A.add)
 
+    def offsets():
+        ts("OQ:0:40:2", "KS:15:320:16", "EVN:0:1", A.mult, "NO:0:1", A.add)
+        ts("OQ:1:40:2", "KS:15:320:16", "ODD:0:1", A.mult, "NE:0:1", A.add)
+
     def spread(sem, a, b):
         moves = []
         for h in range(8):
@@ -302,27 +308,37 @@ def rank_program(g, core, T, topo):
     def order(kf, first, joined, nv, during, scalar_tail):
         row = "KP" if first else kf
         if not first:
-            scan("KM", kf, "MASK", 0.0, A.max, A.mult)
-        ts("R16", row, 16.0, A.mult, "CR:0:1", A.add)
-        if not first:
-            scan("KS", "RS", "KM", 0.0, A.mult, A.add)
+            for r in HALVES:
+                scan("KM" + r, kf + r, "MASK" + r, 0.0, A.max, A.mult)
+            for r in HALVES:
+                scan("KS" + r, "RS" + r, "KM" + r, 0.0, A.mult, A.add)
         key = ["KS:%d:%d" % (16 * c + 15, 16 * c + 16) for c in range(20)]
         for k in range(NS):
             act("JUNK%d" % k, row, F.Sign, acc="ACC:%d:%d" % (k, k + 1), bias=key[2 * k], scale=-1.0)
         if first:
             constants()
+        ts("R16:0:160", row + ":0:160", 16.0, A.mult, "CR:0:1", A.add)
         ts("TH:0:10", "KS:31:320:32", 16.0, A.mult, "CH:0:1", A.add)
-        for k in range(10, 20 - NS):
-            ts("CMP%d" % k, row, key[2 * (NS + k - 10)], A.is_lt)
+        ts("TA:0:10", "KS:31:320:32", 16.0, A.mult, "CH:0:1", A.add)
+        ts("R16:160:320", row + ":160:320", 16.0, A.mult, "CR:0:1", A.add)
+        tt("TB:0:10", "TH:0:10", "TA:0:10", A.subtract)
+        if first:
+            cp("KFA", "KP@PERM")
+        else:
+            offsets()
         for k in range(10):
-            ts("CMP%d" % k, "R16", "TH:%d:%d" % (k, k + 1), A.is_lt)
-            half((k - 1) % (20 - NS))
-        for k in range(9, 19 - NS):
-            half(k)
-        ts("RP:0:%d:2" % (2 * NS), "ACC:0:%d" % NS, 319.0, A.add, 0.5, A.mult)
-        cp("RP:%d:20:2" % (2 * NS), "VSB:1759:%d:160" % (160 * (20 - NS)))
+            ts("CMP%d" % k, "R16", "TA:%d:%d" % (k, k + 1), A.subtract, "TB:%d:%d" % (k, k + 1), A.is_lt)
+            if k:
+                half(k - 1)
+        if first:
+            offsets()
+        half(9)
+        ts("RP:0:20:2", "ACC:0:10", 319.0, A.add, 0.5, A.mult)
         cp("RP:1:20:2", "VSB:159:1600:160")
         cp("SK@RP", kf)
+        if joined:
+            act("O0", "SK", F.Identity, bias=WHOLE)
+            act("O1", "O0", F.Identity, bias=-WHOLE)
         scan("S1", "SK", "MB", 0.0, A.min, A.max)
         op("v", lambda: V.tensor_tensor_scan(ap("S2"), T.SKB[:, 1:C + 1], ap("MB"), 0.0, A.min, A.max), ["S2"], ["SK", "SKE", "MB"])
         tt("P1", "S1:15:320:16", "SK:0:320:16", A.max)
@@ -336,27 +352,23 @@ def rank_program(g, core, T, topo):
         lo, hi = "0:%d" % h, "%d:%d" % (h, nv)
         scan("CC:" + lo, "W:" + lo, "W:" + lo, -160.0, A.max, A.max)
         spread("dd", 0, h)
+        ts("RKX:0:640:32", "RP", -160.0, A.add)
         scan("CC:" + hi, "W:" + hi, "W:" + hi, "CC:%d:%d" % (h - 1, h), A.max, A.max)
         spread("de", h, nv)
         scalar_tail()
-        if first:
-            fill("RKX", 32768.0)
-        ts("OQ:0:40:2", "KS:15:320:16", "EVN:0:1", A.mult, "NO:0:1", A.add)
-        ts("OQ:1:40:2", "KS:15:320:16", "ODD:0:1", A.mult, "NE:0:1", A.add)
         if joined:
             iota("W:0:%d" % NV, [[0, NV]], -160)
-            cp("OWD@RP", "JR")
-        ts("RKX:0:640:32", "RP", -160.0, A.add)
-        if joined:
+            scan("OWD:0:320", "SK", "O1", 0.0, A.max, A.subtract)
+            act("O2", "OWD:0:320", F.Identity, bias=161.0, scale=512.0)
             cp("OWD:320:321", "OWD:319:320")
-            ts("O2", "OWD:0:320", 512.0, A.mult)
-            tt("O3", "O2", "OWD:1:321", A.add)
+            scan("O3", "OWD:1:321", "O2", 1.0, A.min, A.add)
         during()
         act("G:320:640", "D@OQ:20:40", F.Copy)
         cp("G:0:320", "D@OQ:0:20")
-        turn("GT:0:320", "G:0:320")
-        turn("GT:320:640", "G:320:640")
-        scan("GS", "RKX", "GT", 4096.0, A.min, A.add)
+        for r in (":0:320", ":320:640"):
+            turn("GT" + r, "G" + r)
+        for r in (":0:320", ":320:640"):
+            scan("GS" + r, "RKX" + r, "GT" + r, 4096.0, A.min, A.add)
         ts("C2OFF", "GS:30:640:32", 1.0 / 16, A.mult, 80.0 - 15.0 / 32, A.add)
 
     def add_x(b):
@@ -377,14 +389,16 @@ def rank_program(g, core, T, topo):
         deal(3)
         ts("IXU", "IXM", 159.0, A.add, 0.0, A.max)
         deal(4)
-        tt("MM", "O3@IXU", "MASK", A.mult)
-        scan("MS", "RS", "MM", 0.0, A.mult, A.add)
-        ts("MOFF", "MS:15:320:16", 2.0 ** -9, A.mult, -0.3125, A.add)
+        for r, l in zip(HALVES, LISTS):
+            tt("MM" + r, "O3@IXU" + l, "MASK" + r, A.mult)
+        for r in HALVES:
+            scan("MS" + r, "RS" + r, "MM" + r, 0.0, A.mult, A.add)
+        ts("MOFF", "MS:15:320:16", -1.0, A.add)
         cp("MI", "MS:15:320:16")
         deal(5)
-        ts("NJ", "MI", 511, A.bitwise_and)
+        tt("NJ", "MS:15:320:16", "MI", A.subtract)
         deal(6)
-        cp("NOFF", "NJ")
+        ts("NOFF", "NJ", 512.0, A.mult, 160.0, A.add)
 
     def new_x(k):
         if k < 4:
@@ -415,8 +429,10 @@ def rank_program(g, core, T, topo):
         cnt["sent"], cnt[arr] = cnt.get("sent", 0) + n, n
         mm("PS", "UR", 0, qz)
         mm("PSB", "UR", 0, qz)
-        tt("SM:1:321", "PS:0:320", "SEL", A.min)
-        scan("SS", "HOLD", "SM:1:321", -HUGE, A.min, A.max)
+        for r, r1 in zip(HALVES, (":1:161", ":161:321")):
+            tt("SM" + r1, "PS" + r, "SEL" + r, A.min)
+        for r, r1 in zip(HALVES, (":1:161", ":161:321")):
+            scan("SS" + r, "HOLD" + r, "SM" + r1, -HUGE, A.min, A.max)
         act("NA", "SS:15:320:16", F.Abs, bias="TNY", scale=1.01 * 2.0 ** -24)
         scan("SX", "SM:0:320", "HOLD", -HUGE, A.max, A.min)
         tt("ND", "SS:15:320:16", "NA", A.subtract)
@@ -429,17 +445,18 @@ def rank_program(g, core, T, topo):
                 if a < 19:
                     act("CT%d:%d:1280:4" % (w, 64 * a + 64 + e), "PSB:%d:320" % (16 * a + 16), F.Sign, bias="ND:%d:%d" % (a, a + 1), scale=-1.0)
             act("CT%d" % w, "CT%d" % w, F.Relu, scale=-1.0)
-        tiles = (0, 5, 1, 3, 2, 4)
-        for w in tiles:
-            for e, a in enumerate(VKEYS[4 * w:4 * w + 4]):
-                s = "SS:%d:%d" % (16 * a + 15, 16 * a + 16)
-                ts("CT%d:%d:%d:4" % (w, e, 64 * a + 64), "PS:0:%d" % (16 * a + 16), s, A.is_gt)
-                ts("CT%d:%d:1280:4" % (w, 64 * a + 64 + e), "PS:%d:320" % (16 * a + 16), s, A.is_ge)
-            quant("C%d" % w, "CT%d" % w)
-            mm("PK", "OB", 0, "C%d" % w, w == tiles[0], w == tiles[-1])
+        after = {0: (5,), 4: (0,), 8: (1, 3), 11: (4, 2)}
+        for k, a in enumerate(VKEYS):
+            w, e, s = k // 4, k % 4, "SS:%d:%d" % (16 * a + 15, 16 * a + 16)
+            ts("CT%d:%d:%d:4" % (w, e, 64 * a + 64), "PS:0:%d" % (16 * a + 16), s, A.is_gt)
+            ts("CT%d:%d:1280:4" % (w, 64 * a + 64 + e), "PS:%d:320" % (16 * a + 16), s, A.is_ge)
+            for w in after.get(k, ()):
+                quant("C%d" % w, "CT%d" % w)
+                mm("PK", "OB", 0, "C%d" % w, w == 5, w == 2)
         act("STEP", "PK:0:320", F.Copy)
         old, new = names[t % 2], names[(t + 1) % 2]
-        tt(new, "STEP@COFF", old, A.add)
+        for r, l in zip(HALVES, LISTS):
+            tt(new + r, "STEP@COFF" + l, old + r, A.add)
 
         def deal(t=t, arr=arr):
             banks = ("PH", "PS", "PSB", "PK")
@@ -452,24 +469,31 @@ def rank_program(g, core, T, topo):
             if last:
                 ts("PT1", new, WHOLE, A.add, WHOLE + 1.0, A.subtract)
                 quant("V", "VT")
+                for b in range(2, 4):
+                    cp("FH%d" % b, "PF%d:0:320" % b)
 
         order(new, False, not last, (2896, 3216, NV)[t], final, deal)
         if last:
             dma("dpt", [("y", T.pt[:, :], T.PT1[0:P:16, :])], [], ["PT1"])
-        for b in range(4):
-            if last and b > 1:
-                cp("GB%d" % b, "HB%d@C2OFF" % b)
-            else:
-                act("GB%d" % b, "HB%d@C2OFF" % b, F.Copy)
         if not last:
+            for b in range(4):
+                act("GB%d" % b, "HB%d@C2OFF" % b, F.Copy)
             lists(t + 1 < R - 1, new_x)
 
-    for b in (2, 0, 3, 1):
-        add_x(b)
-    quant("X", "X")
-    mm("PS", "V", 0, "X")
-    dma("dout", [("y", T.oc[:, :], T.qX[:, 0:C].bitcast(dt.uint8))] +
-        [("ys"[k % 2], T.osc[4 * k:4 * k + 4, :], T.sX[32 * k:32 * k + 4, 0:C]) for k in range(4)], [], ["qX", "sX"])
-    act("YB", "PS:0:320", F.Copy)
-    dma("dy", [("s", T.y[:, :], T.YB[:, :])], [], ["YB"])
+    for r, l in zip(HALVES, LISTS):
+        for b in range(2):
+            act("GB%d" % b + r, "HB%d@C2OFF" % b + l, F.Copy)
+    for h, bank in enumerate(("PS", "PSB")):
+        r, a, x = HALVES[h], 160 * h, "X:%d:%d" % (640 * h, 640 * h + 640)
+        for b in range(2, 4):
+            tt("X:%d:%d:4" % (4 * a + b, 4 * a + 640), "HB%d@C2OFF" % b + LISTS[h], "FH%d" % b + r, A.add)
+        for b in range(2):
+            tt("X:%d:%d:4" % (4 * a + b, 4 * a + 640), "GB%d" % b + r, "PF%d" % b + r, A.add)
+        op("v", lambda: V.quantize_mx(ap("qX" + r), ap("sX" + r), ap(x)), ["qX" + r, "sX" + r], [x])
+        i = ["qV", "sV", "qX" + r, "sX" + r]
+        op("t", lambda: TE.matmul_mx(ap(bank + ":0:160"), ap(i[0]), ap(i[1]), ap(i[2]), ap(i[3]), True, True), [bank], i)
+        dma("dout", [("y", T.oc[:, 4 * a:4 * a + 640], T.qX[:, a:a + 160].bitcast(dt.uint8))], [], ["qX" + r])
+        act("YB" + r, bank + ":0:160", F.Copy)
+        dma("dy", [("s", T.y[:, a:a + 160], T.YB[:, a:a + 160])], [], ["YB" + r])
+    dma("dout", [("y", T.osc[4 * k:4 * k + 4, :], T.sX[32 * k:32 * k + 4, 0:C]) for k in range(4)], [], ["sX"])
     wait("g", list(cnt.items()))

@@ -2,12 +2,13 @@ from concourse.mybir import dt, AluOpType as A, ActivationFunctionType as F
 
 C, P, R = 320, 128, 3
 NV = 3520
-NULL = 3528
 WW = 2 * NV + C
-NS = 10
-SKEYS = (0, 19, 1, 18, 2, 17, 3, 16)
+NS = 11
+SKEYS = (0, 1, 19, 18, 2, 3, 17, 16)
 VKEYS = tuple(a for a in range(20) if a not in SKEYS)
 HALVES, LISTS = (":0:160", ":160:320"), (":0:10", ":10:20")
+PIECES = ((0, 176), (176, C))
+MADE = ((0, 192, ":0:12"), (192, C, ":12:20"))
 BIG = 4194304.0
 HUGE = 1e25
 WHOLE = 12582912.0
@@ -29,47 +30,47 @@ def _t(n, d, parts, where="sbuf"):
 
 
 for _n, _w in (("E16", C), ("JR", C), ("JP0", C), ("JP", C), ("TNY", 1), ("MASK", C), ("RS", C), ("MB0", C), ("MB", C), ("SEL", C), ("HOLD", C),
-               ("KP", C), ("KFA", C), ("KFB", C), ("KM", C), ("KS", C), ("S1", C), ("S2", C), ("OWD", 336), ("O0", C), ("O1", C), ("O2", C), ("O3", C),
-               ("MM", C), ("MS", C), ("SM", C + 1), ("SS", C), ("SX", C), ("NA", 20), ("ND", 20), ("STEP", C), ("PT1", C), ("YB", C),
-               ("XA", 40), ("XB", 40), ("OW", 40)):
+               ("KP", C), ("KF", C), ("KM", C), ("KS", C), ("S1", C), ("S2", C), ("SM", C + 1), ("SS", C), ("SX", C), ("NA", 20), ("ND", 20),
+               ("STEP", C), ("PT0", C), ("PT1", C), ("YB", C), ("XA", 40), ("XB", 40), ("OW", 40)):
     _b(_n, _w)
 _t("SKB", "float32", [("SK", C), ("SKE", 16)])
-_t("CTAB", "float32", [("C16", 20), ("C1", 20), ("QP", 4), ("Q20", 4), ("ODD", 4), ("EVN", 4), ("NO", 4), ("NE", 4), ("CR", 4), ("CH", 4),
-                       ("TOP", 4), ("JT0", 20), ("JT", 20)])
-_t("FTAB", "float32", [("ACC", 20), ("TH", 12), ("IXM", 20), ("NJ", 20)])
+_t("CTAB", "float32", [("C16", 20), ("C1", 20), ("QP", 4), ("Q20", 4), ("ODD", 4), ("NO", 4), ("NE", 4), ("CR", 4), ("CH", 4),
+                       ("TOP", 4), ("JT0", 20), ("JT", 20), ("FE", 4), ("FO", 4), ("QH", 4)])
+_t("FTAB", "float32", [("ACC", 20), ("TH", 12), ("FR", 20), ("PL", 20), ("KT", 32), ("KA", 64), ("KB", 64)])
 _t("TAB", "bfloat16", [("TA", 12), ("TB", 12)])
-_b("VSB", 160 * (20 - NS), "float16")
+_b("VSB", 1600, "float16")
 _b("GS", 640, "float16")
-_t("CTABI", "int32", [("QI", 4), ("QA", 4), ("QB", 4), ("QC", 4)])
-_t("ITAB", "int32", [("P1", 20), ("P2", 20), ("MI", 20)])
-_t("UTAB", "uint16", [("OQ", 40)] + [(k, 20) for k in ("PERM", "RP", "OWU", "COFF", "C2OFF", "P2U", "IXU", "MOFF", "NOFF")])
+_t("CTABI", "int32", [("QI", 4), ("QA", 4), ("QB", 4)])
+_t("ITAB", "int32", [("P1", 20), ("P2", 20), ("KI", 20)])
+_t("UTAB", "uint16", [("OQ", 40)] + [(k, 20) for k in ("PERM", "RP", "OWU", "COFF", "C2OFF", "P2U", "IXU", "INV", "JU")])
 _b("R16", C, "uint16")
 _b("UI", 8, "int32")
 _b("PR", C, "int32")
 _b("PTAB", 20, "int32")
 _b("UL", 8, "uint16")
-for _n, _w in (("ZER", 512), ("ONE", 512), ("ZD", 512), ("OB1", 512), ("OB2", 512), ("CDF", C), ("ONES", C), ("UT", 512), ("VT", 512), ("X", 4 * C),
-               ("Z", 4 * C), ("W", WW), ("CC", NV), ("D", 3536), ("G", 640), ("GT", 640), ("W2", 8 * C), ("N2", 4 * C), ("RKX", 640),
-               ("MBH", C), ("IX", C)):
+for _n, _w in (("ZER", 512), ("ONE", 512), ("OB1", 512), ("OB2", 512), ("CDF", C), ("ONES", C), ("UT", 512), ("VT", 512), ("XIN", 4 * C),
+               ("X", 4 * C + 8), ("Z", 4 * C), ("W", WW), ("CC", NV), ("D", 3536), ("G", 640), ("GT", 640), ("W2", 8 * C), ("N2", 4 * C), ("RKX", 640),
+               ("MBH", 640), ("IX", 640), ("SELH", C), ("HOLDH", C), ("I0", C), ("I1", C), ("I2", C)):
     _b(_n, _w, "bfloat16")
 _t("JUNK", "bfloat16", [("JUNK%d" % k, C) for k in range(NS)])
-_t("CMPB", "bfloat16", [("CMP%d" % k, C) for k in range(20 - NS)])
+_t("CMPB", "bfloat16", [("CMP%d" % k, C) for k in range(10)])
 _t("EBB", "bfloat16", [("EB%d" % k, 512) for k in range(4)])
-for _n, _w in (("FH", C), ("GB", C), ("HB", 160)):
+for _n, _w in (("FB", C), ("FS", C), ("PB", C), ("GB", C), ("HB", 160)):
     _t(_n + "B", "bfloat16", [("%s%d" % (_n, k), _w) for k in range(4)])
 _t("CTB", "bfloat16", [("CT%d" % k, 4 * C) for k in range(6)])
 _t("PFB", "float32", [("PF%d" % k, 512) for k in range(4)], "psum")
 for _n in ("PS", "PSB", "PK", "PH"):
     _b(_n, 512, "float32", "psum")
-for _n, _w in [("OB", P), ("U", P), ("UR", P), ("V", P), ("L", 512), ("X", C)] + [("%s%d" % (z, k), C) for k in range(R) for z in "ZA"]:
+for _n, _w in [("OB", P), ("U", P), ("UR", P), ("V", P), ("L", 512), ("X", C), ("Y", C)] + [("%s%d" % (z, k), C) for k in range(R) for z in "ZA"]:
     _b("q" + _n, _w, "float8_e4m3fn_x4")
     _b("s" + _n, _w, "uint8")
 for _n, _d in (("q", "float8_e4m3fn_x4"), ("s", "uint8")):
     _t(_n + "EB", _d, [("%sE%d" % (_n, k), P) for k in range(4)])
     _t(_n + "CB", _d, [("%sC%d" % (_n, k), C) for k in range(6)])
 PSUM = ["PF0", "PF1", "PF2", "PF3", "PS", "PSB", "PK", "PH"]
+BANKS = ("PH", "PK", "PS", "PSB")
 
-SEMAPHORES = ["cv", "cs", "ct", "cg", "dp", "dt", "dx", "du", "dv", "dw", "dz", "dd", "de", "dout", "dpt", "dy", "sent"] + ["arr%d" % k for k in range(R)]
+SEMAPHORES = ["cv", "cs", "ct", "cg", "dp", "dt", "dx", "du", "dv", "dw", "dd", "de", "dout", "dpt", "dy", "sent"] + ["arr%d" % k for k in range(R)]
 
 
 def region(s):
@@ -171,16 +172,16 @@ def rank_program(g, core, T, topo):
     def fill(n, c):
         op("v", lambda: V.memset(ap(n), c), [n], [])
 
-    def quant(q, t):
-        op("v", lambda: V.quantize_mx(ap("q" + q), ap("s" + q), ap(t)), ["q" + q, "s" + q], [t])
+    def quant(q, t, r=""):
+        op("v", lambda: V.quantize_mx(ap("q" + q + r), ap("s" + q + r), ap(t)), ["q" + q + r, "s" + q + r], [t])
 
     def turn(o, i):
         op("v", lambda: V.transpose(ap(o), ap(i)), [o], [i])
 
-    def mm(ps, a, a0, b, start=True, stop=True, extra=()):
-        r = ":%d:%d" % (a0, a0 + P)
-        i = ["q" + a + r, "s" + a + r, "q" + b, "s" + b]
-        op("t", lambda: TE.matmul_mx(ap(ps + ":0:320"), ap(i[0]), ap(i[1]), ap(i[2]), ap(i[3]), start, stop), [ps], i, extra)
+    def mm(ps, a, a0, b, start=True, stop=True, extra=(), r=""):
+        w = ":%d:%d" % (a0, a0 + P)
+        i = ["q" + a + w, "s" + a + w, "q" + b + r, "s" + b + r]
+        op("t", lambda: TE.matmul_mx(ap(ps + ":0:%d" % len(region(i[2])[1])), ap(i[0]), ap(i[1]), ap(i[2]), ap(i[3]), start, stop), [ps], i, extra)
 
     def act(o, i, f, acc=None, bias=None, scale=None):
         kw = {}
@@ -199,9 +200,9 @@ def rank_program(g, core, T, topo):
     def sel(o, i, pattern, cop, c, base, cm):
         op("g", lambda: g.affine_select(ap(o), ap(i), pattern, cop, c, base, cm), [o], [i])
 
-    dma("dp", [("ys"[k % 2], T.PR[k:P:16, :], T.p[:, :]) for k in range(16)], ["PR"], [])
-    dma("dt", [("s", T.PTAB[:, :], T.p[:, :])], ["PTAB"], [])
-    dma("dx", [("y", T.X[:, :], T.x[:, :])], ["X"], [])
+    dma("dt", [("y", T.PTAB[:, :], T.p[:, :])], ["PTAB"], [])
+    dma("dp", [("sy"[k % 2], T.PR[k:P:16, :], T.p[:, :]) for k in range(16)], ["PR"], [])
+    dma("dx", [("y", T.XIN[:, :], T.x[:, :])], ["XIN"], [])
     dma("du", [("y", T.UT[:, :], T.u[:, :])], ["UT"], [])
 
     iota("QI:0:2", [[0, 2]], 0, 1)
@@ -210,216 +211,264 @@ def rank_program(g, core, T, topo):
     iota("C1", [[1, 20]])
     iota("E16", [[0, 20], [1, 16]])
     iota("JR", [[1, C]])
-    iota("W:0:%d" % NV, [[0, NV]], -160)
+    iota("W:0:2576", [[0, 2576]], -160)
     fill("ZER", 0.0)
-    fill("ONE", 1.0)
     ts("QA:0:2", "QI:0:2", 15, A.bitwise_and)
     ts("QB:0:2", "QI:0:2", 4, A.arith_shift_right, 1, A.bitwise_and)
-    ts("QC:0:2", "QI:0:2", 31, A.bitwise_and)
+    ts("TOP:0:1", "QA:0:1", 15.0, A.is_equal, 4096.0, A.mult)
     cp("QP:0:1", "QA:0:1")
     cp("ODD:0:1", "QB:0:1")
-    ts("TOP:0:1", "QC:0:1", 31.0, A.is_equal, 4096.0, A.mult)
-    ts("Q20:0:1", "QP:0:1", 20.0, A.mult)
     ts("JT0", "C16", "QP:0:1", A.add, 352.0, A.add)
+    ts("QH:0:1", "QP:0:1", 0.5, A.add)
+    ts("QH:1:2", "QP:0:1", -0.5, A.add)
+    ts("Q20:0:1", "QP:0:1", 20.0, A.mult)
     ts("CR:0:1", "QP:0:1", -1.0 / 32, A.mult, 160.5 / 32, A.add)
     ts("CH:0:1", "QP:0:1", -1.0 / 32, A.mult, 176.0 / 32, A.add)
-    ts("ZD", "ONE", "TOP:0:1", A.mult)
+    ts("FE:0:1", "ODD:0:1", -65536.0, A.mult, 32768.0, A.add)
+    ts("FO:0:1", "ODD:0:1", 65536.0, A.mult, -32768.0, A.add)
+    ts("NO:0:1", "ODD:0:1", 32768.0, A.mult)
     ts("JP", "JP0", 2.0 ** -9, A.mult)
     ts("JT", "JT0", 2.0 ** -9, A.mult)
-    for a in range(0, 2560, 512):
-        act("D:%d:%d" % (a, a + 512), "ZER", F.Identity, bias="TOP:0:1")
-    dma("dz", [("y", T.D[:, a:min(a + 512, 3536)], T.ZD[:, 0:min(512, 3536 - a)]) for a in range(2560, 3536, 512)], ["D:2560:3536"], ["ZD"])
-    dma("dw", [("y", T.qL[:, 0:512].bitcast(dt.uint8), T.wc[:, :]), ("y", T.sL[:, 0:512], T.ws[:, :])], ["qL", "sL"], [])
-    dma("dv", [("y", T.VT[:, :], T.v[:, :])], ["VT"], [])
     ts("PERM", "C1", "Q20:0:1", A.add)
-    ts("EVN:0:1", "ODD:0:1", -1.0, A.mult, 1.0, A.add)
-    ts("NO:0:1", "ODD:0:1", float(NULL), A.mult)
-    ts("NE:0:1", "EVN:0:1", float(NULL), A.mult)
+    ts("NE:0:1", "ODD:0:1", -32768.0, A.mult, 32768.0, A.add)
+    ts("XB:0:40:2", "C16", "QP:0:1", A.add, float(NV), A.add)
     fill("SKE", 3600.0)
     fill("XA:0:40:2", 0.0)
-    ts("XB:0:40:2", "C16", "QP:0:1", A.add, float(NV), A.add)
-    fill("RKX", 32768.0)
-    ts("MB0", "E16", "QP:0:1", A.is_lt)
+    fill("KT", 0.0)
+    fill("SM:0:1", -HUGE)
+
+    def clear(a, b):
+        for c in range(a, b, 512):
+            act("D:%d:%d" % (c, min(c + 512, b)), "ZER:0:%d" % min(512, b - c), F.Identity, bias="TOP:0:1")
+
+    clear(0, 1024)
+    act("MB0", "E16", F.Sign, bias="QH:1:2", scale=-1.0)
+    act("ONE", "ZER", F.Identity, bias=1.0)
+    dma("dw", [("y", T.qL[:, 0:512].bitcast(dt.uint8), T.wc[:, :]), ("y", T.sL[:, 0:512], T.ws[:, :])], ["qL", "sL"], [])
+    dma("dv", [("y", T.VT[:, :], T.v[:, :])], ["VT"], [])
     for b in range(4):
         sel("EB%d" % b, "ZER", [[1, 512]], A.not_equal, 1.0, -b, -4)
     iota("W2", [[0, 8 * C]])
     iota("UI", [[16, 8]])
     sel("OB1", "ONE", [[-16, 8], [0, 64]], A.is_ge, 0.0, 0, 1)
     sel("OB2", "OB1", [[16, 8], [0, 64]], A.is_ge, 0.0, 15, -1)
-    tt("KP", "PR", "JP", A.add)
     tt("KS:15:320:16", "PTAB", "JT", A.add)
-
-    def constants():
-        act("MB", "MB0", F.Identity, bias=-BIG, scale=2.0 * BIG)
-        act("CDF", "JR", F.Identity, bias=-159.0)
-        act("MBH", "MB0", F.Identity, bias=-1024.0, scale=2048.0)
-        act("RS", "E16", F.Sign)
-        act("HOLD", "RS", F.Identity, bias=-HUGE, scale=2.0 * HUGE)
-        act("ONES", "ONE:0:320", F.Copy)
-        for a in range(0, 4 * C, 512):
-            act("CT5:%d:%d" % (a, min(a + 512, 4 * C)), "ZER:0:%d" % min(512, 4 * C - a), F.Copy)
-
-    def unpack():
-        for b in range(4):
-            mm("PF%d" % b, "E%d" % b, 0, "X")
-        for b in range(2):
-            act("FH%d" % b, "PF%d:0:320" % b, F.Copy, scale=0.5)
-
-    def first_tiles():
-        ts("MASK", "E16", "QP:0:1", A.is_equal)
-        for b in range(4):
-            quant("E%d" % b, "EB%d" % b)
-
-    def sides(k):
-        if k == 0:
-            quant("X", "X")
-            unpack()
-            for b in range(2, 4):
-                act("FH%d" % b, "PF%d:0:320" % b, F.Copy, scale=0.5)
-            act("SEL", "MASK", F.Identity, bias=-HUGE, scale=2.0 * HUGE)
-        elif k == 1:
-            cp("UL", "UI")
-            quant("U", "UT")
-        elif k == 2:
-            quant("OB", "OB2")
-        elif k == 3:
-            op("v", lambda: V.tensor_copy(T.qUR[:, 0:P].bitcast(dt.uint32), T.qU[:, 0:P].bitcast(dt.uint32).indirect(T.UL[:, 0:8])), ["qUR"], ["qU", "UL"])
-        elif k == 4:
-            act("sUR", "sU@UL", F.Copy)
-            fill("TNY", 2.0 ** -126)
-            fill("SM:0:1", -HUGE)
+    fill("RKX:0:320", 32768.0)
+    ts("TH:0:10", "KS:31:320:32", 16.0, A.mult, "CH:0:1", A.add)
+    ts("TA:0:10", "KS:31:320:32", 16.0, A.mult, "CH:0:1", A.add)
+    for r in HALVES:
+        tt("KP" + r, "PR" + r, "JP" + r, A.add)
 
     def half(k):
         scan("VSB:%d:%d" % (160 * k, 160 * k + 160), "CMP%d:0:160" % k, "CMP%d:160:320" % k, 0.0, A.add, A.add)
 
-    def offsets():
-        ts("OQ:0:40:2", "KS:15:320:16", "EVN:0:1", A.mult, "NO:0:1", A.add)
-        ts("OQ:1:40:2", "KS:15:320:16", "ODD:0:1", A.mult, "NE:0:1", A.add)
-
     def spread(sem, a, b):
-        moves = []
-        for h in range(8):
-            if h < 7:
-                moves.append((T.D[16 * (h + 1) + h:P:16, a:b], T.CC[16 * h:16 * h + 7 - h, a:b]))
-            if h:
-                moves.append((T.D[h:16 * h:16, a + 1:b + 1], T.CC[16 * h + 8:16 * h + 8 + h, a:b]))
+        moves = [(T.D[0:P:32, a:b], T.CC[0:P:32, a:b]), (T.D[16:P:32, a + 1:b + 1], T.CC[16:P:32, a:b])]
+        for d in range(1, 4):
+            moves.append((T.D[32 * d + 1 + d:P:16, a:b], T.CC[d:P - 32 * d:16, a:b]))
+            moves.append((T.D[4 + d:P - 32 * d:16, a + 1:b + 1], T.CC[32 * d + 4 + d:P:16, a:b]))
         dma(sem, [("ys"[k % 2], o, i) for k, (o, i) in enumerate(moves)], ["D:%d:%d" % (a, b)], ["CC:%d:%d" % (a, b)])
 
-    def order(kf, first, joined, nv, during, scalar_tail):
-        row = "KP" if first else kf
-        if not first:
-            for r in HALVES:
-                scan("KM" + r, kf + r, "MASK" + r, 0.0, A.max, A.mult)
-            for r in HALVES:
-                scan("KS" + r, "RS" + r, "KM" + r, 0.0, A.mult, A.add)
-        key = ["KS:%d:%d" % (16 * c + 15, 16 * c + 16) for c in range(20)]
-        for k in range(NS):
-            act("JUNK%d" % k, row, F.Sign, acc="ACC:%d:%d" % (k, k + 1), bias=key[2 * k], scale=-1.0)
-        if first:
-            constants()
-        ts("R16:0:160", row + ":0:160", 16.0, A.mult, "CR:0:1", A.add)
-        ts("TH:0:10", "KS:31:320:32", 16.0, A.mult, "CH:0:1", A.add)
-        ts("TA:0:10", "KS:31:320:32", 16.0, A.mult, "CH:0:1", A.add)
-        ts("R16:160:320", row + ":160:320", 16.0, A.mult, "CR:0:1", A.add)
+    key = ["KS:%d:%d" % (16 * c + 15, 16 * c + 16) for c in range(20)]
+
+    def first_ranks():
+        for k in range(10):
+            act("JUNK%d" % k, "KP", F.Sign, acc="ACC:%d:%d" % (k, k + 1), bias=key[2 * k], scale=-1.0)
+        act("MB", "MB0", F.Copy, scale=BIG)
+        act("CDF", "JR", F.Identity, bias=-159.0)
+        ts("R16:0:160", "KP:0:160", 16.0, A.mult, "CR:0:1", A.add)
         tt("TB:0:10", "TH:0:10", "TA:0:10", A.subtract)
-        if first:
-            cp("KFA", "KP@PERM")
-        else:
-            offsets()
+        ts("R16:160:320", "KP:160:320", 16.0, A.mult, "CR:0:1", A.add)
+        cp("KF", "KP@PERM")
         for k in range(10):
             ts("CMP%d" % k, "R16", "TA:%d:%d" % (k, k + 1), A.subtract, "TB:%d:%d" % (k, k + 1), A.is_lt)
             if k:
                 half(k - 1)
-        if first:
-            offsets()
+        ts("MASK:0:160", "E16:0:160", "QP:0:1", A.is_equal)
         half(9)
         ts("RP:0:20:2", "ACC:0:10", 319.0, A.add, 0.5, A.mult)
         cp("RP:1:20:2", "VSB:159:1600:160")
-        cp("SK@RP", kf)
-        if joined:
-            act("O0", "SK", F.Identity, bias=WHOLE)
-            act("O1", "O0", F.Identity, bias=-WHOLE)
+        ts("MASK:160:320", "E16:160:320", "QP:0:1", A.is_equal)
+
+    def ranks():
+        for r in HALVES:
+            scan("KM" + r, "KF" + r, "MASK" + r, 0.0, A.max, A.mult)
+        for r in HALVES:
+            scan("KS" + r, "RS" + r, "KM" + r, 0.0, A.mult, A.add)
+        n = 20 - NS
+        for k in range(NS):
+            act("JUNK%d" % k, "KF", F.Sign, acc="ACC:%d:%d" % (k, k + 1), bias=key[n + k], scale=-1.0)
+        for k in range(n):
+            ts("CMP%d" % k, "KF", key[k], A.is_lt)
+            if k:
+                half(k - 1)
+        half(n - 1)
+        ts("RP:%d:20" % n, "ACC:0:%d" % NS, 319.0, A.add, 0.5, A.mult)
+        cp("RP:0:%d" % n, "VSB:159:%d:160" % (160 * n))
+
+    def own(rank, add):
+        ts("RKX:0:640:32", rank, add, A.add, "FE:0:1", A.max)
+        ts("RKX:1:640:32", rank, add, A.add, "FO:0:1", A.max)
+
+    def order(t, scalar_early, scalar_late):
+        last, nv = t == R, 2576 + C * t - 16 * (t == R)
+        cp("SK@RP", "KF")
+        scalar_early()
+        if t == 0:
+            fill("RKX:320:640", 32768.0)
+        if last:
+            cp("KT:0:20", "KS:15:320:16")
+            cp("KI", "KS:15:320:16")
         scan("S1", "SK", "MB", 0.0, A.min, A.max)
         op("v", lambda: V.tensor_tensor_scan(ap("S2"), T.SKB[:, 1:C + 1], ap("MB"), 0.0, A.min, A.max), ["S2"], ["SK", "SKE", "MB"])
+        if not last:
+            tt("KT:0:20", "S1:15:320:16", "SK:0:320:16", A.max)
         tt("P1", "S1:15:320:16", "SK:0:320:16", A.max)
         tt("XB:1:40:2", "S1:15:320:16", "SK:0:320:16", A.max)
         tt("P2", "S2:15:320:16", "SK:1:320:16", A.max)
+        turn("KA:16:48", "KT")
+        if t in (0, R):
+            tt("FR", "KT:0:20", "KI" if last else "P1", A.subtract)
         tt("XA:1:40:2", "P1", "P2", A.is_equal)
+        cp("KA:0:16", "KA:16:32")
+        cp("KA:48:64", "KA:32:48")
         scan("OW", "XA", "XB", 0.0, A.mult, A.add)
+        if t in (0, R):
+            ts("JU" if last else "INV", "FR", 512.0, A.mult, 160.0, A.add)
+        scalar_late(-2)
+        turn("KB", "KA")
         cp("OWU", "OW:1:40:2")
+        if last:
+            own("RP", -160.0)
+        elif t == 0:
+            ts("RKX:16:640:32", "C1", 0.0, A.mult, "NO:0:1", A.add)
+            ts("RKX:17:640:32", "C1", 0.0, A.mult, "NE:0:1", A.add)
         cp("W@OWU", "CDF")
+        cp("OQ:0:40:2", "KB:0:20")
+        cp("OQ:1:40:2", "KB:32:52")
         h = nv // 2
         lo, hi = "0:%d" % h, "%d:%d" % (h, nv)
         scan("CC:" + lo, "W:" + lo, "W:" + lo, -160.0, A.max, A.max)
         spread("dd", 0, h)
-        ts("RKX:0:640:32", "RP", -160.0, A.add)
+        if t == 0:
+            own("JT0", -512.0)
         scan("CC:" + hi, "W:" + hi, "W:" + hi, "CC:%d:%d" % (h - 1, h), A.max, A.max)
         spread("de", h, nv)
-        scalar_tail()
-        if joined:
-            iota("W:0:%d" % NV, [[0, NV]], -160)
-            scan("OWD:0:320", "SK", "O1", 0.0, A.max, A.subtract)
-            act("O2", "OWD:0:320", F.Identity, bias=161.0, scale=512.0)
-            cp("OWD:320:321", "OWD:319:320")
-            scan("O3", "OWD:1:321", "O2", 1.0, A.min, A.add)
-        during()
+        if not last:
+            iota("W:0:%d" % min(nv + C, NV), [[0, min(nv + C, NV)]], -160)
+        scalar_late(-1)
+        if t:
+            cp("I0@" + ("JU" if last else "RP"), "CDF")
+            scalar_late(0)
+            scan("I1", "I0", "SELH", -1024.0, A.max, A.min)
         act("G:320:640", "D@OQ:20:40", F.Copy)
         cp("G:0:320", "D@OQ:0:20")
-        for r in (":0:320", ":320:640"):
-            turn("GT" + r, "G" + r)
+        if t:
+            scan("I2", "HOLDH", "I1", -1024.0, A.min, A.max)
+        turn("GT:0:320", "G:0:320")
+        if t:
+            ts("INV", "I2:15:320:16", 159.0, A.add)
+        scalar_late(1)
+        turn("GT:320:640", "G:320:640")
         for r in (":0:320", ":320:640"):
             scan("GS" + r, "RKX" + r, "GT" + r, 4096.0, A.min, A.add)
-        ts("C2OFF", "GS:30:640:32", 1.0 / 16, A.mult, 80.0 - 15.0 / 32, A.add)
+        scalar_late(2)
+        tt("PL", "GS:14:640:32", "GS:30:640:32", A.add)
+        if t:
+            ts("C2OFF", "PL", 1.0 / 16, A.mult, 80.0 - 15.0 / 32, A.add)
 
-    def add_x(b):
-        tt("X:%d:1280:4" % b, "GB%d" % b, "PF%d:0:320" % b, A.add)
+    def pairs(h):
+        a, e = PIECES[h]
+        r, banks = ":%d:%d" % (a, e), (BANKS, PSUM)[h]
+        quant("X", "X:%d:%d" % (4 * a, 4 * e), r)
+        quant("Y", "X:%d:%d" % (4 * a + 4, 4 * e + 4), r)
+        for b in (2, 0, 3, 1):
+            mm(banks[b], "E%d" % b, 0, "X", True, False, r=r)
+            mm(banks[b], "E%d" % b, 0, "Y", False, True, r=r)
 
-    def lists(again, deal):
-        ts("P2U", "GS:30:640:32", 1280.0, A.add)
-        ts("COFF", "GS:30:640:32", 1.0 / 8, A.mult, 160.0 - 7.0 / 16, A.add)
+    def halve(h, bs, vector=False):
+        a, e = PIECES[h]
+        for b in bs:
+            o, i = "PB%d:%d:%d" % (b, a, e), (BANKS, PSUM)[h][b] + ":0:%d" % (e - a)
+            if vector:
+                ts(o, i, 0.5, A.mult)
+            else:
+                act(o, i, F.Copy, scale=0.5)
+
+    def lists(again, between):
+        ts("P2U", "PL", 1280.0, A.add)
+        ts("COFF", "PL", 1.0 / 8, A.mult, 160.0 - 7.0 / 16, A.add)
+        between(0)
         cp("W2@P2U", "ONES")
-        deal(0)
+        between(1)
         scan("N2", "W2:0:2560:2", "W2:1:2560:2", -160.0, A.add, A.add)
         if again:
             iota("W2", [[0, 8 * C]])
-        deal(1)
-        scan("IX", "N2:3:1280:4", "MBH", 0.0, A.min, A.max)
-        deal(2)
-        tt("IXM", "IX:15:320:16", "N2:3:1280:64", A.max)
-        deal(3)
-        ts("IXU", "IXM", 159.0, A.add, 0.0, A.max)
-        deal(4)
-        for r, l in zip(HALVES, LISTS):
-            tt("MM" + r, "O3@IXU" + l, "MASK" + r, A.mult)
-        for r in HALVES:
-            scan("MS" + r, "RS" + r, "MM" + r, 0.0, A.mult, A.add)
-        ts("MOFF", "MS:15:320:16", -1.0, A.add)
-        cp("MI", "MS:15:320:16")
-        deal(5)
-        tt("NJ", "MS:15:320:16", "MI", A.subtract)
-        deal(6)
-        ts("NOFF", "NJ", 512.0, A.mult, 160.0, A.add)
+        between(2)
+        scan("IX", "N2:1:1280:2", "MBH", 0.0, A.min, A.max)
+        between(3)
+        ts("IXU", "IX:31:640:32", 159.0, A.add, 0.0, A.max)
+        between(4)
 
-    def new_x(k):
-        if k < 4:
-            add_x(k)
-        elif k == 4:
-            quant("X", "X")
-            unpack()
-        else:
-            ts("FH%d" % (k - 3), "PF%d:0:320" % (k - 3), 0.5, A.mult)
+    def x_early():
+        for b in range(4):
+            act("FB%d" % b, "XIN:%d:1280:4" % b, F.Copy)
+        clear(1024, 3536)
 
-    order("KFA", True, True, 2576, first_tiles, lambda: None)
+    def x_late(k):
+        if k == -2:
+            for b in range(2):
+                act("X:%d:1280:4" % b, "FB%d@INV" % b, F.Copy)
+        elif k == -1:
+            for b in range(2, 4):
+                cp("X:%d:1280:4" % b, "FB%d@INV" % b)
+            for b in range(4):
+                quant("E%d" % b, "EB%d" % b)
+            cp("X:1280:1284", "X:1276:1280")
+            act("JUNK10", "E16", F.Sign, bias="QH:0:1", scale=-1.0)
+            act("MBH:1:640:2", "MB0", F.Copy, scale=1024.0)
+            act("MBH:0:640:2", "JUNK10", F.Copy, scale=1024.0)
+            act("RS", "E16", F.Sign)
+            pairs(0)
+            pairs(1)
+        elif k == 1:
+            halve(0, range(4))
+            halve(1, range(4))
+            act("SEL", "MASK", F.Identity, bias=-HUGE, scale=2.0 * HUGE)
+            act("HOLD", "RS", F.Identity, bias=-HUGE, scale=2.0 * HUGE)
+        elif k == 2:
+            fill("ONES", 1.0)
+
+    first_ranks()
+    order(0, x_early, x_late)
+
+    def sides(k):
+        if k == 0:
+            cp("UL", "UI")
+            fill("TNY", 2.0 ** -126)
+        elif k == 1:
+            quant("U", "UT")
+            act("sUR", "sU@UL", F.Copy)
+            act("SELH", "MASK", F.Identity, bias=-1024.0, scale=2048.0)
+            act("HOLDH", "RS", F.Identity, bias=-1024.0, scale=2048.0)
+        elif k == 2:
+            op("v", lambda: V.tensor_copy(T.qUR[:, 0:P].bitcast(dt.uint32), T.qU[:, 0:P].bitcast(dt.uint32).indirect(T.UL[:, 0:8])), ["qUR"], ["qU", "UL"])
+        elif k == 3:
+            quant("OB", "OB2")
+
     lists(True, sides)
-    names = ["KFA", "KFB"]
     for t in range(R):
         last = t == R - 1
         qz = "Z%d" % t
-        for b in range(4):
-            act("GB%d" % b, "FH%d@MOFF" % b, F.Copy)
-        for b in range(4):
-            tt("Z:%d:1280:4" % b, "FH%d@NOFF" % b, "GB%d" % b, A.add)
-        quant(qz, "Z")
+        for b in range(2):
+            act("Z:%d:1280:4" % (b + 2), "PB%d@IXU" % (b + 2), F.Copy)
+            cp("Z:%d:1280:4" % b, "PB%d@IXU" % b)
+        if t == 0:
+            for a in range(0, 4 * C, 512):
+                act("CT5:%d:%d" % (a, min(a + 512, 4 * C)), "ZER:0:%d" % min(512, 4 * C - a), F.Copy)
+        for h, bank in enumerate(("PK", "PH")):
+            quant(qz, "Z:%d:%d" % (640 * h, 640 * h + 640), HALVES[h])
+            mm(bank, "UR", 0, qz, r=HALVES[h])
         wait("g", [x[1:] for x in wr["q" + qz] + wr["s" + qz]])
         rid, pid, _s = topo.addr(nxt)
         m, arr = topo.mask(core, nxt), "arr%d" % t
@@ -429,71 +478,119 @@ def rank_program(g, core, T, topo):
         cnt["sent"], cnt[arr] = cnt.get("sent", 0) + n, n
         mm("PS", "UR", 0, qz)
         mm("PSB", "UR", 0, qz)
-        for r, r1 in zip(HALVES, (":1:161", ":161:321")):
-            tt("SM" + r1, "PS" + r, "SEL" + r, A.min)
+        for bank, r, r1 in zip(("PK", "PH"), HALVES, (":1:161", ":161:321")):
+            tt("SM" + r1, bank + ":0:160", "SEL" + r, A.min)
         for r, r1 in zip(HALVES, (":1:161", ":161:321")):
             scan("SS" + r, "HOLD" + r, "SM" + r1, -HUGE, A.min, A.max)
-        act("NA", "SS:15:320:16", F.Abs, bias="TNY", scale=1.01 * 2.0 ** -24)
-        scan("SX", "SM:0:320", "HOLD", -HUGE, A.max, A.min)
-        tt("ND", "SS:15:320:16", "NA", A.subtract)
-        tt("CT5:0:1280:4", "PS:0:320", "SX", A.is_equal)
-        for w in range(3, 5):
-            ks = list(enumerate(SKEYS[4 * w - 12:4 * w - 8]))
-            for e, a in ks:
-                act("CT%d:%d:%d:4" % (w, e, 64 * a + 64), "PSB:0:%d" % (16 * a + 16), F.Sign, bias="SS:%d:%d" % (16 * a + 15, 16 * a + 16), scale=-1.0)
-            for e, a in ks:
-                if a < 19:
-                    act("CT%d:%d:1280:4" % (w, 64 * a + 64 + e), "PSB:%d:320" % (16 * a + 16), F.Sign, bias="ND:%d:%d" % (a, a + 1), scale=-1.0)
-            act("CT%d" % w, "CT%d" % w, F.Relu, scale=-1.0)
-        after = {0: (5,), 4: (0,), 8: (1, 3), 11: (4, 2)}
-        for k, a in enumerate(VKEYS):
+
+        def over(k):
+            a = VKEYS[k]
             w, e, s = k // 4, k % 4, "SS:%d:%d" % (16 * a + 15, 16 * a + 16)
             ts("CT%d:%d:%d:4" % (w, e, 64 * a + 64), "PS:0:%d" % (16 * a + 16), s, A.is_gt)
             ts("CT%d:%d:1280:4" % (w, 64 * a + 64 + e), "PS:%d:320" % (16 * a + 16), s, A.is_ge)
-            for w in after.get(k, ()):
-                quant("C%d" % w, "CT%d" % w)
-                mm("PK", "OB", 0, "C%d" % w, w == 5, w == 2)
-        act("STEP", "PK:0:320", F.Copy)
-        old, new = names[t % 2], names[(t + 1) % 2]
+
+        def upto(k):
+            a = SKEYS[k]
+            act("CT%d:%d:%d:4" % (3 + k // 4, k % 4, 64 * a + 64), "PSB:0:%d" % (16 * a + 16), F.Sign, bias="SS:%d:%d" % (16 * a + 15, 16 * a + 16), scale=-1.0)
+
+        def behind(k):
+            a = SKEYS[k]
+            act("CT%d:%d:1280:4" % (3 + k // 4, 64 * a + 64 + k % 4), "PSB:%d:320" % (16 * a + 16), F.Sign, bias="ND:%d:%d" % (a, a + 1), scale=-1.0)
+
+        act("NA", "SS:15:320:16", F.Abs, bias="TNY", scale=1.01 * 2.0 ** -24)
+        upto(0)
+        upto(1)
+        scan("SX", "SM:0:320", "HOLD", -HUGE, A.max, A.min)
+        over(0)
+        tt("ND", "SS:15:320:16", "NA", A.subtract)
+        tt("CT5:0:1280:4", "PS:0:320", "SX", A.is_equal)
+        for f, k in ((upto, 2), (upto, 3), (behind, 0), (behind, 1), (behind, 3), (upto, 4), (upto, 5), (upto, 6)):
+            f(k)
+        act("CT3", "CT3", F.Relu, scale=-1.0)
+        for f, k in ((behind, 4), (behind, 5), (upto, 7), (behind, 6), (behind, 7)):
+            f(k)
+        for r in (":0:640", ":640:1280"):
+            act("CT4" + r, "CT4" + r, F.Relu, scale=-1.0)
+        after = {1: ((5, 0), (5, 1)), 4: ((0, 0), (0, 1)), 8: ((1, 0), (1, 1)), 9: ((3, 0), (3, 1)), 10: ((4, 0),), 11: ((4, 1), (2, 0), (2, 1))}
+        for k in range(1, 12):
+            over(k)
+            for w, h in after.get(k, ()):
+                if w in (2, 4):
+                    quant("C%d" % w, "CT%d:%d:%d" % (w, 640 * h, 640 * h + 640), HALVES[h])
+                elif h == 0:
+                    quant("C%d" % w, "CT%d" % w)
+                mm(("PK", "PH")[h], "OB", 0, "C%d" % w, w == 5, w == 2, r=HALVES[h])
+        act("STEP:0:160", "PK:0:160", F.Copy)
+        cp("STEP:160:320", "PH:0:160")
+        for b in range(4):
+            mm("PF%d" % b, "E%d" % b, 0, "X")
         for r, l in zip(HALVES, LISTS):
-            tt(new + r, "STEP@COFF" + l, old + r, A.add)
+            tt("KF" + r, "STEP@COFF" + l, "SK" + r, A.add)
+        ranks()
 
-        def deal(t=t, arr=arr):
-            banks = ("PH", "PS", "PSB", "PK")
+        def early(t=t, arr=arr, last=last):
+            for b in range(2 * last, 4):
+                act("FB%d" % b, "PF%d:0:320" % b, F.Copy)
             for b in range(4):
-                mm(banks[b], "L", P * b, "A%d" % t, extra=[(arr, cnt[arr])])
+                mm(BANKS[b], "L", P * b, "A%d" % t, extra=[(arr, cnt[arr])])
             for b in range(4):
-                act("HB%d" % b, banks[b] + ":1:320:2", F.Copy, scale=0.03125)
+                act("HB%d" % b, BANKS[b] + ":1:320:2", F.Copy, scale=0.03125)
 
-        def final(new=new):
-            if last:
-                ts("PT1", new, WHOLE, A.add, WHOLE + 1.0, A.subtract)
+        def late(k, last=last):
+            if last and k == 0:
                 quant("V", "VT")
-                for b in range(2, 4):
-                    cp("FH%d" % b, "PF%d:0:320" % b)
+            elif last and k == -1:
+                ts("PT0", "KF", WHOLE, A.add, WHOLE + 1.0, A.subtract)
+            elif last and k == 1:
+                act("PT1", "PT0@INV", F.Copy)
+                dma("dpt", [("y", T.pt[:, :], T.PT1[0:P:16, :])], [], ["PT1"])
+            elif k == 1:
+                for a, e, l in MADE:
+                    for b in range(4):
+                        act("FS%d:%d:%d" % (b, a, e), "FB%d@INV" % b + l, F.Copy)
 
-        order(new, False, not last, (2896, 3216, NV)[t], final, deal)
-        if last:
-            dma("dpt", [("y", T.pt[:, :], T.PT1[0:P:16, :])], [], ["PT1"])
+        def add(h, b):
+            a, e, l = MADE[h]
+            tt("X:%d:%d:4" % (4 * a + b, 4 * e), "HB%d@C2OFF" % b + l, "FS%d:%d:%d" % (b, a, e), A.add)
+
+        def new_x(k):
+            if k == 0:
+                for b in range(4):
+                    add(0, b)
+                add(1, 0)
+                pairs(0)
+                halve(0, (2, 0, 3, 1))
+                for b in range(1, 4):
+                    add(1, b)
+            elif k == 1:
+                cp("X:1280:1284", "X:1276:1280")
+                pairs(1)
+                halve(1, (2, 0, 3))
+            elif k == 4:
+                halve(1, (1,), True)
+
+        order(t + 1, early, late)
         if not last:
-            for b in range(4):
-                act("GB%d" % b, "HB%d@C2OFF" % b, F.Copy)
             lists(t + 1 < R - 1, new_x)
 
-    for r, l in zip(HALVES, LISTS):
-        for b in range(2):
-            act("GB%d" % b + r, "HB%d@C2OFF" % b + l, F.Copy)
-    for h, bank in enumerate(("PS", "PSB")):
-        r, a, x = HALVES[h], 160 * h, "X:%d:%d" % (640 * h, 640 * h + 640)
+    for b in range(2):
+        act("GB%d" % b, "HB%d@C2OFF" % b, F.Copy)
+    for b in range(2, 4):
+        tt("FS%d" % b, "HB%d@C2OFF" % b, "FB%d" % b, A.add)
+    for b in range(2):
+        tt("FS%d" % b, "GB%d" % b, "PF%d:0:320" % b, A.add)
+    for h in range(2):
         for b in range(2, 4):
-            tt("X:%d:%d:4" % (4 * a + b, 4 * a + 640), "HB%d@C2OFF" % b + LISTS[h], "FH%d" % b + r, A.add)
-        for b in range(2):
-            tt("X:%d:%d:4" % (4 * a + b, 4 * a + 640), "GB%d" % b + r, "PF%d" % b + r, A.add)
-        op("v", lambda: V.quantize_mx(ap("qX" + r), ap("sX" + r), ap(x)), ["qX" + r, "sX" + r], [x])
-        i = ["qV", "sV", "qX" + r, "sX" + r]
-        op("t", lambda: TE.matmul_mx(ap(bank + ":0:160"), ap(i[0]), ap(i[1]), ap(i[2]), ap(i[3]), True, True), [bank], i)
+            act("X:%d:%d:4" % (640 * h + b, 640 * h + 640), "FS%d@INV" % b + LISTS[h], F.Copy)
+    for h, bank in enumerate(("PS", "PSB")):
+        r, a = HALVES[h], 160 * h
+        for k, b in (((0, 0), (0, 1), (1, 0)), ((1, 1),))[h]:
+            cp("X:%d:%d:4" % (640 * k + b, 640 * k + 640), "FS%d@INV" % b + LISTS[k])
+        quant("X", "X:%d:%d" % (4 * a, 4 * a + 640), r)
+        mm(bank, "V", 0, "X", r=r)
         dma("dout", [("y", T.oc[:, 4 * a:4 * a + 640], T.qX[:, a:a + 160].bitcast(dt.uint8))], [], ["qX" + r])
+        if h:
+            dma("dout", [("sy"[k // 2], T.osc[4 * k:4 * k + 4, :], T.sX[32 * k:32 * k + 4, 0:C]) for k in range(4)], [], ["sX"])
         act("YB" + r, bank + ":0:160", F.Copy)
         dma("dy", [("s", T.y[:, a:a + 160], T.YB[:, a:a + 160])], [], ["YB" + r])
-    dma("dout", [("y", T.osc[4 * k:4 * k + 4, :], T.sX[32 * k:32 * k + 4, 0:C]) for k in range(4)], [], ["sX"])
     wait("g", list(cnt.items()))

@@ -2,8 +2,9 @@ from concourse.mybir import dt, AluOpType as A, ActivationFunctionType as F
 
 C, P, R = 320, 128, 3
 NV = 3520
+WIDE = (2576, 2896, 3216, NV)
 WW = 2 * NV + C
-NS = 11
+UP = 1776
 SKEYS = (0, 1, 19, 18, 2, 3, 17, 16)
 VKEYS = tuple(a for a in range(20) if a not in SKEYS)
 HALVES, LISTS = (":0:160", ":160:320"), (":0:10", ":10:20")
@@ -30,32 +31,33 @@ def _t(n, d, parts, where="sbuf"):
 
 
 for _n, _w in (("E16", C), ("JR", C), ("JP0", C), ("JP", C), ("TNY", 1), ("MASK", C), ("RS", C), ("MB0", C), ("MB", C), ("SEL", C), ("HOLD", C),
-               ("KP", C), ("KF", C), ("KM", C), ("KS", C), ("S1", C), ("S2", C), ("SM", C + 1), ("SS", C), ("SX", C), ("NA", 20), ("ND", 20),
+               ("KP", C), ("KF0", C), ("KF1", C), ("KM", C), ("KS", C), ("S1", C), ("S2", C), ("SM", C), ("SS", C + 1), ("NA", 20), ("ND", 20),
                ("STEP", C), ("PT0", C), ("PT1", C), ("YB", C), ("XA", 40), ("XB", 40), ("OW", 40)):
     _b(_n, _w)
 _t("SKB", "float32", [("SK", C), ("SKE", 16)])
 _t("CTAB", "float32", [("C16", 20), ("C1", 20), ("QP", 4), ("Q20", 4), ("ODD", 4), ("NO", 4), ("NE", 4), ("CR", 4), ("CH", 4),
                        ("TOP", 4), ("JT0", 20), ("JT", 20), ("FE", 4), ("FO", 4), ("QH", 4)])
-_t("FTAB", "float32", [("ACC", 20), ("TH", 12), ("FR", 20), ("PL", 20), ("KT", 32), ("KA", 64), ("KB", 64)])
+_t("FTAB", "float32", [("ACC", 20), ("TH", 12), ("FR", 20), ("PL", 20), ("KT", 20)] +
+   [(k + x, w) for x in ("", "J") for k, w in (("KU", 20), ("KV", 32), ("KA", 64), ("KB", 64))])
 _t("TAB", "bfloat16", [("TA", 12), ("TB", 12)])
 _b("VSB", 1600, "float16")
 _b("GS", 640, "float16")
 _t("CTABI", "int32", [("QI", 4), ("QA", 4), ("QB", 4)])
-_t("ITAB", "int32", [("P1", 20), ("P2", 20), ("KI", 20)])
-_t("UTAB", "uint16", [("OQ", 40)] + [(k, 20) for k in ("PERM", "RP", "OWU", "COFF", "C2OFF", "P2U", "IXU", "INV", "JU")])
+_t("ITAB", "int32", [("P1", 20), ("P2", 20)])
+_t("UTAB", "uint16", [("OQ", 40), ("OQJ", 40)] + [(k, 20) for k in ("PERM", "RP0", "RP1", "OWU", "COFF", "C2OFF", "P2U", "IXU", "JU", "X40", "X41", "X42", "X43")])
 _b("R16", C, "uint16")
 _b("UI", 8, "int32")
 _b("PR", C, "int32")
 _b("PTAB", 20, "int32")
 _b("UL", 8, "uint16")
-for _n, _w in (("ZER", 512), ("ONE", 512), ("OB1", 512), ("OB2", 512), ("CDF", C), ("ONES", C), ("UT", 512), ("VT", 512), ("XIN", 4 * C),
-               ("X", 4 * C + 8), ("Z", 4 * C), ("W", WW), ("CC", NV), ("D", 3536), ("G", 640), ("GT", 640), ("W2", 8 * C), ("N2", 4 * C), ("RKX", 640),
-               ("MBH", 640), ("IX", 640), ("SELH", C), ("HOLDH", C), ("I0", C), ("I1", C), ("I2", C)):
+for _n, _w in (("ZER", 512), ("ONE", 512), ("OB1", 512), ("OB2", 512), ("CDF", C), ("UT", 512), ("VT", 512), ("XIN", 4 * C),
+               ("X", 4 * C + 8), ("Z", 4 * C), ("W", WW), ("CC", NV // 2), ("D", 2 * UP), ("G", 640), ("GT", 640), ("W2", 8 * C), ("N2", 4 * C), ("RKX", 640),
+               ("MBH", 640), ("IX", 640), ("GJ", 640), ("RKXJ", 640)):
     _b(_n, _w, "bfloat16")
-_t("JUNK", "bfloat16", [("JUNK%d" % k, C) for k in range(NS)])
+_t("JUNK", "bfloat16", [("JUNK%d" % k, C) for k in range(10)])
 _t("CMPB", "bfloat16", [("CMP%d" % k, C) for k in range(10)])
 _t("EBB", "bfloat16", [("EB%d" % k, 512) for k in range(4)])
-for _n, _w in (("FB", C), ("FS", C), ("PB", C), ("GB", C), ("HB", 160)):
+for _n, _w in (("FB", C), ("FJ", C), ("FS", C), ("PB", C), ("HB", 160)):
     _t(_n + "B", "bfloat16", [("%s%d" % (_n, k), _w) for k in range(4)])
 _t("CTB", "bfloat16", [("CT%d" % k, 4 * C) for k in range(6)])
 _t("PFB", "float32", [("PF%d" % k, 512) for k in range(4)], "psum")
@@ -215,9 +217,11 @@ def rank_program(g, core, T, topo):
     fill("ZER", 0.0)
     ts("QA:0:2", "QI:0:2", 15, A.bitwise_and)
     ts("QB:0:2", "QI:0:2", 4, A.arith_shift_right, 1, A.bitwise_and)
+    fill("ONE:0:256", 1.0)
     ts("TOP:0:1", "QA:0:1", 15.0, A.is_equal, 4096.0, A.mult)
     cp("QP:0:1", "QA:0:1")
     cp("ODD:0:1", "QB:0:1")
+    fill("ONE:256:512", 1.0)
     ts("JT0", "C16", "QP:0:1", A.add, 352.0, A.add)
     ts("QH:0:1", "QP:0:1", 0.5, A.add)
     ts("QH:1:2", "QP:0:1", -0.5, A.add)
@@ -234,8 +238,10 @@ def rank_program(g, core, T, topo):
     ts("XB:0:40:2", "C16", "QP:0:1", A.add, float(NV), A.add)
     fill("SKE", 3600.0)
     fill("XA:0:40:2", 0.0)
-    fill("KT", 0.0)
-    fill("SM:0:1", -HUGE)
+    fill("KV", 0.0)
+    fill("KVJ", 0.0)
+    fill("SS:0:1", -HUGE)
+    fill("TNY", 2.0 ** -126)
 
     def clear(a, b):
         for c in range(a, b, 512):
@@ -243,13 +249,13 @@ def rank_program(g, core, T, topo):
 
     clear(0, 1024)
     act("MB0", "E16", F.Sign, bias="QH:1:2", scale=-1.0)
-    act("ONE", "ZER", F.Identity, bias=1.0)
+    clear(1024, 1536)
     dma("dw", [("y", T.qL[:, 0:512].bitcast(dt.uint8), T.wc[:, :]), ("y", T.sL[:, 0:512], T.ws[:, :])], ["qL", "sL"], [])
     dma("dv", [("y", T.VT[:, :], T.v[:, :])], ["VT"], [])
     for b in range(4):
         sel("EB%d" % b, "ZER", [[1, 512]], A.not_equal, 1.0, -b, -4)
-    iota("W2", [[0, 8 * C]])
     iota("UI", [[16, 8]])
+    iota("W2", [[0, 8 * C]])
     sel("OB1", "ONE", [[-16, 8], [0, 64]], A.is_ge, 0.0, 0, 1)
     sel("OB2", "OB1", [[16, 8], [0, 64]], A.is_ge, 0.0, 15, -1)
     tt("KS:15:320:16", "PTAB", "JT", A.add)
@@ -262,16 +268,17 @@ def rank_program(g, core, T, topo):
     def half(k):
         scan("VSB:%d:%d" % (160 * k, 160 * k + 160), "CMP%d:0:160" % k, "CMP%d:160:320" % k, 0.0, A.add, A.add)
 
-    def spread(sem, a, b):
-        moves = [(T.D[0:P:32, a:b], T.CC[0:P:32, a:b]), (T.D[16:P:32, a + 1:b + 1], T.CC[16:P:32, a:b])]
+    def spread(sem, n, a, b, to):
+        e = to + b - a
+        moves = [(T.D[0:P:32, to:e], T[n][0:P:32, a:b]), (T.D[16:P:32, to + 1:e + 1], T[n][16:P:32, a:b])]
         for d in range(1, 4):
-            moves.append((T.D[32 * d + 1 + d:P:16, a:b], T.CC[d:P - 32 * d:16, a:b]))
-            moves.append((T.D[4 + d:P - 32 * d:16, a + 1:b + 1], T.CC[32 * d + 4 + d:P:16, a:b]))
-        dma(sem, [("ys"[k % 2], o, i) for k, (o, i) in enumerate(moves)], ["D:%d:%d" % (a, b)], ["CC:%d:%d" % (a, b)])
+            moves.append((T.D[32 * d + 1 + d:P:16, to:e], T[n][d:P - 32 * d:16, a:b]))
+            moves.append((T.D[4 + d:P - 32 * d:16, to + 1:e + 1], T[n][32 * d + 4 + d:P:16, a:b]))
+        dma(sem, [("ys"[k % 2], o, i) for k, (o, i) in enumerate(moves)], ["D:%d:%d" % (to, e + 1)], ["%s:%d:%d" % (n, a, b)])
 
     key = ["KS:%d:%d" % (16 * c + 15, 16 * c + 16) for c in range(20)]
 
-    def first_ranks():
+    def first_ranks(by_column):
         for k in range(10):
             act("JUNK%d" % k, "KP", F.Sign, acc="ACC:%d:%d" % (k, k + 1), bias=key[2 * k], scale=-1.0)
         act("MB", "MB0", F.Copy, scale=BIG)
@@ -279,103 +286,142 @@ def rank_program(g, core, T, topo):
         ts("R16:0:160", "KP:0:160", 16.0, A.mult, "CR:0:1", A.add)
         tt("TB:0:10", "TH:0:10", "TA:0:10", A.subtract)
         ts("R16:160:320", "KP:160:320", 16.0, A.mult, "CR:0:1", A.add)
-        cp("KF", "KP@PERM")
+        cp("KF0", "KP@PERM")
         for k in range(10):
             ts("CMP%d" % k, "R16", "TA:%d:%d" % (k, k + 1), A.subtract, "TB:%d:%d" % (k, k + 1), A.is_lt)
-            if k:
-                half(k - 1)
-        ts("MASK:0:160", "E16:0:160", "QP:0:1", A.is_equal)
+            if k > 1:
+                half(k - 2)
+            if k in (1, 5):
+                next(by_column)
+        half(8)
+        next(by_column)
         half(9)
-        ts("RP:0:20:2", "ACC:0:10", 319.0, A.add, 0.5, A.mult)
-        cp("RP:1:20:2", "VSB:159:1600:160")
-        ts("MASK:160:320", "E16:160:320", "QP:0:1", A.is_equal)
+        ts("MASK:0:160", "E16:0:160", "QP:0:1", A.is_equal)
+        ts("RP0:0:20:2", "ACC:0:10", 319.0, A.add, 0.5, A.mult)
+        cp("RP0:1:20:2", "VSB:159:1600:160")
 
-    def ranks():
+    def ranks(t, by_column):
+        kf, rp = "KF%d" % (t % 2), "RP%d" % (t % 2)
         for r in HALVES:
-            scan("KM" + r, "KF" + r, "MASK" + r, 0.0, A.max, A.mult)
+            scan("KM" + r, kf + r, "MASK" + r, 0.0, A.max, A.mult)
         for r in HALVES:
             scan("KS" + r, "RS" + r, "KM" + r, 0.0, A.mult, A.add)
-        n = 20 - NS
-        for k in range(NS):
-            act("JUNK%d" % k, "KF", F.Sign, acc="ACC:%d:%d" % (k, k + 1), bias=key[n + k], scale=-1.0)
-        for k in range(n):
-            ts("CMP%d" % k, "KF", key[k], A.is_lt)
-            if k:
-                half(k - 1)
-        half(n - 1)
-        ts("RP:%d:20" % n, "ACC:0:%d" % NS, 319.0, A.add, 0.5, A.mult)
-        cp("RP:0:%d" % n, "VSB:159:%d:160" % (160 * n))
+        for k in range(10):
+            act("JUNK%d" % k, kf, F.Sign, acc="ACC:%d:%d" % (k, k + 1), bias=key[2 * k], scale=-1.0)
+        ts("R16:0:160", kf + ":0:160", 16.0, A.mult, "CR:0:1", A.add)
+        ts("TH:0:10", "KS:31:320:32", 16.0, A.mult, "CH:0:1", A.add)
+        ts("TA:0:10", "KS:31:320:32", 16.0, A.mult, "CH:0:1", A.add)
+        ts("R16:160:320", kf + ":160:320", 16.0, A.mult, "CR:0:1", A.add)
+        tt("TB:0:10", "TH:0:10", "TA:0:10", A.subtract)
+        next(by_column)
+        for k in range(10):
+            ts("CMP%d" % k, "R16", "TA:%d:%d" % (k, k + 1), A.subtract, "TB:%d:%d" % (k, k + 1), A.is_lt)
+            if k > 1:
+                half(k - 2)
+        half(8)
+        next(by_column)
+        half(9)
+        ts(rp + ":0:20:2", "ACC:0:10", 319.0, A.add, 0.5, A.mult)
+        next(by_column)
+        cp(rp + ":1:20:2", "VSB:159:1600:160")
 
-    def own(rank, add):
-        ts("RKX:0:640:32", rank, add, A.add, "FE:0:1", A.max)
-        ts("RKX:1:640:32", rank, add, A.add, "FO:0:1", A.max)
+    def own(x, rank, add):
+        ts("RKX%s:0:640:32" % x, rank, add, A.add, "FE:0:1", A.max)
+        ts("RKX%s:1:640:32" % x, rank, add, A.add, "FO:0:1", A.max)
 
-    def order(t, scalar_early, scalar_late):
-        last, nv = t == R, 2576 + C * t - 16 * (t == R)
-        cp("SK@RP", "KF")
-        scalar_early()
+    def offsets(x, keys, h):
+        ts("KU" + x, keys, h - 0.5, A.is_ge, float(UP + 1 - h), A.mult)
+        yield
+        tt("KV%s:0:20" % x, "KU" + x, keys, A.add)
+        yield
+        turn("KA%s:16:48" % x, "KV" + x)
+        yield
+        cp("KA%s:0:16" % x, "KA%s:16:32" % x)
+        cp("KA%s:48:64" % x, "KA%s:32:48" % x)
+        yield
+        turn("KB" + x, "KA" + x)
+        yield
+        cp("OQ%s:0:40:2" % x, "KB%s:0:20" % x)
+        cp("OQ%s:1:40:2" % x, "KB%s:32:52" % x)
+        yield
+
+    def order(t, by_column, scalar_early, scalar_late):
+        last, nv = t == R, WIDE[t]
+        h = nv // 2
+        rp, x = "RP%d" % (t % 2), "J" if last else ""
+        by_slot = iter(()) if last else offsets("", "KT", h)
+        next(by_column)
+        cp("SK@" + rp, "KF%d" % (t % 2))
+        act("JUNK0", "KF%d" % (t % 2), F.Sign, acc="ACC:0:1", bias=h - 0.5, scale=-1.0)
+        scalar_early(0)
+        act("W:%d:%d" % (h - 1, h), "ACC:0:1", F.Copy, scale=0.5)
+        scalar_early(1)
+        next(by_column)
         if t == 0:
             fill("RKX:320:640", 32768.0)
-        if last:
-            cp("KT:0:20", "KS:15:320:16")
-            cp("KI", "KS:15:320:16")
+        else:
+            own("J", rp, -160.0)
         scan("S1", "SK", "MB", 0.0, A.min, A.max)
         op("v", lambda: V.tensor_tensor_scan(ap("S2"), T.SKB[:, 1:C + 1], ap("MB"), 0.0, A.min, A.max), ["S2"], ["SK", "SKE", "MB"])
         if not last:
-            tt("KT:0:20", "S1:15:320:16", "SK:0:320:16", A.max)
+            tt("KT", "S1:15:320:16", "SK:0:320:16", A.max)
         tt("P1", "S1:15:320:16", "SK:0:320:16", A.max)
         tt("XB:1:40:2", "S1:15:320:16", "SK:0:320:16", A.max)
         tt("P2", "S2:15:320:16", "SK:1:320:16", A.max)
-        turn("KA:16:48", "KT")
-        if t in (0, R):
-            tt("FR", "KT:0:20", "KI" if last else "P1", A.subtract)
+        next(by_slot, 0)
+        if not last:
+            tt("FR", "KT", "P1", A.subtract)
         tt("XA:1:40:2", "P1", "P2", A.is_equal)
-        cp("KA:0:16", "KA:16:32")
-        cp("KA:48:64", "KA:32:48")
+        next(by_slot, 0)
+        if not last:
+            ts("JU", "FR", 512.0, A.mult, 160.0, A.add)
         scan("OW", "XA", "XB", 0.0, A.mult, A.add)
-        if t in (0, R):
-            ts("JU" if last else "INV", "FR", 512.0, A.mult, 160.0, A.add)
-        scalar_late(-2)
-        turn("KB", "KA")
-        cp("OWU", "OW:1:40:2")
-        if last:
-            own("RP", -160.0)
-        elif t == 0:
-            ts("RKX:16:640:32", "C1", 0.0, A.mult, "NO:0:1", A.add)
-            ts("RKX:17:640:32", "C1", 0.0, A.mult, "NE:0:1", A.add)
-        cp("W@OWU", "CDF")
-        cp("OQ:0:40:2", "KB:0:20")
-        cp("OQ:1:40:2", "KB:32:52")
-        h = nv // 2
-        lo, hi = "0:%d" % h, "%d:%d" % (h, nv)
-        scan("CC:" + lo, "W:" + lo, "W:" + lo, -160.0, A.max, A.max)
-        spread("dd", 0, h)
+        scalar_late(-3)
+        next(by_slot, 0)
         if t == 0:
-            own("JT0", -512.0)
-        scan("CC:" + hi, "W:" + hi, "W:" + hi, "CC:%d:%d" % (h - 1, h), A.max, A.max)
-        spread("de", h, nv)
+            ts("RKX:16:640:32", "C1", 0.0, A.mult, "NO:0:1", A.add)
+        cp("OWU", "OW:1:40:2")
+        next(by_slot, 0)
+        cp("W@OWU", "CDF")
+        spread("de", "W", h - 1, nv, UP)
+        next(by_slot, 0)
+        if t == 0:
+            ts("RKX:17:640:32", "C1", 0.0, A.mult, "NE:0:1", A.add)
+        scan("CC:0:%d" % h, "W:0:%d" % h, "W:0:%d" % h, -160.0, A.max, A.max)
+        spread("dd", "CC", 0, h, 0)
         if not last:
             iota("W:0:%d" % min(nv + C, NV), [[0, min(nv + C, NV)]], -160)
+        next(by_slot, 0)
+        next(by_column)
+        if t == 0:
+            own("", "JT0", -512.0)
         scalar_late(-1)
-        if t:
-            cp("I0@" + ("JU" if last else "RP"), "CDF")
-            scalar_late(0)
-            scan("I1", "I0", "SELH", -1024.0, A.max, A.min)
-        act("G:320:640", "D@OQ:20:40", F.Copy)
-        cp("G:0:320", "D@OQ:0:20")
-        if t:
-            scan("I2", "HOLDH", "I1", -1024.0, A.min, A.max)
-        turn("GT:0:320", "G:0:320")
-        if t:
-            ts("INV", "I2:15:320:16", 159.0, A.add)
-        scalar_late(1)
-        turn("GT:320:640", "G:320:640")
+        up = "D:%d:%d" % (UP, UP + nv - h + 2)
+        scan(up, up, up, -160.0, A.max, A.max)
+        scalar_late(-2)
+        act("G:320:640", "D@OQ%s:20:40" % x, F.Copy)
+        for r, l in zip(HALVES, LISTS):
+            cp("G" + r, "D@OQ" + x + l)
+        scalar_late(0)
+        for r in HALVES + (":320:640",):
+            turn("GT" + r, "G" + r)
         for r in (":0:320", ":320:640"):
-            scan("GS" + r, "RKX" + r, "GT" + r, 4096.0, A.min, A.add)
-        scalar_late(2)
+            scan("GS" + r, "RKX" + x + r, "GT" + r, 4096.0, A.min, A.add)
+        scalar_late(1)
         tt("PL", "GS:14:640:32", "GS:30:640:32", A.add)
         if t:
             ts("C2OFF", "PL", 1.0 / 16, A.mult, 80.0 - 15.0 / 32, A.add)
+
+    def cells(k):
+        if k < 2:
+            turn("GT" + (":0:320", ":320:640")[k], "GJ" + (":0:320", ":320:640")[k])
+        elif k < 4:
+            r = (":0:320", ":320:640")[k - 2]
+            scan("GS" + r, "RKXJ" + r, "GT" + r, 4096.0, A.min, A.add)
+        elif k == 4:
+            tt("PL", "GS:14:640:32", "GS:30:640:32", A.add)
+        else:
+            ts("COFF", "PL", 1.0 / 8, A.mult, 160.0 - 7.0 / 16, A.add)
 
     def pairs(h):
         a, e = PIECES[h]
@@ -397,9 +443,8 @@ def rank_program(g, core, T, topo):
 
     def lists(again, between):
         ts("P2U", "PL", 1280.0, A.add)
-        ts("COFF", "PL", 1.0 / 8, A.mult, 160.0 - 7.0 / 16, A.add)
         between(0)
-        cp("W2@P2U", "ONES")
+        cp("W2@P2U", "ONE:0:320")
         between(1)
         scan("N2", "W2:0:2560:2", "W2:1:2560:2", -160.0, A.add, A.add)
         if again:
@@ -410,51 +455,56 @@ def rank_program(g, core, T, topo):
         ts("IXU", "IX:31:640:32", 159.0, A.add, 0.0, A.max)
         between(4)
 
-    def x_early():
-        for b in range(4):
-            act("FB%d" % b, "XIN:%d:1280:4" % b, F.Copy)
-        clear(1024, 3536)
+    def x_early(k):
+        for b in range(2 * k, 2 * k + 2):
+            act("FJ%d" % b, "XIN:%d:1280:4" % b, F.Copy)
+        if k:
+            clear(1536, 3072)
+            act("D:%d:%d" % (UP, UP + 1), "ZER:0:1", F.Identity, bias=-160.0)
 
     def x_late(k):
-        if k == -2:
+        if k == -3:
             for b in range(2):
-                act("X:%d:1280:4" % b, "FB%d@INV" % b, F.Copy)
+                act("X:%d:1280:4" % b, "FJ%d@JU" % b, F.Copy)
         elif k == -1:
             for b in range(2, 4):
-                cp("X:%d:1280:4" % b, "FB%d@INV" % b)
+                cp("X:%d:1280:4" % b, "FJ%d@JU" % b)
             for b in range(4):
                 quant("E%d" % b, "EB%d" % b)
             cp("X:1280:1284", "X:1276:1280")
-            act("JUNK10", "E16", F.Sign, bias="QH:0:1", scale=-1.0)
+            clear(3072, 2 * UP)
+            act("JUNK9", "E16", F.Sign, bias="QH:0:1", scale=-1.0)
             act("MBH:1:640:2", "MB0", F.Copy, scale=1024.0)
-            act("MBH:0:640:2", "JUNK10", F.Copy, scale=1024.0)
+            act("MBH:0:640:2", "JUNK9", F.Copy, scale=1024.0)
             act("RS", "E16", F.Sign)
+        elif k == -2:
             pairs(0)
-            pairs(1)
+        elif k == 0:
+            halve(0, (2, 0, 3, 1))
+            act("GJ", "D@OQJ", F.Copy)
         elif k == 1:
-            halve(0, range(4))
-            halve(1, range(4))
-            act("SEL", "MASK", F.Identity, bias=-HUGE, scale=2.0 * HUGE)
-            act("HOLD", "RS", F.Identity, bias=-HUGE, scale=2.0 * HUGE)
-        elif k == 2:
-            fill("ONES", 1.0)
+            pairs(1)
+            halve(1, (2, 0, 3, 1))
+            act("RKXJ", "RKX", F.Copy)
 
-    first_ranks()
-    order(0, x_early, x_late)
+    by_column = offsets("J", "KS:15:320:16", WIDE[0] // 2)
+    first_ranks(by_column)
+    order(0, by_column, x_early, x_late)
 
     def sides(k):
         if k == 0:
             cp("UL", "UI")
-            fill("TNY", 2.0 ** -126)
+            ts("MASK:160:320", "E16:160:320", "QP:0:1", A.is_equal)
         elif k == 1:
             quant("U", "UT")
             act("sUR", "sU@UL", F.Copy)
-            act("SELH", "MASK", F.Identity, bias=-1024.0, scale=2048.0)
-            act("HOLDH", "RS", F.Identity, bias=-1024.0, scale=2048.0)
+            act("SEL", "MASK", F.Identity, bias=-HUGE, scale=2.0 * HUGE)
         elif k == 2:
             op("v", lambda: V.tensor_copy(T.qUR[:, 0:P].bitcast(dt.uint32), T.qU[:, 0:P].bitcast(dt.uint32).indirect(T.UL[:, 0:8])), ["qUR"], ["qU", "UL"])
         elif k == 3:
-            quant("OB", "OB2")
+            cells(0)
+        else:
+            cells(1)
 
     lists(True, sides)
     for t in range(R):
@@ -463,7 +513,11 @@ def rank_program(g, core, T, topo):
         for b in range(2):
             act("Z:%d:1280:4" % (b + 2), "PB%d@IXU" % (b + 2), F.Copy)
             cp("Z:%d:1280:4" % b, "PB%d@IXU" % b)
-        if t == 0:
+        if t:
+            cells(3)
+        else:
+            own("J", "RP0", -160.0)
+            act("HOLD", "RS", F.Identity, bias=-HUGE, scale=2.0 * HUGE)
             for a in range(0, 4 * C, 512):
                 act("CT5:%d:%d" % (a, min(a + 512, 4 * C)), "ZER:0:%d" % min(512, 4 * C - a), F.Copy)
         for h, bank in enumerate(("PK", "PH")):
@@ -476,34 +530,43 @@ def rank_program(g, core, T, topo):
         g.remote_dma(T["qA%d" % t][:, 0:C].bitcast(dt.uint8), T["q" + qz][:, 0:C].bitcast(dt.uint8), T.sem[arr], T.sem.sent, pid, rid, m)
         g.remote_dma(T["sA%d" % t][:, 0:C], T["s" + qz][:, 0:C], T.sem[arr], T.sem.sent, pid, rid, m)
         cnt["sent"], cnt[arr] = cnt.get("sent", 0) + n, n
-        mm("PS", "UR", 0, qz)
         mm("PSB", "UR", 0, qz)
-        for bank, r, r1 in zip(("PK", "PH"), HALVES, (":1:161", ":161:321")):
-            tt("SM" + r1, bank + ":0:160", "SEL" + r, A.min)
+        mm("PS", "UR", 0, qz)
+        if t:
+            cells(4)
+        else:
+            quant("OB", "OB2")
+            cells(2)
+        for bank, r in zip(("PK", "PH"), HALVES):
+            tt("SM" + r, bank + ":0:160", "SEL" + r, A.min)
         for r, r1 in zip(HALVES, (":1:161", ":161:321")):
-            scan("SS" + r, "HOLD" + r, "SM" + r1, -HUGE, A.min, A.max)
+            scan("SS" + r1, "HOLD" + r, "SM" + r, -HUGE, A.min, A.max)
 
         def over(k):
             a = VKEYS[k]
-            w, e, s = k // 4, k % 4, "SS:%d:%d" % (16 * a + 15, 16 * a + 16)
-            ts("CT%d:%d:%d:4" % (w, e, 64 * a + 64), "PS:0:%d" % (16 * a + 16), s, A.is_gt)
-            ts("CT%d:%d:1280:4" % (w, 64 * a + 64 + e), "PS:%d:320" % (16 * a + 16), s, A.is_ge)
+            w, e, s = k // 4, k % 4, "SS:%d:%d" % (16 * a + 16, 16 * a + 17)
+            ts("CT%d:%d:%d:4" % (w, e, 64 * a + 68), "PS:0:%d" % (16 * a + 17), s, A.is_gt)
+            ts("CT%d:%d:1280:4" % (w, 64 * a + 68 + e), "PS:%d:320" % (16 * a + 17), s, A.is_ge)
 
         def upto(k):
             a = SKEYS[k]
-            act("CT%d:%d:%d:4" % (3 + k // 4, k % 4, 64 * a + 64), "PSB:0:%d" % (16 * a + 16), F.Sign, bias="SS:%d:%d" % (16 * a + 15, 16 * a + 16), scale=-1.0)
+            n = min(16 * a + 17, C)
+            act("CT%d:%d:%d:4" % (3 + k // 4, k % 4, 4 * n), "PSB:0:%d" % n, F.Sign, bias="SS:%d:%d" % (16 * a + 16, 16 * a + 17), scale=-1.0)
 
         def behind(k):
             a = SKEYS[k]
-            act("CT%d:%d:1280:4" % (3 + k // 4, 64 * a + 64 + k % 4), "PSB:%d:320" % (16 * a + 16), F.Sign, bias="ND:%d:%d" % (a, a + 1), scale=-1.0)
+            act("CT%d:%d:1280:4" % (3 + k // 4, 64 * a + 68 + k % 4), "PSB:%d:320" % (16 * a + 17), F.Sign, bias="ND:%d:%d" % (a, a + 1), scale=-1.0)
 
-        act("NA", "SS:15:320:16", F.Abs, bias="TNY", scale=1.01 * 2.0 ** -24)
+        act("NA", "SS:16:321:16", F.Abs, bias="TNY", scale=1.01 * 2.0 ** -24)
         upto(0)
         upto(1)
-        scan("SX", "SM:0:320", "HOLD", -HUGE, A.max, A.min)
-        over(0)
-        tt("ND", "SS:15:320:16", "NA", A.subtract)
-        tt("CT5:0:1280:4", "PS:0:320", "SX", A.is_equal)
+        for h, bank in enumerate(("PK", "PH")):
+            tt("CT5:%d:%d:4" % (640 * h, 640 * h + 640), bank + ":0:160", "SS" + HALVES[h], A.is_equal)
+        if t == 0:
+            cells(3)
+        tt("ND", "SS:16:321:16", "NA", A.subtract)
+        if t == 0:
+            cells(4)
         for f, k in ((upto, 2), (upto, 3), (behind, 0), (behind, 1), (behind, 3), (upto, 4), (upto, 5), (upto, 6)):
             f(k)
         act("CT3", "CT3", F.Relu, scale=-1.0)
@@ -511,43 +574,62 @@ def rank_program(g, core, T, topo):
             f(k)
         for r in (":0:640", ":640:1280"):
             act("CT4" + r, "CT4" + r, F.Relu, scale=-1.0)
-        after = {1: ((5, 0), (5, 1)), 4: ((0, 0), (0, 1)), 8: ((1, 0), (1, 1)), 9: ((3, 0), (3, 1)), 10: ((4, 0),), 11: ((4, 1), (2, 0), (2, 1))}
-        for k in range(1, 12):
-            over(k)
+        after = {-1: ((5, 0), (5, 1)), 4: ((0, 0), (0, 1)), 8: ((1, 0), (1, 1)), 9: ((3, 0), (3, 1)), 10: ((4, 0),), 11: ((4, 1), (2, 0), (2, 1))}
+        for k in range(-1, 12):
+            if k >= 0:
+                over(k)
             for w, h in after.get(k, ()):
                 if w in (2, 4):
                     quant("C%d" % w, "CT%d:%d:%d" % (w, 640 * h, 640 * h + 640), HALVES[h])
                 elif h == 0:
                     quant("C%d" % w, "CT%d" % w)
                 mm(("PK", "PH")[h], "OB", 0, "C%d" % w, w == 5, w == 2, r=HALVES[h])
+        cells(5)
+        if t == 0:
+            quant("V", "VT")
+        for b in range(4 * last):
+            ts("X4%d" % b, "RP%d" % (t % 2), 4.0, A.mult, float(b), A.add)
         act("STEP:0:160", "PK:0:160", F.Copy)
         cp("STEP:160:320", "PH:0:160")
-        for b in range(4):
+        for b in range(4 - 4 * last):
             mm("PF%d" % b, "E%d" % b, 0, "X")
+        for b in range(4):
+            mm(BANKS[b], "L", P * b, "A%d" % t, extra=[(arr, cnt[arr])])
         for r, l in zip(HALVES, LISTS):
-            tt("KF" + r, "STEP@COFF" + l, "SK" + r, A.add)
-        ranks()
+            tt("KF%d" % ((t + 1) % 2) + r, "STEP@COFF" + l, "KF%d" % (t % 2) + r, A.add)
+        by_column = offsets("J", "KS:15:320:16", WIDE[t + 1] // 2)
+        ranks(t + 1, by_column)
 
-        def early(t=t, arr=arr, last=last):
-            for b in range(2 * last, 4):
-                act("FB%d" % b, "PF%d:0:320" % b, F.Copy)
-            for b in range(4):
-                mm(BANKS[b], "L", P * b, "A%d" % t, extra=[(arr, cnt[arr])])
-            for b in range(4):
+        def early(k, t=t, last=last):
+            for b in range(2 * k, 2 * k + 2):
+                if last:
+                    act("Z:%d:1280:4" % b, "X:0:1280@X4%d" % b, F.Copy)
+                else:
+                    act("FB%d" % b, "PF%d:0:320" % b, F.Copy)
+            for b in range(2 * k * (not last)):
+                act("FJ%d" % b, "FB%d@RP%d" % (b, t % 2), F.Copy)
+            for b in range(4 * k):
                 act("HB%d" % b, BANKS[b] + ":1:320:2", F.Copy, scale=0.03125)
 
-        def late(k, last=last):
-            if last and k == 0:
-                quant("V", "VT")
-            elif last and k == -1:
-                ts("PT0", "KF", WHOLE, A.add, WHOLE + 1.0, A.subtract)
-            elif last and k == 1:
-                act("PT1", "PT0@INV", F.Copy)
+        def late(k, t=t, last=last):
+            moves = [("FS%d:%d:%d" % (b, a, e), "FJ%d@JU" % b + l) for a, e, l in MADE for b in range(4)]
+            if last and k == -1:
+                quant("Y", "Z")
+                for b in (2, 3, 0, 1):
+                    mm("PF%d" % b, "E%d" % b, 0, "Y")
+                act("PT0", "KF%d" % ((t + 1) % 2), F.Identity, bias=WHOLE)
+                act("FJ2", "PF2:0:320", F.Copy)
+                act("PT1", "PT0", F.Identity, bias=-WHOLE - 1.0)
+                act("FJ3", "PF3:0:320", F.Copy)
                 dma("dpt", [("y", T.pt[:, :], T.PT1[0:P:16, :])], [], ["PT1"])
-            elif k == 1:
-                for a, e, l in MADE:
-                    for b in range(4):
-                        act("FS%d:%d:%d" % (b, a, e), "FB%d@INV" % b + l, F.Copy)
+            elif k == -1:
+                cp("FJ3", "FB3@RP%d" % (t % 2))
+                act("FJ2", "FB2@RP%d" % (t % 2), F.Copy)
+            if not last and k in (-1, 0):
+                for o, i in (moves[:2], moves[2:])[k + 1]:
+                    act(o, i, F.Copy)
+                if k == 0:
+                    act("GJ", "D@OQJ", F.Copy)
 
         def add(h, b):
             a, e, l = MADE[h]
@@ -566,31 +648,36 @@ def rank_program(g, core, T, topo):
                 cp("X:1280:1284", "X:1276:1280")
                 pairs(1)
                 halve(1, (2, 0, 3))
-            elif k == 4:
+            elif k < 4:
+                cells(k - 2)
+            else:
+                cells(2)
                 halve(1, (1,), True)
 
-        order(t + 1, early, late)
+        order(t + 1, by_column, early, late)
         if not last:
             lists(t + 1 < R - 1, new_x)
 
-    for b in range(2):
-        act("GB%d" % b, "HB%d@C2OFF" % b, F.Copy)
-    for b in range(2, 4):
-        tt("FS%d" % b, "HB%d@C2OFF" % b, "FB%d" % b, A.add)
-    for b in range(2):
-        tt("FS%d" % b, "GB%d" % b, "PF%d:0:320" % b, A.add)
-    for h in range(2):
-        for b in range(2, 4):
-            act("X:%d:%d:4" % (640 * h + b, 640 * h + 640), "FS%d@INV" % b + LISTS[h], F.Copy)
+    for a, e, l in MADE:
+        for b in range(2):
+            act("FS%d:%d:%d" % (b, a, e), "HB%d@C2OFF" % b + l, F.Copy)
     for h, bank in enumerate(("PS", "PSB")):
-        r, a = HALVES[h], 160 * h
-        for k, b in (((0, 0), (0, 1), (1, 0)), ((1, 1),))[h]:
-            cp("X:%d:%d:4" % (640 * k + b, 640 * k + 640), "FS%d@INV" % b + LISTS[k])
-        quant("X", "X:%d:%d" % (4 * a, 4 * a + 640), r)
+        for k, b in (((0, 2), (0, 3), (0, 0), (0, 1), (1, 2)), ((1, 3), (1, 0), (1, 1)))[h]:
+            a, e, l = MADE[k]
+            r = ":%d:%d" % (a, e)
+            if b < 2:
+                tt("X:%d:%d:4" % (4 * a + b, 4 * e), "FS%d" % b + r, "PF%d" % b + r, A.add)
+            else:
+                tt("X:%d:%d:4" % (4 * a + b, 4 * e), "HB%d@C2OFF" % b + l, "FJ%d" % b + r, A.add)
+        a, e, l = MADE[h]
+        r = ":%d:%d" % (a, e)
+        quant("X", "X:%d:%d" % (4 * a, 4 * e), r)
         mm(bank, "V", 0, "X", r=r)
-        dma("dout", [("y", T.oc[:, 4 * a:4 * a + 640], T.qX[:, a:a + 160].bitcast(dt.uint8))], [], ["qX" + r])
+        dma("dout", [("y", T.oc[:, 4 * a:4 * e], T.qX[:, a:e].bitcast(dt.uint8))], [], ["qX" + r])
         if h:
             dma("dout", [("sy"[k // 2], T.osc[4 * k:4 * k + 4, :], T.sX[32 * k:32 * k + 4, 0:C]) for k in range(4)], [], ["sX"])
-        act("YB" + r, bank + ":0:160", F.Copy)
-        dma("dy", [("s", T.y[:, a:a + 160], T.YB[:, a:a + 160])], [], ["YB" + r])
+            cp("YB" + r, bank + ":0:%d" % (e - a))
+        else:
+            act("YB" + r, bank + ":0:%d" % (e - a), F.Copy)
+        dma("dy", [("s", T.y[:, a:e], T.YB[:, a:e])], [], ["YB" + r])
     wait("g", list(cnt.items()))

from concourse.mybir import dt, AluOpType as A, ActivationFunctionType as F

C, P, R = 320, 128, 3
NV = 3520
WIDE = (2576, 2896, 3216, NV)
WW = 2 * NV + C
UP = 1776
SKEYS = (0, 1, 19, 18, 2, 3, 17, 16)
VKEYS = tuple(a for a in range(20) if a not in SKEYS)
HALVES, LISTS = (":0:160", ":160:320"), (":0:10", ":10:20")
PIECES = ((0, 176), (176, C))
MADE = ((0, 192, ":0:12"), (192, C, ":12:20"))
BIG = 4194304.0
HUGE = 1e25
WHOLE = 12582912.0

SCRATCH, AT = {}, {}


def _b(n, w, d="float32", where="sbuf"):
    SCRATCH[n] = (where, [P, w], d)
    AT[n] = (n, 0, w)


def _t(n, d, parts, where="sbuf"):
    a = 0
    for k, w in parts:
        AT[k] = (n, a, w)
        a += w
    SCRATCH[n] = (where, [P, a], d)


for _n, _w in (("E16", C), ("JR", C), ("JP0", C), ("JP", C), ("TNY", 1), ("MASK", C), ("RS", C), ("MB0", C), ("MB", C), ("SEL", C), ("HOLD", C),
               ("KP", C), ("KF0", C), ("KF1", C), ("KM", C), ("KS", C), ("S1", C), ("S2", C), ("SM", C), ("SS", C + 1), ("NA", 20), ("ND", 20),
               ("STEP", C), ("PT0", C), ("PT1", C), ("YB", C), ("XA", 40), ("XB", 40), ("OW", 40)):
    _b(_n, _w)
_t("SKB", "float32", [("SK", C), ("SKE", 16)])
_t("CTAB", "float32", [("C16", 20), ("C1", 20), ("QP", 4), ("Q20", 4), ("ODD", 4), ("NO", 4), ("NE", 4), ("CR", 4), ("CH", 4),
                       ("TOP", 4), ("JT0", 20), ("JT", 20), ("FE", 4), ("FO", 4), ("QH", 4)])
_t("FTAB", "float32", [("ACC", 20), ("TH", 12), ("FR", 20), ("PL", 20), ("KT", 20)] +
   [(k + x, w) for x in ("", "J") for k, w in (("KU", 20), ("KV", 32), ("KA", 64), ("KB", 64))])
_t("TAB", "bfloat16", [("TA", 12), ("TB", 12)])
_b("VSB", 1600, "float16")
_b("GS", 640, "float16")
_t("CTABI", "int32", [("QI", 4), ("QA", 4), ("QB", 4)])
_t("ITAB", "int32", [("P1", 20), ("P2", 20)])
_t("UTAB", "uint16", [("OQ", 40), ("OQJ", 40)] + [(k, 20) for k in ("PERM", "RP0", "RP1", "OWU", "COFF", "C2OFF", "P2U", "IXU", "JU", "X40", "X41", "X42", "X43")])
_b("R16", C, "uint16")
_b("UI", 8, "int32")
_b("PR", C, "int32")
_b("PTAB", 20, "int32")
_b("UL", 8, "uint16")
for _n, _w in (("ZER", 512), ("ONE", 512), ("OB1", 512), ("OB2", 512), ("CDF", C), ("UT", 512), ("VT", 512), ("XIN", 4 * C),
               ("X", 4 * C + 8), ("Z", 4 * C), ("W", WW), ("CC", NV // 2), ("D", 2 * UP), ("G", 640), ("GT", 640), ("W2", 8 * C), ("N2", 4 * C), ("RKX", 640),
               ("MBH", 640), ("IX", 640), ("GJ", 640), ("RKXJ", 640)):
    _b(_n, _w, "bfloat16")
_t("JUNK", "bfloat16", [("JUNK%d" % k, C) for k in range(10)])
_t("CMPB", "bfloat16", [("CMP%d" % k, C) for k in range(10)])
_t("EBB", "bfloat16", [("EB%d" % k, 512) for k in range(4)])
for _n, _w in (("FB", C), ("FJ", C), ("FS", C), ("PB", C), ("HB", 160)):
    _t(_n + "B", "bfloat16", [("%s%d" % (_n, k), _w) for k in range(4)])
_t("CTB", "bfloat16", [("CT%d" % k, 4 * C) for k in range(6)])
_t("PFB", "float32", [("PF%d" % k, 512) for k in range(4)], "psum")
for _n in ("PS", "PSB", "PK", "PH"):
    _b(_n, 512, "float32", "psum")
for _n, _w in [("OB", P), ("U", P), ("UR", P), ("V", P), ("L", 512), ("X", C), ("Y", C)] + [("%s%d" % (z, k), C) for k in range(R) for z in "ZA"]:
    _b("q" + _n, _w, "float8_e4m3fn_x4")
    _b("s" + _n, _w, "uint8")
for _n, _d in (("q", "float8_e4m3fn_x4"), ("s", "uint8")):
    _t(_n + "EB", _d, [("%sE%d" % (_n, k), P) for k in range(4)])
    _t(_n + "CB", _d, [("%sC%d" % (_n, k), C) for k in range(6)])
PSUM = ["PF0", "PF1", "PF2", "PF3", "PS", "PSB", "PK", "PH"]
BANKS = ("PH", "PK", "PS", "PSB")

SEMAPHORES = ["cv", "cs", "ct", "cg", "dp", "dt", "dx", "du", "dv", "dw", "dd", "de", "dout", "dpt", "dy", "sent"] + ["arr%d" % k for k in range(R)]


def region(s):
    f = s.split("@")[0].split(":")
    if len(f) < 3 or "@" in s:
        return f[0], range(AT[f[0]][2])
    return f[0], range(int(f[1]), int(f[2]), int((f + [1])[3]))


def meet(a, b):
    if a[-1] < b[0] or b[-1] < a[0]:
        return False
    return a.step == 1 or b.step == 1 or a.step != b.step or (a[0] - b[0]) % a.step == 0


def rank_program(g, core, T, topo):
    rank = T.rank_of(core)
    if rank is None:
        return
    nxt = T.cores[(rank + 1) % len(T.cores)]
    V, S, TE = g.vector, g.scalar, g.tensor
    eng = {"v": V, "s": S, "t": TE, "g": g, "y": g.sync}
    cnt, seen, wr, rd = {}, {e: {} for e in eng}, {}, {}

    def ap(s):
        s, _x, by = s.partition("@")
        n, o, w = AT[s.split(":")[0]]
        r = region(s)[1]
        a, e = o + r.start, o + r.stop
        v = T[n][:, a:e:r.step] if r.step > 1 else T[n][:, a:e]
        return v.indirect(ap(by)) if by else v

    def wait(e, deps):
        most = {}
        for s, n in deps:
            most[s] = max(most.get(s, 0), n)
        for s, n in most.items():
            if seen[e].get(s, 0) < n:
                eng[e].wait_ge(T.sem[s], n)
                seen[e][s] = n

    def deps_of(outs, ins, own):
        d = []
        for k, r in ins:
            d += [x[1:] for x in wr.get(k, []) if meet(x[0], r)]
            if k in PSUM:
                d += [x[1:] for x in rd.get(k, []) if x[1] != own]
        for k, r in outs:
            for x in wr.get(k, []) + rd.get(k, []):
                if (meet(x[0], r) or k in PSUM) and not (own == "ct" and x[1] == own):
                    d.append(x[1:])
        return d

    def note(outs, ins, sem, n):
        for k, r in ins:
            rd[k] = [x for x in rd.get(k, []) if x[1] != sem or x[0] != r] + [(r, sem, n)]
        for k, r in outs:
            whole = len(r) == AT[k][2] or k in PSUM
            wr[k] = ([] if whole else [x for x in wr.get(k, []) if x[0] != r]) + [(r, sem, n)]
            if whole:
                rd[k] = [x for x in rd.get(k, []) if x[2] == n and x[1] == sem]

    def op(e, call, outs, ins, extra=()):
        own = "c" + e
        lists = [s.split("@")[1] for s in list(outs) + list(ins) if "@" in s]
        o, i = [region(s) for s in outs], [region(s) for s in list(ins) + lists]
        wait(e, deps_of(o, i, own) + list(extra))
        cnt[own] = cnt.get(own, 0) + 1
        call().then_inc(T.sem[own], 1)
        note(o, i, own, cnt[own])

    def dma(sem, moves, outs, ins):
        o, i = [region(s) for s in outs], [region(s) for s in ins]
        d = deps_of(o, i, "")
        for q, to, fr in moves:
            wait(q, d)
            eng[q].dma_start(to, fr).then_inc(T.sem[sem], 16)
            cnt[sem] = cnt.get(sem, 0) + 16
        note(o, i, sem, cnt[sem])

    def ts(o, i, s1, op0, s2=None, op1=None):
        a1, a2 = [ap(s) if isinstance(s, str) else s for s in (s1, s2)]
        names = [i] + [s for s in (s1, s2) if isinstance(s, str)]
        if op1 is None:
            op("v", lambda: V.tensor_scalar(ap(o), ap(i), a1, None, op0), [o], names)
        else:
            op("v", lambda: V.tensor_scalar(ap(o), ap(i), a1, a2, op0, op1), [o], names)

    def tt(o, a, b, o2):
        op("v", lambda: V.tensor_tensor(ap(o), ap(a), ap(b), o2), [o], [a, b])

    def cp(o, i):
        op("v", lambda: V.tensor_copy(ap(o), ap(i)), [o], [i])

    def scan(o, a, b, init, op0, op1):
        first = isinstance(init, str)
        op("v", lambda: V.tensor_tensor_scan(ap(o), ap(a), ap(b), ap(init) if first else init, op0, op1), [o], [a, b] + ([init] if first else []))

    def fill(n, c):
        op("v", lambda: V.memset(ap(n), c), [n], [])

    def quant(q, t, r=""):
        op("v", lambda: V.quantize_mx(ap("q" + q + r), ap("s" + q + r), ap(t)), ["q" + q + r, "s" + q + r], [t])

    def turn(o, i):
        op("v", lambda: V.transpose(ap(o), ap(i)), [o], [i])

    def mm(ps, a, a0, b, start=True, stop=True, extra=(), r=""):
        w = ":%d:%d" % (a0, a0 + P)
        i = ["q" + a + w, "s" + a + w, "q" + b + r, "s" + b + r]
        op("t", lambda: TE.matmul_mx(ap(ps + ":0:%d" % len(region(i[2])[1])), ap(i[0]), ap(i[1]), ap(i[2]), ap(i[3]), start, stop), [ps], i, extra)

    def act(o, i, f, acc=None, bias=None, scale=None):
        kw = {}
        if bias is not None:
            kw["bias"] = ap(bias) if isinstance(bias, str) else bias
        if scale is not None:
            kw["scale"] = scale
        if acc is not None:
            kw["accum_out"] = ap(acc)
        op("s", lambda: S.activation(ap(o), ap(i), f, **kw), [o] + [s for s in (acc,) if s], [i] + [s for s in (bias,) if isinstance(s, str)])

    def iota(n, pattern, base=0, cm=0):
        kw = {} if SCRATCH[AT[n.split(":")[0]][0]][2] == "int32" else {"allow_small_or_imprecise_dtypes": True}
        op("g", lambda: g.iota(ap(n), pattern, base, cm, **kw), [n], [])

    def sel(o, i, pattern, cop, c, base, cm):
        op("g", lambda: g.affine_select(ap(o), ap(i), pattern, cop, c, base, cm), [o], [i])

    dma("dt", [("y", T.PTAB[:, :], T.p[:, :])], ["PTAB"], [])
    dma("dp", [("sy"[k % 2], T.PR[k:P:16, :], T.p[:, :]) for k in range(16)], ["PR"], [])
    dma("dx", [("y", T.XIN[:, :], T.x[:, :])], ["XIN"], [])
    dma("du", [("y", T.UT[:, :], T.u[:, :])], ["UT"], [])

    iota("QI:0:2", [[0, 2]], 0, 1)
    iota("C16", [[16, 20]])
    iota("JP0", [[1, 16], [16, 20]], 352)
    iota("C1", [[1, 20]])
    iota("E16", [[0, 20], [1, 16]])
    iota("JR", [[1, C]])
    iota("W:0:2576", [[0, 2576]], -160)
    fill("ZER", 0.0)
    ts("QA:0:2", "QI:0:2", 15, A.bitwise_and)
    ts("QB:0:2", "QI:0:2", 4, A.arith_shift_right, 1, A.bitwise_and)
    fill("ONE:0:256", 1.0)
    ts("TOP:0:1", "QA:0:1", 15.0, A.is_equal, 4096.0, A.mult)
    cp("QP:0:1", "QA:0:1")
    cp("ODD:0:1", "QB:0:1")
    fill("ONE:256:512", 1.0)
    ts("JT0", "C16", "QP:0:1", A.add, 352.0, A.add)
    ts("QH:0:1", "QP:0:1", 0.5, A.add)
    ts("QH:1:2", "QP:0:1", -0.5, A.add)
    ts("Q20:0:1", "QP:0:1", 20.0, A.mult)
    ts("CR:0:1", "QP:0:1", -1.0 / 32, A.mult, 160.5 / 32, A.add)
    ts("CH:0:1", "QP:0:1", -1.0 / 32, A.mult, 176.0 / 32, A.add)
    ts("FE:0:1", "ODD:0:1", -65536.0, A.mult, 32768.0, A.add)
    ts("FO:0:1", "ODD:0:1", 65536.0, A.mult, -32768.0, A.add)
    ts("NO:0:1", "ODD:0:1", 32768.0, A.mult)
    ts("JP", "JP0", 2.0 ** -9, A.mult)
    ts("JT", "JT0", 2.0 ** -9, A.mult)
    ts("PERM", "C1", "Q20:0:1", A.add)
    ts("NE:0:1", "ODD:0:1", -32768.0, A.mult, 32768.0, A.add)
    ts("XB:0:40:2", "C16", "QP:0:1", A.add, float(NV), A.add)
    fill("SKE", 3600.0)
    fill("XA:0:40:2", 0.0)
    fill("KV", 0.0)
    fill("KVJ", 0.0)
    fill("SS:0:1", -HUGE)
    fill("TNY", 2.0 ** -126)

    def clear(a, b):
        for c in range(a, b, 512):
            act("D:%d:%d" % (c, min(c + 512, b)), "ZER:0:%d" % min(512, b - c), F.Identity, bias="TOP:0:1")

    clear(0, 1024)
    act("MB0", "E16", F.Sign, bias="QH:1:2", scale=-1.0)
    clear(1024, 1536)
    dma("dw", [("y", T.qL[:, 0:512].bitcast(dt.uint8), T.wc[:, :]), ("y", T.sL[:, 0:512], T.ws[:, :])], ["qL", "sL"], [])
    dma("dv", [("y", T.VT[:, :], T.v[:, :])], ["VT"], [])
    for b in range(4):
        sel("EB%d" % b, "ZER", [[1, 512]], A.not_equal, 1.0, -b, -4)
    iota("UI", [[16, 8]])
    iota("W2", [[0, 8 * C]])
    sel("OB1", "ONE", [[-16, 8], [0, 64]], A.is_ge, 0.0, 0, 1)
    sel("OB2", "OB1", [[16, 8], [0, 64]], A.is_ge, 0.0, 15, -1)
    tt("KS:15:320:16", "PTAB", "JT", A.add)
    fill("RKX:0:320", 32768.0)
    ts("TH:0:10", "KS:31:320:32", 16.0, A.mult, "CH:0:1", A.add)
    ts("TA:0:10", "KS:31:320:32", 16.0, A.mult, "CH:0:1", A.add)
    for r in HALVES:
        tt("KP" + r, "PR" + r, "JP" + r, A.add)

    def half(k):
        scan("VSB:%d:%d" % (160 * k, 160 * k + 160), "CMP%d:0:160" % k, "CMP%d:160:320" % k, 0.0, A.add, A.add)

    def spread(sem, n, a, b, to):
        e = to + b - a
        moves = [(T.D[0:P:32, to:e], T[n][0:P:32, a:b]), (T.D[16:P:32, to + 1:e + 1], T[n][16:P:32, a:b])]
        for d in range(1, 4):
            moves.append((T.D[32 * d + 1 + d:P:16, to:e], T[n][d:P - 32 * d:16, a:b]))
            moves.append((T.D[4 + d:P - 32 * d:16, to + 1:e + 1], T[n][32 * d + 4 + d:P:16, a:b]))
        dma(sem, [("ys"[k % 2], o, i) for k, (o, i) in enumerate(moves)], ["D:%d:%d" % (to, e + 1)], ["%s:%d:%d" % (n, a, b)])

    key = ["KS:%d:%d" % (16 * c + 15, 16 * c + 16) for c in range(20)]

    def first_ranks(by_column):
        for k in range(10):
            act("JUNK%d" % k, "KP", F.Sign, acc="ACC:%d:%d" % (k, k + 1), bias=key[2 * k], scale=-1.0)
        act("MB", "MB0", F.Copy, scale=BIG)
        act("CDF", "JR", F.Identity, bias=-159.0)
        ts("R16:0:160", "KP:0:160", 16.0, A.mult, "CR:0:1", A.add)
        tt("TB:0:10", "TH:0:10", "TA:0:10", A.subtract)
        ts("R16:160:320", "KP:160:320", 16.0, A.mult, "CR:0:1", A.add)
        cp("KF0", "KP@PERM")
        for k in range(10):
            ts("CMP%d" % k, "R16", "TA:%d:%d" % (k, k + 1), A.subtract, "TB:%d:%d" % (k, k + 1), A.is_lt)
            if k > 1:
                half(k - 2)
            if k in (1, 5):
                next(by_column)
        half(8)
        next(by_column)
        half(9)
        ts("MASK:0:160", "E16:0:160", "QP:0:1", A.is_equal)
        ts("RP0:0:20:2", "ACC:0:10", 319.0, A.add, 0.5, A.mult)
        cp("RP0:1:20:2", "VSB:159:1600:160")

    def ranks(t, by_column):
        kf, rp = "KF%d" % (t % 2), "RP%d" % (t % 2)
        for r in HALVES:
            scan("KM" + r, kf + r, "MASK" + r, 0.0, A.max, A.mult)
        for r in HALVES:
            scan("KS" + r, "RS" + r, "KM" + r, 0.0, A.mult, A.add)
        for k in range(10):
            act("JUNK%d" % k, kf, F.Sign, acc="ACC:%d:%d" % (k, k + 1), bias=key[2 * k], scale=-1.0)
        ts("R16:0:160", kf + ":0:160", 16.0, A.mult, "CR:0:1", A.add)
        ts("TH:0:10", "KS:31:320:32", 16.0, A.mult, "CH:0:1", A.add)
        ts("TA:0:10", "KS:31:320:32", 16.0, A.mult, "CH:0:1", A.add)
        ts("R16:160:320", kf + ":160:320", 16.0, A.mult, "CR:0:1", A.add)
        tt("TB:0:10", "TH:0:10", "TA:0:10", A.subtract)
        next(by_column)
        for k in range(10):
            ts("CMP%d" % k, "R16", "TA:%d:%d" % (k, k + 1), A.subtract, "TB:%d:%d" % (k, k + 1), A.is_lt)
            if k > 1:
                half(k - 2)
        half(8)
        next(by_column)
        half(9)
        ts(rp + ":0:20:2", "ACC:0:10", 319.0, A.add, 0.5, A.mult)
        next(by_column)
        cp(rp + ":1:20:2", "VSB:159:1600:160")

    def own(x, rank, add):
        ts("RKX%s:0:640:32" % x, rank, add, A.add, "FE:0:1", A.max)
        ts("RKX%s:1:640:32" % x, rank, add, A.add, "FO:0:1", A.max)

    def offsets(x, keys, h):
        ts("KU" + x, keys, h - 0.5, A.is_ge, float(UP + 1 - h), A.mult)
        yield
        tt("KV%s:0:20" % x, "KU" + x, keys, A.add)
        yield
        turn("KA%s:16:48" % x, "KV" + x)
        yield
        cp("KA%s:0:16" % x, "KA%s:16:32" % x)
        cp("KA%s:48:64" % x, "KA%s:32:48" % x)
        yield
        turn("KB" + x, "KA" + x)
        yield
        cp("OQ%s:0:40:2" % x, "KB%s:0:20" % x)
        cp("OQ%s:1:40:2" % x, "KB%s:32:52" % x)
        yield

    def order(t, by_column, scalar_early, scalar_late):
        last, nv = t == R, WIDE[t]
        h = nv // 2
        rp, x = "RP%d" % (t % 2), "J" if last else ""
        by_slot = iter(()) if last else offsets("", "KT", h)
        next(by_column)
        cp("SK@" + rp, "KF%d" % (t % 2))
        act("JUNK0", "KF%d" % (t % 2), F.Sign, acc="ACC:0:1", bias=h - 0.5, scale=-1.0)
        scalar_early(0)
        act("W:%d:%d" % (h - 1, h), "ACC:0:1", F.Copy, scale=0.5)
        scalar_early(1)
        next(by_column)
        if t == 0:
            fill("RKX:320:640", 32768.0)
        else:
            own("J", rp, -160.0)
        scan("S1", "SK", "MB", 0.0, A.min, A.max)
        op("v", lambda: V.tensor_tensor_scan(ap("S2"), T.SKB[:, 1:C + 1], ap("MB"), 0.0, A.min, A.max), ["S2"], ["SK", "SKE", "MB"])
        if not last:
            tt("KT", "S1:15:320:16", "SK:0:320:16", A.max)
        tt("P1", "S1:15:320:16", "SK:0:320:16", A.max)
        tt("XB:1:40:2", "S1:15:320:16", "SK:0:320:16", A.max)
        tt("P2", "S2:15:320:16", "SK:1:320:16", A.max)
        next(by_slot, 0)
        if not last:
            tt("FR", "KT", "P1", A.subtract)
        tt("XA:1:40:2", "P1", "P2", A.is_equal)
        next(by_slot, 0)
        if not last:
            ts("JU", "FR", 512.0, A.mult, 160.0, A.add)
        scan("OW", "XA", "XB", 0.0, A.mult, A.add)
        scalar_late(-3)
        next(by_slot, 0)
        if t == 0:
            ts("RKX:16:640:32", "C1", 0.0, A.mult, "NO:0:1", A.add)
        cp("OWU", "OW:1:40:2")
        next(by_slot, 0)
        cp("W@OWU", "CDF")
        spread("de", "W", h - 1, nv, UP)
        next(by_slot, 0)
        if t == 0:
            ts("RKX:17:640:32", "C1", 0.0, A.mult, "NE:0:1", A.add)
        scan("CC:0:%d" % h, "W:0:%d" % h, "W:0:%d" % h, -160.0, A.max, A.max)
        spread("dd", "CC", 0, h, 0)
        if not last:
            iota("W:0:%d" % min(nv + C, NV), [[0, min(nv + C, NV)]], -160)
        next(by_slot, 0)
        next(by_column)
        if t == 0:
            own("", "JT0", -512.0)
        scalar_late(-1)
        up = "D:%d:%d" % (UP, UP + nv - h + 2)
        scan(up, up, up, -160.0, A.max, A.max)
        scalar_late(-2)
        act("G:320:640", "D@OQ%s:20:40" % x, F.Copy)
        for r, l in zip(HALVES, LISTS):
            cp("G" + r, "D@OQ" + x + l)
        scalar_late(0)
        for r in HALVES + (":320:640",):
            turn("GT" + r, "G" + r)
        for r in (":0:320", ":320:640"):
            scan("GS" + r, "RKX" + x + r, "GT" + r, 4096.0, A.min, A.add)
        scalar_late(1)
        tt("PL", "GS:14:640:32", "GS:30:640:32", A.add)
        if t:
            ts("C2OFF", "PL", 1.0 / 16, A.mult, 80.0 - 15.0 / 32, A.add)

    def cells(k):
        if k < 2:
            turn("GT" + (":0:320", ":320:640")[k], "GJ" + (":0:320", ":320:640")[k])
        elif k < 4:
            r = (":0:320", ":320:640")[k - 2]
            scan("GS" + r, "RKXJ" + r, "GT" + r, 4096.0, A.min, A.add)
        elif k == 4:
            tt("PL", "GS:14:640:32", "GS:30:640:32", A.add)
        else:
            ts("COFF", "PL", 1.0 / 8, A.mult, 160.0 - 7.0 / 16, A.add)

    def pairs(h):
        a, e = PIECES[h]
        r, banks = ":%d:%d" % (a, e), (BANKS, PSUM)[h]
        quant("X", "X:%d:%d" % (4 * a, 4 * e), r)
        quant("Y", "X:%d:%d" % (4 * a + 4, 4 * e + 4), r)
        for b in (2, 0, 3, 1):
            mm(banks[b], "E%d" % b, 0, "X", True, False, r=r)
            mm(banks[b], "E%d" % b, 0, "Y", False, True, r=r)

    def halve(h, bs, vector=False):
        a, e = PIECES[h]
        for b in bs:
            o, i = "PB%d:%d:%d" % (b, a, e), (BANKS, PSUM)[h][b] + ":0:%d" % (e - a)
            if vector:
                ts(o, i, 0.5, A.mult)
            else:
                act(o, i, F.Copy, scale=0.5)

    def lists(again, between):
        ts("P2U", "PL", 1280.0, A.add)
        between(0)
        cp("W2@P2U", "ONE:0:320")
        between(1)
        scan("N2", "W2:0:2560:2", "W2:1:2560:2", -160.0, A.add, A.add)
        if again:
            iota("W2", [[0, 8 * C]])
        between(2)
        scan("IX", "N2:1:1280:2", "MBH", 0.0, A.min, A.max)
        between(3)
        ts("IXU", "IX:31:640:32", 159.0, A.add, 0.0, A.max)
        between(4)

    def x_early(k):
        for b in range(2 * k, 2 * k + 2):
            act("FJ%d" % b, "XIN:%d:1280:4" % b, F.Copy)
        if k:
            clear(1536, 3072)
            act("D:%d:%d" % (UP, UP + 1), "ZER:0:1", F.Identity, bias=-160.0)

    def x_late(k):
        if k == -3:
            for b in range(2):
                act("X:%d:1280:4" % b, "FJ%d@JU" % b, F.Copy)
        elif k == -1:
            for b in range(2, 4):
                cp("X:%d:1280:4" % b, "FJ%d@JU" % b)
            for b in range(4):
                quant("E%d" % b, "EB%d" % b)
            cp("X:1280:1284", "X:1276:1280")
            clear(3072, 2 * UP)
            act("JUNK9", "E16", F.Sign, bias="QH:0:1", scale=-1.0)
            act("MBH:1:640:2", "MB0", F.Copy, scale=1024.0)
            act("MBH:0:640:2", "JUNK9", F.Copy, scale=1024.0)
            act("RS", "E16", F.Sign)
        elif k == -2:
            pairs(0)
        elif k == 0:
            halve(0, (2, 0, 3, 1))
            act("GJ", "D@OQJ", F.Copy)
        elif k == 1:
            pairs(1)
            halve(1, (2, 0, 3, 1))
            act("RKXJ", "RKX", F.Copy)

    by_column = offsets("J", "KS:15:320:16", WIDE[0] // 2)
    first_ranks(by_column)
    order(0, by_column, x_early, x_late)

    def sides(k):
        if k == 0:
            cp("UL", "UI")
            ts("MASK:160:320", "E16:160:320", "QP:0:1", A.is_equal)
        elif k == 1:
            quant("U", "UT")
            act("sUR", "sU@UL", F.Copy)
            act("SEL", "MASK", F.Identity, bias=-HUGE, scale=2.0 * HUGE)
        elif k == 2:
            op("v", lambda: V.tensor_copy(T.qUR[:, 0:P].bitcast(dt.uint32), T.qU[:, 0:P].bitcast(dt.uint32).indirect(T.UL[:, 0:8])), ["qUR"], ["qU", "UL"])
        elif k == 3:
            cells(0)
        else:
            cells(1)

    lists(True, sides)
    for t in range(R):
        last = t == R - 1
        qz = "Z%d" % t
        for b in range(2):
            act("Z:%d:1280:4" % (b + 2), "PB%d@IXU" % (b + 2), F.Copy)
            cp("Z:%d:1280:4" % b, "PB%d@IXU" % b)
        if t:
            cells(3)
        else:
            own("J", "RP0", -160.0)
            act("HOLD", "RS", F.Identity, bias=-HUGE, scale=2.0 * HUGE)
            for a in range(0, 4 * C, 512):
                act("CT5:%d:%d" % (a, min(a + 512, 4 * C)), "ZER:0:%d" % min(512, 4 * C - a), F.Copy)
        for h, bank in enumerate(("PK", "PH")):
            quant(qz, "Z:%d:%d" % (640 * h, 640 * h + 640), HALVES[h])
            mm(bank, "UR", 0, qz, r=HALVES[h])
        wait("g", [x[1:] for x in wr["q" + qz] + wr["s" + qz]])
        rid, pid, _s = topo.addr(nxt)
        m, arr = topo.mask(core, nxt), "arr%d" % t
        n = 2 * len(topo.engines(core, nxt))
        g.remote_dma(T["qA%d" % t][:, 0:C].bitcast(dt.uint8), T["q" + qz][:, 0:C].bitcast(dt.uint8), T.sem[arr], T.sem.sent, pid, rid, m)
        g.remote_dma(T["sA%d" % t][:, 0:C], T["s" + qz][:, 0:C], T.sem[arr], T.sem.sent, pid, rid, m)
        cnt["sent"], cnt[arr] = cnt.get("sent", 0) + n, n
        mm("PSB", "UR", 0, qz)
        mm("PS", "UR", 0, qz)
        if t:
            cells(4)
        else:
            quant("OB", "OB2")
            cells(2)
        for bank, r in zip(("PK", "PH"), HALVES):
            tt("SM" + r, bank + ":0:160", "SEL" + r, A.min)
        for r, r1 in zip(HALVES, (":1:161", ":161:321")):
            scan("SS" + r1, "HOLD" + r, "SM" + r, -HUGE, A.min, A.max)

        def over(k):
            a = VKEYS[k]
            w, e, s = k // 4, k % 4, "SS:%d:%d" % (16 * a + 16, 16 * a + 17)
            ts("CT%d:%d:%d:4" % (w, e, 64 * a + 68), "PS:0:%d" % (16 * a + 17), s, A.is_gt)
            ts("CT%d:%d:1280:4" % (w, 64 * a + 68 + e), "PS:%d:320" % (16 * a + 17), s, A.is_ge)

        def upto(k):
            a = SKEYS[k]
            n = min(16 * a + 17, C)
            act("CT%d:%d:%d:4" % (3 + k // 4, k % 4, 4 * n), "PSB:0:%d" % n, F.Sign, bias="SS:%d:%d" % (16 * a + 16, 16 * a + 17), scale=-1.0)

        def behind(k):
            a = SKEYS[k]
            act("CT%d:%d:1280:4" % (3 + k // 4, 64 * a + 68 + k % 4), "PSB:%d:320" % (16 * a + 17), F.Sign, bias="ND:%d:%d" % (a, a + 1), scale=-1.0)

        act("NA", "SS:16:321:16", F.Abs, bias="TNY", scale=1.01 * 2.0 ** -24)
        upto(0)
        upto(1)
        for h, bank in enumerate(("PK", "PH")):
            tt("CT5:%d:%d:4" % (640 * h, 640 * h + 640), bank + ":0:160", "SS" + HALVES[h], A.is_equal)
        if t == 0:
            cells(3)
        tt("ND", "SS:16:321:16", "NA", A.subtract)
        if t == 0:
            cells(4)
        for f, k in ((upto, 2), (upto, 3), (behind, 0), (behind, 1), (behind, 3), (upto, 4), (upto, 5), (upto, 6)):
            f(k)
        act("CT3", "CT3", F.Relu, scale=-1.0)
        for f, k in ((behind, 4), (behind, 5), (upto, 7), (behind, 6), (behind, 7)):
            f(k)
        for r in (":0:640", ":640:1280"):
            act("CT4" + r, "CT4" + r, F.Relu, scale=-1.0)
        after = {-1: ((5, 0), (5, 1)), 4: ((0, 0), (0, 1)), 8: ((1, 0), (1, 1)), 9: ((3, 0), (3, 1)), 10: ((4, 0),), 11: ((4, 1), (2, 0), (2, 1))}
        for k in range(-1, 12):
            if k >= 0:
                over(k)
            for w, h in after.get(k, ()):
                if w in (2, 4):
                    quant("C%d" % w, "CT%d:%d:%d" % (w, 640 * h, 640 * h + 640), HALVES[h])
                elif h == 0:
                    quant("C%d" % w, "CT%d" % w)
                mm(("PK", "PH")[h], "OB", 0, "C%d" % w, w == 5, w == 2, r=HALVES[h])
        cells(5)
        if t == 0:
            quant("V", "VT")
        for b in range(4 * last):
            ts("X4%d" % b, "RP%d" % (t % 2), 4.0, A.mult, float(b), A.add)
        act("STEP:0:160", "PK:0:160", F.Copy)
        cp("STEP:160:320", "PH:0:160")
        for b in range(4 - 4 * last):
            mm("PF%d" % b, "E%d" % b, 0, "X")
        for b in range(4):
            mm(BANKS[b], "L", P * b, "A%d" % t, extra=[(arr, cnt[arr])])
        for r, l in zip(HALVES, LISTS):
            tt("KF%d" % ((t + 1) % 2) + r, "STEP@COFF" + l, "KF%d" % (t % 2) + r, A.add)
        by_column = offsets("J", "KS:15:320:16", WIDE[t + 1] // 2)
        ranks(t + 1, by_column)

        def early(k, t=t, last=last):
            for b in range(2 * k, 2 * k + 2):
                if last:
                    act("Z:%d:1280:4" % b, "X:0:1280@X4%d" % b, F.Copy)
                else:
                    act("FB%d" % b, "PF%d:0:320" % b, F.Copy)
            for b in range(2 * k * (not last)):
                act("FJ%d" % b, "FB%d@RP%d" % (b, t % 2), F.Copy)
            for b in range(4 * k):
                act("HB%d" % b, BANKS[b] + ":1:320:2", F.Copy, scale=0.03125)

        def late(k, t=t, last=last):
            moves = [("FS%d:%d:%d" % (b, a, e), "FJ%d@JU" % b + l) for a, e, l in MADE for b in range(4)]
            if last and k == -1:
                quant("Y", "Z")
                for b in (2, 3, 0, 1):
                    mm("PF%d" % b, "E%d" % b, 0, "Y")
                act("PT0", "KF%d" % ((t + 1) % 2), F.Identity, bias=WHOLE)
                act("FJ2", "PF2:0:320", F.Copy)
                act("PT1", "PT0", F.Identity, bias=-WHOLE - 1.0)
                act("FJ3", "PF3:0:320", F.Copy)
                dma("dpt", [("y", T.pt[:, :], T.PT1[0:P:16, :])], [], ["PT1"])
            elif k == -1:
                cp("FJ3", "FB3@RP%d" % (t % 2))
                act("FJ2", "FB2@RP%d" % (t % 2), F.Copy)
            if not last and k in (-1, 0):
                for o, i in (moves[:2], moves[2:])[k + 1]:
                    act(o, i, F.Copy)
                if k == 0:
                    act("GJ", "D@OQJ", F.Copy)

        def add(h, b):
            a, e, l = MADE[h]
            tt("X:%d:%d:4" % (4 * a + b, 4 * e), "HB%d@C2OFF" % b + l, "FS%d:%d:%d" % (b, a, e), A.add)

        def new_x(k):
            if k == 0:
                for b in range(4):
                    add(0, b)
                add(1, 0)
                pairs(0)
                halve(0, (2, 0, 3, 1))
                for b in range(1, 4):
                    add(1, b)
            elif k == 1:
                cp("X:1280:1284", "X:1276:1280")
                pairs(1)
                halve(1, (2, 0, 3))
            elif k < 4:
                cells(k - 2)
            else:
                cells(2)
                halve(1, (1,), True)

        order(t + 1, by_column, early, late)
        if not last:
            lists(t + 1 < R - 1, new_x)

    for a, e, l in MADE:
        for b in range(2):
            act("FS%d:%d:%d" % (b, a, e), "HB%d@C2OFF" % b + l, F.Copy)
    for h, bank in enumerate(("PS", "PSB")):
        for k, b in (((0, 2), (0, 3), (0, 0), (0, 1), (1, 2)), ((1, 3), (1, 0), (1, 1)))[h]:
            a, e, l = MADE[k]
            r = ":%d:%d" % (a, e)
            if b < 2:
                tt("X:%d:%d:4" % (4 * a + b, 4 * e), "FS%d" % b + r, "PF%d" % b + r, A.add)
            else:
                tt("X:%d:%d:4" % (4 * a + b, 4 * e), "HB%d@C2OFF" % b + l, "FJ%d" % b + r, A.add)
        a, e, l = MADE[h]
        r = ":%d:%d" % (a, e)
        quant("X", "X:%d:%d" % (4 * a, 4 * e), r)
        mm(bank, "V", 0, "X", r=r)
        dma("dout", [("y", T.oc[:, 4 * a:4 * e], T.qX[:, a:e].bitcast(dt.uint8))], [], ["qX" + r])
        if h:
            dma("dout", [("sy"[k // 2], T.osc[4 * k:4 * k + 4, :], T.sX[32 * k:32 * k + 4, 0:C]) for k in range(4)], [], ["sX"])
            cp("YB" + r, bank + ":0:%d" % (e - a))
        else:
            act("YB" + r, bank + ":0:%d" % (e - a), F.Copy)
        dma("dy", [("s", T.y[:, a:e], T.YB[:, a:e])], [], ["YB" + r])
    wait("g", list(cnt.items()))
